import numpy as np, ml_dtypes
CORES = [3,7,11,15,131,135,139,143]
N = 8
BF = ml_dtypes.bfloat16
V, P, Q, RO, TS = 160, 2, 2, 3, 1024
M, B = 8 * N * V, V // P
def clip(a):
    return np.minimum(np.maximum(np.floor(a), -2 ** 20), 2 ** 20 - 1).astype(np.int64)
def walls(rng, base, size, gap):
    mid = base + size * (rng.random((N, 8, 16, V)) - 0.5)
    h = gap * (16 - np.arange(16)[:, None]) * 0.0625
    l = mid + h * rng.random((N, 8, 16, V)); r = mid - h * rng.random((N, 8, 16, V)); turn = rng.random((N, 8, 1, V)) < 0.25
    return clip(np.where(turn, r, l)), clip(np.where(turn, l, r))
def common(rng):
    return walls(rng, rng.integers(-2 ** 18, 2 ** 18, (N, 8, 1, V)), np.exp2(rng.integers(8, 18, (N, 8, 1, V))), 2.0 ** 17 * rng.random((N, 8, 1, V)))
def slots(rng):
    share = rng.choice(np.array([0.1, 0.4, 0.7, 0.9]), (N, 8, 2, 1, V))
    o = rng.integers(0, M, (N, 8, 16, V)); none = (rng.random((N, 8, 2, 8, V)) < share).reshape(N, 8, 16, V)
    return np.where(none, M, o)
def pack(l, r, o):
    return {"lw": np.ascontiguousarray(l.reshape(N, 128, V)).astype(np.int32), "rw": np.ascontiguousarray(r.reshape(N, 128, V)).astype(np.int32),
            "opts": np.ascontiguousarray(o.reshape(N, 128, V)).astype(np.int32)}
def setup_inputs(rng):
    l, r = common(rng)
    return pack(l, r, slots(rng))
def setup_inputs_ties(rng):
    ix = rng.integers(0, 5, (N, 8, V)); base = 65536 * np.array([0, 0, 12, 12, -13])[:, None] + 2 * rng.integers(-4, 5, (5, 1)); out = []
    for up in (rng.integers(0, 6), 0):
        prof = base + up + rng.integers(0, 2, (5, 16))
        a = prof[ix].transpose(0, 1, 3, 2)
        i = rng.integers(0, 16, (N, 8, 1, V)); d = rng.choice(np.array([-1, 1]), (N, 8, 1, V)) * (rng.random((N, 8, 1, V)) < 0.3)
        far = 65536 * (rng.random((N, 8, 1, V)) < 0.125)
        out.append(a + d * (np.arange(16)[:, None] == i) + far)
    return pack(out[0], out[1], np.where(rng.random((N, 8, 16, V)) < 0.3, M, rng.integers(0, M, (N, 8, 16, V))))
def setup_inputs_bare(rng):
    l, r = common(rng); kinds = np.zeros((7, 16), bool)
    kinds[1, :8] = True; kinds[2, 8:] = True; kinds[3] = True; kinds[4, [0, 15]] = True; kinds[5, [7, 8]] = True; kinds[6, 0] = True
    cls = rng.integers(0, 7, (N, 8, V)); cls[:, 3] = 0; cls[:, 5] = 3
    o = np.where(kinds[cls].transpose(0, 1, 3, 2), rng.integers(0, M, (N, 8, 16, V)), M)
    for g, s, e, d in ((1, 0, -2 ** 20, 1), (6, 15, 2 ** 20 - 1, -1)):
        l[:, g] = e + d * rng.integers(0, 64, (N, 16, V)); r[:, g] = e + d * rng.integers(0, 64, (N, 16, V))
        o[:, g] = M; o[:, g, s] = V * (8 * rng.integers(0, N, (N, V)) + g) + rng.integers(0, B, (N, V))
    return pack(l, r, o)
def setup_inputs_ends(rng):
    l, r = common(rng); o = slots(rng)
    o[:, ::2] = rng.choice(np.array([0, V - 1, V, 8 * V - 1, 8 * V, M - 1, M]), (N, 4, 16, V))
    o[:, 2] = rng.integers(0, M)
    own = V * np.arange(8 * N).reshape(N, 8, 1, 1) + np.arange(V)
    o[:, 1] = np.where(rng.random((N, 16, V)) < 0.5, own[:, 1], o[:, 1])
    o[:, 3, :8] = o[:, 3, :1]; o[:, 3, 8:] = o[:, 3, 8:9]
    here = 8 * V * np.arange(N)[:, None, None]; nxt = 8 * V * ((np.arange(N) + 1) % N)[:, None, None]
    o[:, 5] = nxt + rng.integers(0, 8 * V, (N, 16, V))
    o[:, 7] = np.where(o[:, 7] < M, here + rng.integers(0, 8 * V, (N, 16, V)), M)
    return pack(l, r, o)
def setup_inputs_late(rng):
    bump = rng.random((N, 8, 1, V)) < 0.0625; bump[:, 4] = False
    l = rng.integers(-2 ** 12, 2 ** 12, (16, 1)) + bump
    r = l + rng.choice(np.array([-3, 0, 3, 5001]), (16, 1))
    z = rng.integers(0, 8, (N, 8, 2, 1, V)); s = np.arange(8)[:, None]
    has = np.where(rng.random((N, 8, 2, 1, V)) < 0.4, s == z, s >= z).reshape(N, 8, 16, V)
    o = np.where(has, rng.integers(0, M, (N, 8, 16, V)), M)
    o[:, 4] = V * (8 * rng.integers(0, N, (N, 16, V)) + 4) + rng.integers(0, V, (N, 16, V))
    return pack(l, r, o)
def setup_inputs_spread(rng):
    base = rng.choice(np.array([-1.0, 1.0]), (N, 8, 1, V)) * np.exp2(20 * rng.random((N, 8, 1, V)))
    l, r = walls(rng, base, np.abs(base) * rng.random((N, 8, 1, V)), np.exp2(18 * rng.random((N, 8, 1, V))))
    e = rng.integers(1, 5, (1, 8, 1, 1))
    o = np.minimum((M * rng.random((N, 8, 16, V)) ** e).astype(np.int64), M - 1)
    share = rng.random((N, 8, 1, V)); share[rng.integers(0, N)] = 0.0
    return pack(l, r, np.where(rng.random((N, 8, 16, V)) < share, M, o))
def check_inputs(d):
    bad = []
    for k, lo, hi in (("lw", -2 ** 20, 2 ** 20 - 1), ("rw", -2 ** 20, 2 ** 20 - 1), ("opts", 0, M)):
        if np.min(d[k]) < lo or np.max(d[k]) > hi: bad.append("range of " + k)
    return bad
def world(a, last):
    w = a.reshape(N, 8, 16, V).transpose(2, 0, 1, 3).reshape(16, M).astype(np.int32)
    return np.concatenate([w, np.full((16, 1), last, np.int32)], axis=1)
def back(w):
    return np.ascontiguousarray(w[:, :M].reshape(16, N, 8, V).transpose(1, 2, 0, 3)).reshape(N, 128, V).astype(np.float32)
def inner(L, R, ix):
    return np.concatenate([R[:, ix[:8]], -L[:, ix[8:]]], axis=1)
def reference(lw, rw, opts):
    L, R, O = world(lw, 0), world(rw, 0), world(opts, M)
    temp = (TS * np.arange(16, dtype=np.int32))[:, None]; s16 = np.arange(16); left = (s16 < 8)[:, None]
    for t in range(RO):
        nL, nR, nO = L.copy(), R.copy(), O.copy()
        v = np.tile(B * (t % P) + np.arange(B), 8 * N); c = V * np.repeat(np.arange(8 * N), B) + v
        o = O[:, c]; xl, xr = L[:, c], R[:, c]; has = o < M
        u = inner(L, R, o); gone = np.zeros(o.shape, bool)
        for q in range(Q):
            p = s16 ^ (1 + (t + 3 * q) % 7); up = u[:, p]
            ge = np.all(up >= u, axis=0); eq = np.all(up == u, axis=0)
            gone = gone | (has & has[p] & ge & (~eq | (p < s16)[:, None]))
        sl = (v + t) & 7; k = O[np.where(left, 8 + sl, sl), o]
        kl, kr = L[:, k], R[:, k]; yl, yr = xl[:, None, :], xr[:, None, :]
        under = np.all((kl[:, :8] <= yl) & (kr[:, :8] <= yr), axis=0); over = np.all((kl[:, 8:] >= yl) & (kr[:, 8:] >= yr), axis=0)
        rev = (has & ~gone & (k < M) & np.concatenate([under, over], axis=0)).reshape(2, 8, -1).astype(np.int64)
        first = (rev == 1) & (np.add.accumulate(rev, axis=1) == 1)
        ch = np.where(np.any(first, axis=1), np.add.reduce(first * k.reshape(2, 8, -1), axis=1), M)
        ent = O[s16[:, None], np.repeat(ch, 8, axis=0)]
        n = np.where(has & ~gone & ~first.reshape(16, -1), o, ent); hn = n < M
        w = np.where(hn[None], inner(L, R, n), -2 ** 23)
        l = np.where(np.any(hn[:8], axis=0)[None], np.max(w[:, :8], axis=1) - temp, xl)
        r = np.where(np.any(hn[8:], axis=0)[None], temp - np.max(w[:, 8:], axis=1), xr)
        low = l < r; mid = (l + r) >> 1
        nL[:, c] = np.where(low, mid, l); nR[:, c] = np.where(low, mid, r); nO[:, c] = n
        L, R, O = nL, nR, nO
    return {"yl": back(L), "yr": back(R), "yo": back(O)}

@@ -1,0 +1,585 @@
+from concourse.bass import DstId, RemoteDMATransfer
+from concourse.mybir import AluOpType as A, ActivationFunctionType as AF
+
+N, V, B, E = 8, 160, 80, 10240
+BIG = 8388608.0
+MG = 12582912.0
+FI, FB, II, UU = "float32", "bfloat16", "int32", "uint16"
+SCRATCH = {
+    "W": ("sbuf", [128, E + 8], FI), "OT": ("sbuf", [128, E + 16], FB),
+    "MB": ("sbuf", [128, 1312], FB), "mI": ("sbuf", [128, 1312], II),
+    "d0": ("sbuf", [128, 160, 2, 2], FB), "d1": ("sbuf", [128, 160, 2, 2], FB),
+    "V0": ("sbuf", [128, 160, 2, 2, 2], FB), "V1": ("sbuf", [128, 160, 2, 2, 2], FB),
+    "F": ("sbuf", [128, 2304], FB), "EX": ("sbuf", [128, 80, 16], FB),
+    "t1": ("sbuf", [128, 640], FI), "t2": ("sbuf", [128, 5, 8, 2, 2, 2], FI), "m4": ("sbuf", [128, 5, 2, 16], FI),
+    "X": ("sbuf", [128, 2, 2, 80], II), "Y": ("sbuf", [128, 2, 2, 80], FI), "TN": ("sbuf", [128, 5, 2, 16], FB),
+    "HB": ("sbuf", [128, 2, 5, 16], FB), "LB": ("sbuf", [128, 2, 5, 16], FB), "T4": ("sbuf", [128, 2, 5, 2, 16], FB),
+    "CI": ("sbuf", [128, 16], II), "CF": ("sbuf", [128, 16], FI), "CC": ("sbuf", [128, 64], FI),
+    "ci": ("sbuf", [128, 143], FI), "kr": ("sbuf", [128, 128], FI), "pr": ("sbuf", [128, 128], FI),
+    "DL": ("sbuf", [128, 16], FI), "F9": ("sbuf", [128, 9], FI),
+    "MZ": ("sbuf", [128, 720], FB), "M8": ("sbuf", [128, 2688], FB), "M4": ("sbuf", [128, 1408], FI),
+}
+for _n, _w, _t in (("u x0 x1 AW0 AW1 AW2 AW3", 1280, FI), ("gO cm1 cm2 AO0 AO1 AO2 AO3", 1280, FB), ("bI f1 f2", 256, FI),
+                   ("w", 640, FI), ("RAW yi si0 si1 si2 ti hI lI", 160, II), ("FT dT mT nd", 160, FB), ("LQn LQs", 160, UU),
+                   ("YO C nf tf tf0 tf1 tf2 eQ XO0 XO1 xs0 xs1 xx mm nn pp qq RF", 160, FI), ("LMn LMs L1 L2 LN slU", 80, UU),
+                   ("slT", 80, II), ("KC RS H2 kb kb2 g0 g1 gs gm gb sc da RM QF", 80, FI), ("fb cx", 10, FI), ("Mi cd cv", 10, II),
+                   ("iu cu", 10, UU)):
+    for _k in _n.split():
+        SCRATCH[_k] = ("sbuf", [128, _w], _t)
+for _k in range(8):
+    SCRATCH["P%d" % _k] = ("psum", [128, 512], FI)
+SEMAPHORES = ["qv", "qt", "qs", "qg", "ls"] + ["%s%s%d" % (a, b, e) for a in ("rw", "ro") for b in ("n", "f") for e in range(4)] \
+    + ["dm%d" % k for k in range(32)]
+
+
+def rank_program(g, core, T, topo):
+    rank = T.rank_of(core)
+    if rank is None:
+        return
+    QU = {"v": g.vector, "t": g.tensor, "s": g.scalar, "g": g, "y": g.sync}
+    tot = {}
+    waited = {q: {} for q in QU}
+    lastw, lastr = {}, {}
+    ndma = [0]
+
+    def wait(q, tok):
+        sem, val, tq = tok
+        if waited[q].get(sem, 0) < val:
+            QU[q].wait_ge(T.sem[sem], val)
+            waited[q][sem] = val
+
+    def need(q, r, w):
+        for k in r:
+            for t in lastw.get(k, []):
+                wait(q, t)
+            if k[0] == "P":
+                for t in lastr.get(k, []):
+                    if t[2] != q:
+                        wait(q, t)
+        for k in w:
+            for t in lastw.get(k, []) + lastr.get(k, []):
+                if not (q == "t" and t[2] == "t"):
+                    wait(q, t)
+
+    def done(tok, r, w):
+        for k in r:
+            lastr.setdefault(k, []).append(tok)
+        for k in w:
+            lastw[k], lastr[k] = [tok], []
+
+    def op(q, fn, r=(), w=()):
+        need(q, r, w)
+        s = "q" + q
+        tot[s] = tot.get(s, 0) + 1
+        fn(QU[q]).then_inc(T.sem[s], 1)
+        done((s, tot[s], q), r, w)
+
+    def dma(q, pairs, r=(), w=()):
+        need(q, r, w)
+        s = "dm%d" % ndma[0]
+        ndma[0] += 1
+        for o, i in pairs:
+            QU[q].dma_start(o, i).then_inc(T.sem[s], 16)
+        tot[s] = 16 * len(pairs)
+        done((s, tot[s], "d" + s), r, w)
+
+    def mm(out, pairs, r, w, first=True, last=True):
+        need("t", r, w)
+        for k, (l, x) in enumerate(pairs):
+            ins = g.tensor.matmul(out, l, x, first and k == 0, last and k == len(pairs) - 1)
+            if k == len(pairs) - 1:
+                tot["qt"] = tot.get("qt", 0) + 1
+                ins.then_inc(T.sem.qt, 1)
+                done(("qt", tot["qt"], "t"), r, w)
+
+    def ts(out, i, s1, o1, s2=None, o2=None, r=(), w=()):
+        if o2 is None:
+            op("v", lambda e: e.tensor_scalar(out, i, s1, None, o1), r, w)
+        else:
+            op("v", lambda e: e.tensor_scalar(out, i, s1, s2, o1, o2), r, w)
+
+    def tt(out, a, b, o, r, w):
+        op("v", lambda e: e.tensor_tensor(out, a, b, o), r, w)
+
+    def cp(out, i, r, w, q="v"):
+        if q == "v":
+            op("v", lambda e: e.tensor_copy(out, i), r, w)
+        else:
+            op("s", lambda e: e.activation(out, i, AF.Identity), r, w)
+
+    own = rank * 160
+    nearH = 0 if topo.host(T.cores[0]) == topo.host(core) else 1
+    partner = [c for c in T.cores if c != core and c in topo.cores_of(core)]
+    near = [c for c in T.cores if topo.host(c) == topo.host(core) and c != core and c not in partner]
+    far = [c for c in T.cores if topo.host(c) != topo.host(core)]
+    far = [c for c in far if topo.same_plane(core, c)] + [c for c in far if not topo.same_plane(core, c)]
+    offe = topo.engines(core, far[0])
+    one = [e for e in topo.engines(core, partner[0]) if e not in offe]
+    moff, mon = sum(1 << e for e in offe), sum(1 << e for e in one)
+
+    def send(kind, e):
+        name = "A%s%d" % (kind.upper(), e)
+        src = T[name][:, own:own + 160]
+        need("g", [name + "o"], [])
+
+        def tr(dst, m, sem):
+            ids = []
+            for c in dst:
+                rid, pid = topo.addr(c, core)
+                ids.append(DstId(rid=rid, pnc=pid))
+            return RemoteDMATransfer(dst_ids=ids, dma_engine_mask=m, remote_sem=T.sem[sem], srcs=[src],
+                                     dsts=[src for _ in dst], alu_op=0)
+        g.remote_dma_fused([tr(partner, mon, "r%sn%d" % (kind, e)), tr(near, moff, "r%sn%d" % (kind, e))], local_sem=T.sem.ls)
+        g.remote_dma_fused([tr(far, moff, "r%sf%d" % (kind, e))], local_sem=T.sem.ls)
+        tot["ls"] = tot.get("ls", 0) + len(one) + 2 * len(offe)
+        for s, n in (("n", len(one) + len(near) * len(offe)), ("f", len(far) * len(offe))):
+            sem = "r%s%s%d" % (kind, s, e)
+            tot[sem] = n
+            lastw[name + s] = [(sem, n, "x")]
+
+    def wr(sd, G):
+        o = 64 * sd + 32 * (G // 2)
+        return slice(o + G % 2, o + 32, 2)
+
+    for q, sd, t, k in (("y", 0, T.lw, "XA"), ("s", 1, T.rw, "XB")):
+        dma(q, [(T.X[wr(sd, G), :, h, :], t[16 * (2 * G + h):16 * (2 * G + h) + 16, :])
+                for G in range(4) for h in range(2)], [], [k])
+    dma("y", [(T.RAW[:], T.opts[:])], [], ["RAW"])
+
+    def iota(name, pat, base=0, ch=0):
+        if name in ("CI", "mI", "slT"):
+            out = T.CI[:, 0:1] if name == "CI" else T[name][:]
+            op("g", lambda e: e.iota(out, pat, base, ch), [], [name])
+        else:
+            op("g", lambda e: e.iota(T[name][:], pat, base, ch, allow_small_or_imprecise_dtypes=True), [], [name])
+    iota("CI", [[0, 1]], 0, 1)
+    iota("ci", [[1, 143]])
+    iota("kr", [[16, 2], [0, 4], [1, 16]])
+    names = ["p", "i", "i8", "pg", "sd", "Gp", "xi", "xG", "rs", "g1", "gG", "b0", "b1", "b2", "xh", "Gh"]
+    spec = [None, (0, 15), (0, 7), (4, 7), (6, 1), (4, 3), (1, 15), (0, 1), (3, 1), (4, 1), (5, 3), (0, 1), (1, 1), (2, 1),
+            (5, 1), (5, 1)]
+    for k, s in enumerate(spec):
+        if s:
+            ts(T.CI[:, k:k + 1], T.CI[:, 0:1], s[0], A.logical_shift_right, s[1], A.bitwise_and, ["CI"], ["CI%d" % k])
+    cp(T.CF[:], T.CI[:], ["CI"] + ["CI%d" % k for k in range(1, 16)], ["CF"])
+    col = {n: T.CF[:, k:k + 1] for k, n in enumerate(names)}
+    ckey = {n: "CF" for n in names}
+    nc = [0]
+
+    def mk(name, src, s1, o1, s2=None, o2=None):
+        def val(s):
+            return col[s] if isinstance(s, str) else s
+        k = nc[0]
+        nc[0] += 1
+        rk = [ckey[src]] + [ckey[s] for s in (s1, s2) if isinstance(s, str)]
+        ts(T.CC[:, k:k + 1], col[src], val(s1), o1, val(s2), o2, rk, ["CC%d" % k])
+        col[name], ckey[name] = T.CC[:, k:k + 1], "CC%d" % k
+
+    def ma(name, src, m, a):
+        mk(name, src, m, A.mult, a, A.add)
+    ma("sgn", "sd", 2.0, -1.0)
+    for b in range(2):
+        aw = T["AW%d" % b]
+        for c in range(5):
+            ts(aw[:, own + c * 32:own + c * 32 + 32], T.X[:, b, :, c::5], col["sgn"], A.mult, None, None,
+               ["XA", "XB", ckey["sgn"]], ["AW%do" % b])
+        send("w", b)
+    iota("mI", [[1, 82], [0, 16]])
+    iota("slT", [[16, 10], [0, 8]])
+    iota("RS", [[0, 10], [1, 8]])
+    iota("bI", [[1, 256]])
+    iota("KC", [[0, 10], [-16384, 8]], 141312)
+    iota("pr", [[1, 8], [0, 16]])
+    cp(T.nf[:], T.RAW[:], ["RAW"], ["nf"])
+    ts(T.tf[:], T.nf[:], 0.2, A.mult, -0.4, A.add, ["nf"], ["tf"])
+    cp(T.yi[:], T.tf[:], ["tf"], ["yi"])
+    ts(T.C[:], T.nf[:], 10240.0, A.is_ge, 5120.0, A.mult, ["nf"], ["C"])
+
+    def terms(acc, lst, n):
+        st, kacc = [], "C"
+        for j, (f, x, kx, sh) in enumerate(lst):
+            s, t, ks, kt = T["si%d" % (j % 3)][:, 0:n], T["tf%d" % (j % 3)][:, 0:n], "si%d" % (j % 3), "tf%d" % (j % 3)
+            one = [None, (ts, (t, x, float(f), A.mult, None, None, [kx], [kt])), (tt, (acc, acc, t, A.add, [kacc, kt], [kacc]))]
+            if sh:
+                one[0] = (ts, (s, x, sh, A.logical_shift_right, None, None, [kx], [ks]))
+                one[1] = (ts, (t, s, float(f), A.mult, None, None, [ks], [kt]))
+            st += [(2 * j + 3 * k, j, o) for k, o in enumerate(one) if o]
+        return [o for _, _, o in sorted(st, key=lambda z: z[:2])]
+
+    def run(steps):
+        for f, a in steps:
+            f(*a)
+    run(terms(T.C[:], [(32, T.nf[:], "nf", 0), (-159, T.yi[:], "yi", 0)] +
+              [(f, T.yi[:], "yi", sh) for sh, f in ((4, 5104), (5, -10224), (6, 608), (8, -2400), (10, 1920))], 160))
+    cp(T.ti[:], T.C[:], ["C"], ["ti"])
+    ts(T.hI[:], T.ti[:], 7, A.logical_shift_right, None, None, ["ti"], ["hI"])
+    ts(T.lI[:], T.ti[:], 127, A.bitwise_and, None, None, ["ti"], ["lI"])
+    for c in range(5):
+        cp(T.HB[:, :, c, :], T.hI[:, c::5], ["hI"], ["HB%d" % c])
+        cp(T.LB[:, :, c, :], T.lI[:, c::5], ["lI"], ["LB%d" % c])
+    ma("a4", "gG", 16.0, "i8")
+    ma("th", "rs", 64.0, "a4")
+    mk("tlo", "th", 8.0, A.add)
+    ma("m0", "g1", -1.0, 1.0)
+
+    mats = {}
+
+    def mat(name, buf, k, width, step, row, rk, t, wgt):
+        ap = T[buf][:, k * step:k * step + width]
+        rks = [rk, ckey[t]] + ([ckey[wgt]] if isinstance(wgt, str) else [])
+        ts(ap, row, col[t], A.is_equal, col[wgt] if isinstance(wgt, str) else wgt, A.mult, rks, ["M" + name])
+        mats[name] = (buf, k * step)
+
+    def lz(name, a):
+        buf, k = mats[name]
+        return T[buf][:, k + 15 - a:k + 143 - a]
+
+    def lm(name):
+        buf, k = mats[name]
+        return T[buf][:, k:k + 128]
+    c128 = T.ci[:, 0:128]
+    for k, (n, t, m) in enumerate((("TH0", "th", "m0"), ("TL0", "tlo", "m0"), ("TH1", "th", "g1"), ("TL1", "tlo", "g1"))):
+        mat(n, "M8", k, 128, 128, c128, "ci", t, m)
+    hb = ["HB%d" % c for c in range(5)] + ["LB%d" % c for c in range(5)]
+    for b in range(2):
+        for h in range(2):
+            o = (b * 2 + h) * 80
+            mm(T.P6[:, o:o + 80], [(lm("TH%d" % h), T.HB[:, b, :, :]), (lm("TL%d" % h), T.LB[:, b, :, :])],
+               ["MTH%d" % h, "MTL%d" % h] + hb, ["P6"])
+    for b in range(2):
+        for h in range(2):
+            o = (b * 2 + h) * 80
+            cp(T.T4[:, b, :, h, :], T.P6[:, o:o + 80], ["P6"], ["T4%d%d" % (b, h)])
+        cp(T["AO%d" % b][:, own:own + 160], T.T4[:, b, :, :, :], ["T4%d0" % b, "T4%d1" % b], ["AO%do" % b])
+        send("o", b)
+    ma("swr", "rs", -128.0, 64.0)
+    ma("a3", "pg", 8.0, "i8")
+    ma("qt", "rs", 64.0, "a3")
+    mk("qst", "qt", "swr", A.add)
+    ma("kc", "sd", 16.0, "i")
+    ma("xq", "xh", 2.0, "xG")
+    ma("kw", "sd", -16.0, 16.0)
+    mk("kcw", "kw", "xi", A.add)
+    for k in range(4):
+        mk("mG%d" % k, "Gp", float(k), A.is_equal)
+        mk("mX%d" % k, "xq", float(k), A.is_equal)
+    mat("QN", "M4", 0, 128, 128, c128, "ci", "qt", 1.0)
+    mat("QS", "M4", 1, 128, 128, c128, "ci", "qst", 1.0)
+    mm(T.P5[:, 0:160], [(lm("QN"), T.C[:])], ["MQN", "C"], ["P5"])
+    mm(T.P5[:, 160:320], [(lm("QS"), T.C[:])], ["MQS", "C"], ["P5"])
+    cp(T.LQn[:], T.P5[:, 0:160], ["P5"], ["LQn"])
+    cp(T.LQs[:], T.P5[:, 160:320], ["P5"], ["LQs"])
+    ts(T.eQ[:], T.P5[:, 0:160], 10240.0, A.is_ge, None, None, ["P5"], ["eQ0"])
+    lastw["eQ1"] = lastw["eQ0"]
+    for k in range(4):
+        mat("WG%d" % k, "M4", 7 + k, 128, 128, T.kr[:], "kr", "kcw", "mX%d" % k)
+        mat("RG%d" % k, "M8", 4 + k, 128, 128, T.kr[:], "kr", "kc", "mG%d" % k)
+
+    turn = [0]
+
+    def through(e, H, out, okey, tile, tkeys, m, eng, Gs=(0, 1, 2, 3)):
+        for G in Gs:
+            for k in range(2):
+                pk = "P%d" % (turn[0] % 4)
+                o = (e % 2) * 5120 + H * 2560 + G * 640 + k * 320
+                mm(T[pk][:, 0:320], [(lm("%s%d" % (m, G)), tile[:, H * 640 + k * 320:H * 640 + k * 320 + 320])],
+                   ["M%s%d" % (m, G)] + tkeys, [pk])
+                cp(out[:, o:o + 320], T[pk][:, 0:320], [pk], ["%s%d" % (okey, o)], eng[turn[0] % 2])
+                turn[0] += 1
+
+    def slots_in(e, eng):
+        for H in (nearH, 1 - nearH):
+            through(e, H, T.OT, "OT", T["AO%d" % e], ["AO%do" % e, "AO%dn" % e] if H == nearH else ["AO%df" % e], "RG", eng)
+
+    def walls_pe(e, eng):
+        through(e, nearH, T.W, "W", T["AW%d" % e], ["AW%do" % e, "AW%dn" % e], "WG", eng, (0, 1))
+
+    def walls_dma(e, H, halves):
+        aw = T["AW%d" % e]
+        for u in halves:
+            c0 = (e % 2) * 5120 + H * 2560 + u * 1280
+            dma("y", [(T.W[16 * q:16 * q + 16, c0:c0 + 1280],
+                       aw[(64 if q < 4 else 0) + 32 * u:(96 if q < 4 else 32) + 32 * u, H * 640:H * 640 + 640])
+                      for q in range(8)], ["AW%do" % e, "AW%dn" % e] if H == nearH else ["AW%df" % e],
+                ["W%d" % (c0 + 320 * k) for k in range(4)])
+    for e in range(2):
+        walls_dma(e, nearH, (1,))
+        walls_dma(e, 1 - nearH, (0, 1))
+    walls_pe(0, "ss")
+    walls_pe(1, "ss")
+    slots_in(0, "ss")
+    mk("lo", "i", 8.0, A.is_ge)
+    ma("w", "lo", -127.0, 128.0)
+    ma("wn", "lo", -1.0, 1.0)
+    mk("hbw", "wn", -BIG, A.mult)
+    mk("e80", "wn", 80.0, A.mult)
+    ma("sw", "sd", -128.0, 64.0)
+    ma("tz", "pg", 16.0, 15.0)
+    mk("tzs", "tz", "sw", A.add)
+    ma("tl0", "pg", 16.0, "i8")
+    mk("tl1", "tl0", 8.0, A.add)
+    mk("tl0s", "tl0", "sw", A.add)
+    mk("tl1s", "tl1", "sw", A.add)
+    ma("a0", "i", 2.0, "g1")
+    ma("a1", "Gh", 32.0, "a0")
+    ma("tp", "sd", 64.0, "a1")
+    mk("tps", "tp", "sw", A.add)
+    ma("a2", "xq", 16.0, "xi")
+    ma("xst", "sd", 64.0, "a2")
+    mk("xot", "xst", "sw", A.add)
+    mk("tm", "i", 1024.0, A.mult)
+    mk("w1", "b2", "w", A.mult)
+    mk("w0", "w", "w1", A.subtract)
+    ma("t2", "b2", -4.0, "i8")
+    ma("t3", "pg", 16.0, "t2")
+    ma("a5", "sd", -0.5, 0.25)
+    mk("tb", "tm", "a5", A.add)
+    ma("a6", "b1", 3.0, 1.0)
+    ma("a7", "b2", 15.0, 1.0)
+    ma("a8", "b0", 1.0 / 128, 1.0 / 128)
+    mk("a9", "a8", "a6", A.mult)
+    mk("c1", "a9", "a7", A.mult)
+    ma("s8", "i8", -1.0, 8.0)
+    op("v", lambda e: e.memset(T.W[:, E:E + 8], -BIG), [], ["We"])
+    op("v", lambda e: e.memset(T.OT[:, E:E + 16], 0.0), [], ["OTz"])
+    cp(T.OT[:, E:E + 1], col["e80"], [ckey["e80"], "OTz"], ["OTe"])
+    ts(T.slU[:], T.slT[:], col["i"], A.add, None, None, ["slT", "CF"], ["slU"])
+    mat("XO", "M4", 2, 128, 128, c128, "ci", "xot", 1.0)
+    mat("XS", "M4", 3, 128, 128, c128, "ci", "xst", -1.0)
+
+    def own_walls(b, src, ksrc):
+        mm(T.P7[:, 0:160], [(lm("XO"), src)], ["MXO", ksrc], ["P7"])
+        mm(T.P7[:, 160:320], [(lm("XS"), src)], ["MXS", ksrc], ["P7"])
+        cp(T["XO%d" % b][:], T.P7[:, 0:160], ["P7"], ["XO%d" % b])
+        ts(T["xs%d" % b][:], T.P7[:, 160:320], col["tm"], A.add, None, None, ["P7", ckey["tm"]], ["xs%d" % b])
+        cp(T["x%d" % b][:], T["XO%d" % b][:].indirect(T.slU[:]), ["XO%d" % b, "slU"], ["x%d" % b], "s")
+    zk = (("ZKs", "tzs", "w"), ("ZK", "tz", "w"), ("Z1", "tz", 1.0), ("ZV", "tz", -262144.0), ("ZVs", "tzs", -262144.0))
+    for k, (n, t, m) in enumerate(zk):
+        mat(n, "MZ", k, 143, 144, T.ci[:], "ci", t, m)
+    ts(T.DL[:], T.ci[:, 0:16], col["i"], A.is_equal, None, None, ["ci", "CF"], ["DL"])
+    ts(T.mI[:], T.mI[:], 7, A.bitwise_and, None, None, ["mI"], ["mI"])
+    ts(T.MB[:], T.mI[:], col["i8"], A.is_equal, None, None, ["mI", "CF"], ["MB"])
+    ts(T.RS[:], T.RS[:], 0.5, A.is_gt, None, None, ["RS"], ["RS"])
+    ts(T.H2[:], T.RS[:], 2.0, A.mult, None, None, ["RS"], ["H2"])
+
+    def empties(eq, keq):
+        for k in range(16):
+            op("s", lambda e: e.activation(T.EX[:, :, k], eq, AF.Identity, scale=T.DL[:, k:k + 1]), [keq, "DL"], ["EX%d" % k])
+        mm(T.P5[:, 0:80], [(lz("Z1", a), T.EX[:, 5 * a:5 * a + 5, :]) for a in range(16)],
+           ["MZ1"] + ["EX%d" % k for k in range(16)], ["P5"])
+    for dst, sc in (("f1", 1.0), ("f2", 0.5)):
+        ts(T[dst][:], T.bI[:], col["c1"], A.mult, sc, A.mult, ["bI", ckey["c1"]], [dst])
+        ts(T[dst][:], T[dst][:], -0.5 + 2.0 ** -9, A.add, None, None, [dst], [dst])
+        ts(T[dst][:], T[dst][:], MG, A.add, MG, A.subtract, [dst], [dst])
+    ts(T.f2[:], T.f2[:], -2.0, A.mult, None, None, ["f2"], ["f2"])
+    tt(T.f1[:], T.f1[:], T.f2[:], A.add, ["f1", "f2"], ["f1"])
+    ts(T.F9[:], T.ci[:, 0:9], col["s8"], A.is_equal, None, None, ["ci", ckey["s8"]], ["F9"])
+    for k in range(9):
+        ts(T.F[:, k::9], T.f1[:], T.F9[:, k:k + 1], A.max, None, None, ["f1", "F9"], ["F%d" % k])
+    kF = ["F%d" % k for k in range(9)]
+    for k, (n, t) in enumerate((("LQ0", "tl0"), ("LQ1", "tl1"), ("LQ0s", "tl0s"), ("LQ1s", "tl1s"))):
+        mat(n, "M8", 8 + k, 128, 128, c128, "ci", t, "w")
+    for h in range(2):
+        for n in range(2):
+            mk("tn%d%d" % (h, n), "t3", 8.0 * h + 4.0 * n, A.add)
+            for k in range(2):
+                mat("LN%d%d%d" % (h, n, k), "M8", 13 + 4 * h + 2 * n + k, 128, 128, c128, "ci", "tn%d%d" % (h, n), "w%d" % k)
+    mat("HA", "M8", 12, 128, 128, T.pr[:], "pr", "pg", "hbw")
+    mat("P1", "M4", 4, 128, 128, c128, "ci", "tp", 1.0)
+    mat("P2", "M4", 5, 128, 128, c128, "ci", "tp", 0.5)
+    mat("P3", "M4", 6, 128, 128, c128, "ci", "tps", -0.5)
+    tt(lm("P2"), lm("P2"), lm("P3"), A.add, ["MP2", "MP3"], ["MP2"])
+
+    kW = ["We"] + ["W%d" % (320 * k) for k in range(32)]
+    kOT = ["OTe"] + ["OT%d" % (320 * k) for k in range(32)]
+    W, OT = T.W[:, 0:E + 8], T.OT[:, 0:E + 16]
+
+    def invert(b):
+        f, i, v = T.nf[:, 0:80], T.ti[:, 0:80], T.hI[:, 0:80]
+        acc, y = T.C[:, 0:80], T.yi[:, 0:80]
+        a = [(cp, (i, T.QF[:], ["QF"], ["ti"])), (ts, (acc, T.QF[:], 10240.0, A.is_ge, 10080.0, A.mult, ["QF"], ["C"])),
+             (ts, (v, i, 5, A.logical_shift_right, None, None, ["ti"], ["hI"])),
+             (ts, (f, v, 0.2, A.mult, -0.4, A.add, ["hI"], ["nf"])), (cp, (y, f, ["nf"], ["yi"]))]
+        a += terms(acc, [(5, T.QF[:], "QF", 0), (80, i, "ti", 4), (-319, i, "ti", 5), (1275, y, "yi", 0)] +
+                   [(k, y, "yi", sh) for sh, k in ((2, -4800), (4, 3840), (5, -10160))], 80)
+        return a + [(cp, (T.YO[:, b * 80 + c:b * 80 + 80:5], T.C[:, c * 16:c * 16 + 16], ["C"], ["YO%d" % b])) for c in range(5)]
+
+    def put_slots(b):
+        dma("y", [(T.yo[16 * gg + 8 * sd:16 * gg + 8 * sd + 8, b * 80:b * 80 + 80],
+                   T.YO[64 * sd + 8 * gg:64 * sd + 8 * gg + 8, b * 80:b * 80 + 80]) for sd in range(2) for gg in range(8)],
+            ["YO%d" % b], [])
+
+    def turn_walls(b, src, ks):
+        for c in range(5):
+            ts(T.Y[:, b, :, c::5], src[:, c * 32:c * 32 + 32], col["sgn"], A.mult, None, None, [ks, ckey["sgn"]], ["Y%d" % b])
+
+    def put_walls(b, qs):
+        for sd, o in ((0, T.yl), (1, T.yr)):
+            dma(qs[sd], [(o[16 * (2 * G + h):16 * (2 * G + h) + 16, b * 80:b * 80 + 80], T.Y[wr(sd, G), b, h, :])
+                         for G in range(4) for h in range(2)], ["Y%d" % b], [])
+
+    def rnd(t):
+        b = t % 2
+        e = t + 2
+        lqn = (T.LQn[:, b * 80:b * 80 + 80], T.LQs[:, b * 80:b * 80 + 80]) if t < 2 else (T.LMn[:], T.LMs[:])
+        kl = ("LQn", "LQs") if t < 2 else ("LMn", "LMs")
+        x, kx = T["x%d" % b][:], "x%d" % b
+        empties(T.eQ[:, 80 * b:80 * b + 80], "eQ%d" % b)
+        op("s", lambda q: q.activation(T.u[:], W.indirect(lqn[0]), AF.Identity), kW + [kl[0]], ["u"])
+        op("v", lambda q: q.tensor_tensor(T.gO[:], OT.indirect(lqn[1]), T.MB[:, 16 * t:16 * t + 1280], A.mult), kOT + [kl[1], "MB"], ["gO"])
+        mm(T.P0[:, 0:80], [(lz("ZKs", a), T.gO[:, 80 * a:80 * a + 80]) for a in range(16)], ["MZKs", "gO"], ["P0"])
+        mm(T.P1[:, 0:80], [(lz("ZK", a), T.gO[:, 80 * a:80 * a + 80]) for a in range(16)], ["MZK", "gO"], ["P1"])
+
+        ms = [1 + (t + 3 * q) % 7 for q in range(2)]
+
+        def diffs(q):
+            m, d = ms[q], T["d%d" % q]
+            hb = m.bit_length() - 1
+            need("v", ["u"], ["d%d" % q])
+            for k in range(1 << hb):
+                out = d[:] if hb == 0 else d[:, :, :, k] if hb == 1 else d[:, :, k >> 1, k & 1]
+                tt(out, T.u[:, (k ^ m)::2 << hb], T.u[:, k::2 << hb], A.subtract, ["u"], ["d%d_%d" % (q, k)])
+            done(("qv", tot["qv"], "v"), [], ["d%d" % q])
+
+        def parts(q):
+            m, d, vv = ms[q], T["d%d" % q], T["V%d" % q]
+            hb = m.bit_length() - 1
+            f = m ^ (1 << hb)
+            need("s", ["d%d" % q], ["V%d" % q])
+
+            def act(o, i, s):
+                op("s", lambda qq: qq.activation(o, i, AF.Relu, scale=s), ["d%d" % q], [])
+            if hb == 0:
+                act(vv[:, :, :, :, 0], d[:], -1.0)
+                act(vv[:, :, :, :, 1], d[:], 1.0)
+            elif hb == 1:
+                act(vv[:, :, :, 0, :], d[:], -1.0)
+                if f == 0:
+                    act(vv[:, :, :, 1, :], d[:], 1.0)
+                else:
+                    for k in range(2):
+                        act(vv[:, :, :, 1, 1 - k], d[:, :, :, k], 1.0)
+            else:
+                act(vv[:, :, 0, :, :], d[:], -1.0)
+                if f == 0:
+                    act(vv[:, :, 1, :, :], d[:], 1.0)
+                for k in range(2 if f else 0):
+                    if f == 1:
+                        act(vv[:, :, 1, :, 1 - k], d[:, :, :, k], 1.0)
+                    else:
+                        act(vv[:, :, 1, 1 - k, :], d[:, :, k, :], 1.0)
+            done(("qs", tot["qs"], "s"), [], ["V%d" % q])
+
+        def sums(q):
+            mm(T["P%d" % (2 + q)][:, 0:80], [(lz("Z1", a), T["V%d" % q][:, 10 * a:10 * a + 10, :, :, :]) for a in range(16)],
+               ["MZ1", "V%d" % q], ["P%d" % (2 + q)])
+
+        def gone():
+            for q in range(2):
+                ts(T["g%d" % q][:], T["P%d" % (2 + q)][:, 0:80], 0.5, A.is_lt, None, None, ["P%d" % (2 + q)], ["g%d" % q])
+            for q in range(2):
+                gt, gk, m = T["g%d" % q], "g%d" % q, ms[q]
+                st = 2 << (m.bit_length() - 1)
+                need("v", [gk], [])
+                for k in range(st // 2):
+                    op("v", lambda qq: qq.tensor_tensor(gt[:, k::st], gt[:, k::st], gt[:, (k ^ m)::st], A.is_gt))
+                done(("qv", tot["qv"], "v"), [], [gk])
+        cp(T.L1[:], T.P0[:, 0:80], ["P0"], ["L1"])
+        cp(T.L2[:], T.P1[:, 0:80], ["P1"], ["L2"])
+        op("v", lambda q: q.tensor_tensor(T.cm1[:], W.indirect(T.L1[:]), x, A.is_gt), kW + ["L1", kx], ["cm1"])
+        mm(T.P4[:, 0:80], [(lz("ZV", a), T.cm1[:, a::16]) for a in range(16)], ["MZV", "cm1"], ["P4"], True, False)
+        for q in range(2):
+            diffs(q)
+            parts(q)
+            sums(q)
+        op("v", lambda q: q.tensor_tensor(T.cm2[:], W.indirect(T.L2[:]), x, A.is_lt), kW + ["L2", kx], ["cm2"])
+        mm(T.P4[:, 0:80], [(lz("ZVs", a), T.cm2[:, a::16]) for a in range(16)], ["MZVs", "cm2"], ["P4"], False, True)
+        tt(T.kb[:], T.KC[:], T.P0[:, 0:80], A.subtract, ["KC", "P0"], ["kb"])
+        gone()
+        tt(T.gs[:], T.g0[:], T.g1[:], A.max, ["g0", "g1"], ["gs"])
+        ts(T.gm[:], T.gs[:], -262144.0, A.mult, None, None, ["gs"], ["gm"])
+        tt(T.gb[:], T.P5[:, 0:80], T.gs[:], A.max, ["gs", "P5"], ["gb"])
+        tt(T.kb2[:], T.kb[:], T.gm[:], A.add, ["kb", "gm"], ["kb2"])
+        op("v", lambda q: q.tensor_tensor_scan(T.sc[:], T.H2[:], T.gb[:], 0.0, A.mult, A.add), ["H2", "gb"], ["sc"])
+        tt(T.da[:], T.P4[:, 0:80], T.kb2[:], A.add, ["P4", "kb2"], ["da"])
+        ts(T.fb[:], T.sc[:, 7::8], 9.0, A.mult, None, None, ["sc"], ["fb"])
+        op("v", lambda q: q.tensor_tensor_scan(T.RM[:], T.RS[:], T.da[:], 0.0, A.mult, A.max), ["RS", "da"], ["RM"])
+        cp(T.Mi[:], T.RM[:, 7::8], ["RM"], ["Mi"])
+        ts(T.cd[:], T.Mi[:], 14, A.logical_shift_right, None, None, ["Mi"], ["cd"])
+        ts(T.cv[:], T.Mi[:], 16383, A.bitwise_and, None, None, ["Mi"], ["cv"])
+        tt(T.cx[:], T.cd[:], T.fb[:], A.add, ["cd", "fb"], ["cx"])
+        ts(T.cu[:], T.cv[:], -1.0, A.mult, 10240.0, A.add, ["cv"], ["cu"])
+        cp(T.iu[:], T.cx[:], ["cx"], ["iu"])
+        op("s", lambda q: q.activation(T.FT[:], T.F[:].indirect(T.iu[:]), AF.Identity), kF + ["iu"], ["FT"])
+        old, ko = T["AO%d" % t][:, own:own + 160], "AO%do" % t
+        op("v", lambda q: q.tensor_tensor(T.dT[:], OT.indirect(T.cu[:]), old, A.subtract), kOT + ["cu", ko], ["dT"])
+        tt(T.mT[:], T.dT[:], T.FT[:], A.mult, ["dT", "FT"], ["mT"])
+        tt(T.TN[:], T.mT[:], old, A.add, ["mT", ko], ["TN"])
+        for k in range(2):
+            mm(T.P5[:, 40 * k:40 * k + 40], [(lm("LN%d%d%d" % (h, n, k)), T.TN[:, :, h, n::2]) for h in range(2) for n in range(2)],
+               ["MLN%d%d%d" % (h, n, k) for h in range(2) for n in range(2)] + ["TN"], ["P5"])
+        cp(T.LN[:], T.P5[:, 0:80], ["P5"], ["LN"])
+        if t < 2:
+            cp(T["AO%d" % e][:, own:own + 160], T.TN[:], ["TN"], ["AO%do" % e], "s")
+            send("o", e)
+        mm(T.P4[:, 160:240], [(lm("LQ0"), T.TN[:, :, 0, :]), (lm("LQ1"), T.TN[:, :, 1, :])], ["MLQ0", "MLQ1", "TN"], ["P4"])
+        for k in range(2):
+            cp(T.w[:, 320 * k:320 * k + 320], W.indirect(T.LN[:, 20 * k:20 * k + 20]), kW + ["LN"], ["w%d" % k], "s")
+        inv = []
+        if t > 0:
+            cp(T.QF[:], T.P4[:, 160:240], ["P4"], ["QF"])
+            inv = invert(b) if t == 2 else []
+        ts(T.nd[:], T.TN[:], 79.5, A.is_lt, None, None, ["TN"], ["nd"])
+        run(inv[0:5])
+        mm(T.P6[:, 0:160], [(lm("HA"), T.nd[:])], ["MHA", "nd"], ["P6"])
+        for k in range(2):
+            o = 320 * k
+            op("v", lambda q: q.tensor_tensor(T.t1[:, o:o + 320], W.indirect(T.LN[:, 40 + 20 * k:60 + 20 * k]), T.w[:, o:o + 320], A.max),
+               kW + ["LN", "w%d" % k], ["t1%d" % k])
+        tt(T.xx[:], T.P6[:, 0:160], T["xs%d" % b][:], A.add, ["P6", "xs%d" % b], ["xx"])
+        tt(T.t2[:], T.t1[:, 0::2], T.t1[:, 1::2], A.max, ["t10", "t11"], ["t2"])
+        for h in range(2):
+            for n in range(2):
+                tt(T.m4[:, :, h, n::2], T.t2[:, :, :, h, n, 0], T.t2[:, :, :, h, n, 1], A.max, ["t2"], ["m4%d%d" % (h, n)])
+        tt(T.mm[:], T.m4[:], T.xx[:], A.max, ["m400", "m401", "m410", "m411", "xx"], ["mm"])
+        ts(T.nn[:], T.mm[:], -1.0, A.mult, col["tb"], A.add, ["mm", ckey["tb"]], ["nn"])
+        mm(T.P6[:, 0:160], [(lm("P1"), T.nn[:])], ["MP1", "nn"], ["P6"])
+        mm(T.P7[:, 0:160], [(lm("P2"), T.nn[:])], ["MP2", "nn"], ["P7"])
+        run(inv[5:13])
+        cp(T.pp[:], T.P6[:, 0:160], ["P6"], ["pp"], "s")
+        tt(T.qq[:], T.P7[:, 0:160], T.pp[:], A.min, ["P7", "pp"], ["qq"])
+        dst, kd = (T["AW%d" % e][:, own:own + 160], "AW%do" % e) if t < 2 else (T.RF[:], "RF")
+        ts(dst, T.qq[:], MG, A.add, MG, A.subtract, ["qq"], [kd])
+        if t < 2:
+            send("w", e)
+        return dst, kd, inv[13:]
+
+    own_walls(0, T.AW0[:, own:own + 160], "AW0o")
+    slots_in(1, "sv")
+    dst, kd, inv = rnd(0)
+    own_walls(1, T.AW1[:, own:own + 160], "AW1o")
+    mm(T.P4[:, 240:320], [(lm("LQ0s"), T.TN[:, :, 0, :]), (lm("LQ1s"), T.TN[:, :, 1, :])], ["MLQ0s", "MLQ1s", "TN"], ["P4"])
+    for c in range(5):
+        cp(T.LMn[:, c::5], T.P4[:, 160 + c * 16:176 + c * 16], ["P4"], ["LMn"])
+        cp(T.LMs[:, c::5], T.P4[:, 240 + c * 16:256 + c * 16], ["P4"], ["LMs"])
+    ts(T.eQ[:, 0:80], T.LMn[:], 10240.0, A.is_ge, None, None, ["LMn"], ["eQ0"])
+    own_walls(0, dst, kd)
+    for H in (nearH, 1 - nearH):
+        walls_dma(2, H, (0, 1))
+    slots_in(2, "sv")
+    dst, kd, inv = rnd(1)
+    turn_walls(1, dst, kd)
+    run(invert(1))
+    for H in (nearH, 1 - nearH):
+        walls_dma(3, H, (0, 1))
+    slots_in(3, "sv")
+    put_walls(1, "yy")
+    put_slots(1)
+    dst, kd, inv = rnd(2)
+    turn_walls(0, dst, kd)
+    put_walls(0, "ys")
+    run(inv)
+    put_slots(0)
+    for s in tot:
+        if waited["g"].get(s, 0) < tot[s]:
+            g.wait_ge(T.sem[s], tot[s])

@@ -1,35 +1,35 @@
 from concourse.bass import DstId, RemoteDMATransfer
 from concourse.mybir import AluOpType as A, ActivationFunctionType as AF
 
-N, V, B, E = 8, 160, 80, 10240
-BIG = 8388608.0
+N = 8
+EC, WD = 10368, 10384
+BIG, HUGE, PEN = 2097152.0, 8388608.0, 262144.0
 MG = 12582912.0
-FI, FB, II, UU = "float32", "bfloat16", "int32", "uint16"
+THR, TB = -15.03, 1.71699
+FI, FB, FH, II, UU = "float32", "bfloat16", "float16", "int32", "uint16"
 SCRATCH = {
-    "W": ("sbuf", [128, E + 8], FI), "OT": ("sbuf", [128, E + 16], FB),
-    "MB": ("sbuf", [128, 1312], FB), "mI": ("sbuf", [128, 1312], II),
+    "W": ("sbuf", [128, WD], FI), "OT": ("sbuf", [128, WD], FB),
+    "AOi": ("sbuf", [128, N, 2, 160], FB), "AWi": ("sbuf", [128, N, 2, 320], FH),
+    "AO0": ("sbuf", [128, N, 160], FB), "AO1": ("sbuf", [128, N, 160], FB), "TN": ("sbuf", [128, 160], FB),
+    "AW0": ("sbuf", [128, N, 2, 160], FH), "AW1": ("sbuf", [128, N, 2, 160], FH),
     "d0": ("sbuf", [128, 160, 2, 2], FB), "d1": ("sbuf", [128, 160, 2, 2], FB),
     "V0": ("sbuf", [128, 160, 2, 2, 2], FB), "V1": ("sbuf", [128, 160, 2, 2, 2], FB),
-    "F": ("sbuf", [128, 2304], FB), "EX": ("sbuf", [128, 80, 16], FB),
-    "t1": ("sbuf", [128, 640], FI), "t2": ("sbuf", [128, 5, 8, 2, 2, 2], FI), "m4": ("sbuf", [128, 5, 2, 16], FI),
-    "X": ("sbuf", [128, 2, 2, 80], II), "Y": ("sbuf", [128, 2, 2, 80], FI), "TN": ("sbuf", [128, 5, 2, 16], FB),
-    "HB": ("sbuf", [128, 2, 5, 16], FB), "LB": ("sbuf", [128, 2, 5, 16], FB), "T4": ("sbuf", [128, 2, 5, 2, 16], FB),
-    "CI": ("sbuf", [128, 16], II), "CF": ("sbuf", [128, 16], FI), "CC": ("sbuf", [128, 64], FI),
-    "ci": ("sbuf", [128, 143], FI), "kr": ("sbuf", [128, 128], FI), "pr": ("sbuf", [128, 128], FI),
-    "DL": ("sbuf", [128, 16], FI), "F9": ("sbuf", [128, 9], FI),
-    "MZ": ("sbuf", [128, 720], FB), "M8": ("sbuf", [128, 2688], FB), "M4": ("sbuf", [128, 1408], FI),
+    "CI": ("sbuf", [128, 12], II), "CF": ("sbuf", [128, 12], FI), "CC": ("sbuf", [128, 48], FI), "CB": ("sbuf", [128, 2], FB),
+    "ZK": ("sbuf", [128, 8, 144], FB), "RW": ("sbuf", [128, 2, 128], FB), "RI": ("sbuf", [128, 4, 128], FB),
+    "RO": ("sbuf", [128, 4, 128], FB), "LM": ("sbuf", [128, 2, 140], FB),
 }
-for _n, _w, _t in (("u x0 x1 AW0 AW1 AW2 AW3", 1280, FI), ("gO cm1 cm2 AO0 AO1 AO2 AO3", 1280, FB), ("bI f1 f2", 256, FI),
-                   ("w", 640, FI), ("RAW yi si0 si1 si2 ti hI lI", 160, II), ("FT dT mT nd", 160, FB), ("LQn LQs", 160, UU),
-                   ("YO C nf tf tf0 tf1 tf2 eQ XO0 XO1 xs0 xs1 xx mm nn pp qq RF", 160, FI), ("LMn LMs L1 L2 LN slU", 80, UU),
-                   ("slT", 80, II), ("KC RS H2 kb kb2 g0 g1 gs gm gb sc da RM QF", 80, FI), ("fb cx", 10, FI), ("Mi cd cv", 10, II),
-                   ("iu cu", 10, UU)):
+for _n, _w, _t in (("u x", 1280, FI), ("gO cm1 cm2", 1280, FB), ("w t1 sw", 640, FI), ("rw4", 640, FB),
+                   ("O32 X32 qi yi hI lI", 320, II), ("ta tb", 320, FI), ("bI", 256, FI), ("fI", 256, II), ("F", 256, FB),
+                   ("ci pr OA OB OH c64 c1 XO0 XO1 y1 q1 q2 r1 FF Yl Yr Yo", 160, FI), ("old0 old1 dT mT nd ind YM", 160, FB),
+                   ("Zs Z1 ZV ZVs", 144, FB), ("LQ", 136, FB), ("kI HA", 128, FB), ("Ms Mo Mh", 128, FI),
+                   ("LQn0 LQn1 LQs0 LQs1 L1 L2 LN xl", 80, UU), ("xI", 80, II),
+                   ("em a1 th y gm gb gk gr sc da e0 e1 S1 S2 H2 CS RR mid", 80, FI), ("cx DL", 10, FI), ("cu iu ol", 10, UU)):
     for _k in _n.split():
         SCRATCH[_k] = ("sbuf", [128, _w], _t)
-for _k in range(8):
-    SCRATCH["P%d" % _k] = ("psum", [128, 512], FI)
-SEMAPHORES = ["qv", "qt", "qs", "qg", "ls"] + ["%s%s%d" % (a, b, e) for a in ("rw", "ro") for b in ("n", "f") for e in range(4)] \
-    + ["dm%d" % k for k in range(32)]
+for _k in "ABCD":
+    SCRATCH["P" + _k] = ("psum", [128, 2, 512], FI)
+TILES = ("AOi", "AWi", "AO0", "AW0", "AO1", "AW1")
+SEMAPHORES = ["qv", "qt", "qs", "qg", "ls"] + ["%s%d" % (a, r) for a in TILES for r in range(N)] + ["dm%d" % k for k in range(12)]
 
 
 def rank_program(g, core, T, topo):
@@ -74,23 +74,25 @@ def rank_program(g, core, T, topo):
         fn(QU[q]).then_inc(T.sem[s], 1)
         done((s, tot[s], q), r, w)
 
-    def dma(q, pairs, r=(), w=()):
-        need(q, r, w)
+    def dma(parts, r=(), w=()):
         s = "dm%d" % ndma[0]
         ndma[0] += 1
-        for o, i in pairs:
+        for q, o, i in parts:
+            need(q, r, w)
             QU[q].dma_start(o, i).then_inc(T.sem[s], 16)
-        tot[s] = 16 * len(pairs)
+        tot[s] = 16 * len(parts)
         done((s, tot[s], "d" + s), r, w)
 
-    def mm(out, pairs, r, w, first=True, last=True):
+    def mms(lst, r, w):
         need("t", r, w)
-        for k, (l, x) in enumerate(pairs):
-            ins = g.tensor.matmul(out, l, x, first and k == 0, last and k == len(pairs) - 1)
-            if k == len(pairs) - 1:
-                tot["qt"] = tot.get("qt", 0) + 1
-                ins.then_inc(T.sem.qt, 1)
-                done(("qt", tot["qt"], "t"), r, w)
+        for o, l, x, a, z in lst:
+            ins = g.tensor.matmul(o, l, x, a, z)
+        tot["qt"] = tot.get("qt", 0) + 1
+        ins.then_inc(T.sem.qt, 1)
+        done(("qt", tot["qt"], "t"), r, w)
+
+    def mm(out, pairs, r, w, first=True, last=True):
+        mms([(out, l, x, first and k == 0, last and k == len(pairs) - 1) for k, (l, x) in enumerate(pairs)], r, w)
 
     def ts(out, i, s1, o1, s2=None, o2=None, r=(), w=()):
         if o2 is None:
@@ -101,485 +103,417 @@ def rank_program(g, core, T, topo):
     def tt(out, a, b, o, r, w):
         op("v", lambda e: e.tensor_tensor(out, a, b, o), r, w)
 
-    def cp(out, i, r, w, q="v"):
+    def cp(out, i, r, w, q="v", bias=0.0):
         if q == "v":
             op("v", lambda e: e.tensor_copy(out, i), r, w)
         else:
-            op("s", lambda e: e.activation(out, i, AF.Identity), r, w)
+            op("s", lambda e: e.activation(out, i, AF.Identity, bias=bias), r, w)
 
-    own = rank * 160
-    nearH = 0 if topo.host(T.cores[0]) == topo.host(core) else 1
-    partner = [c for c in T.cores if c != core and c in topo.cores_of(core)]
-    near = [c for c in T.cores if topo.host(c) == topo.host(core) and c != core and c not in partner]
-    far = [c for c in T.cores if topo.host(c) != topo.host(core)]
-    far = [c for c in far if topo.same_plane(core, c)] + [c for c in far if not topo.same_plane(core, c)]
-    offe = topo.engines(core, far[0])
-    one = [e for e in topo.engines(core, partner[0]) if e not in offe]
-    moff, mon = sum(1 << e for e in offe), sum(1 << e for e in one)
+    def scan(out, a, b, o0, o1, r, w):
+        op("v", lambda e: e.tensor_tensor_scan(out, a, b, 0.0, o0, o1), r, w)
 
-    def send(kind, e):
-        name = "A%s%d" % (kind.upper(), e)
-        src = T[name][:, own:own + 160]
-        need("g", [name + "o"], [])
+    def fill(ap, c, key):
+        op("v", lambda e: e.memset(ap, c), [], [key])
 
-        def tr(dst, m, sem):
+    def iota(ap, key, pat, base=0, ch=0, whole=False):
+        if whole:
+            op("g", lambda e: e.iota(ap, pat, base, ch), [], [key])
+        else:
+            op("g", lambda e: e.iota(ap, pat, base, ch, allow_small_or_imprecise_dtypes=True), [], [key])
+
+    def pick(ap, key, src, ksrc, pat, base, more=None):
+        op("g", lambda e: e.affine_select(ap, src, pat, A.is_equal, 0.0, base, -1), [ksrc], [key])
+        if more:
+            op("g", lambda e: e.affine_select(ap, ap, pat, A.not_equal, more[1], more[0], -1), [key], [key])
+
+    def bank(k):
+        return T["P" + k[1]][:, int(k[2]), :]
+    LO, HI = slice(0, 64), slice(64, 128)
+
+    def kind(c):
+        same = topo.die(c) == topo.die(core)
+        if c in topo.cores_of(core):
+            return 0
+        if topo.mates(core, c):
+            return 1 if same else 3
+        if topo.same_plane(core, c):
+            return 2 if same else 4
+        return 5 if same else 6
+    others = sorted([c for c in T.cores if c != core], key=kind)
+    order = [rank] + [T.rank_of(c) for c in others]
+    offe = topo.engines(core, others[-1])
+    one = [e for e in topo.engines(core, others[0]) if e not in offe]
+
+    def send(name):
+        src = T[name][:, rank]
+        need("g", ["%s%d" % (name, rank)], [])
+        trs = []
+        for dst, es in ((others[:1], one), (others[1:], offe)):
             ids = []
             for c in dst:
                 rid, pid = topo.addr(c, core)
                 ids.append(DstId(rid=rid, pnc=pid))
-            return RemoteDMATransfer(dst_ids=ids, dma_engine_mask=m, remote_sem=T.sem[sem], srcs=[src],
-                                     dsts=[src for _ in dst], alu_op=0)
-        g.remote_dma_fused([tr(partner, mon, "r%sn%d" % (kind, e)), tr(near, moff, "r%sn%d" % (kind, e))], local_sem=T.sem.ls)
-        g.remote_dma_fused([tr(far, moff, "r%sf%d" % (kind, e))], local_sem=T.sem.ls)
-        tot["ls"] = tot.get("ls", 0) + len(one) + 2 * len(offe)
-        for s, n in (("n", len(one) + len(near) * len(offe)), ("f", len(far) * len(offe))):
-            sem = "r%s%s%d" % (kind, s, e)
-            tot[sem] = n
-            lastw[name + s] = [(sem, n, "x")]
+            trs.append(RemoteDMATransfer(dst_ids=ids, dma_engine_mask=sum(1 << e for e in es), remote_sem=T.sem["%s%d" % (name, rank)],
+                                         srcs=[src], dsts=[src for _ in dst], alu_op=0))
+        g.remote_dma_fused(trs, local_sem=T.sem.ls)
+        tot["ls"] = tot.get("ls", 0) + len(one) + len(offe)
+        for j, r in enumerate(order[1:]):
+            k = "%s%d" % (name, r)
+            tot[k] = len(offe) if j else len(one)
+            lastw[k] = [(k, tot[k], "x")]
 
-    def wr(sd, G):
-        o = 64 * sd + 32 * (G // 2)
-        return slice(o + G % 2, o + 32, 2)
+    def base(b, r):
+        return 128 + 5120 * (1 - b) + 640 * r
 
-    for q, sd, t, k in (("y", 0, T.lw, "XA"), ("s", 1, T.rw, "XB")):
-        dma(q, [(T.X[wr(sd, G), :, h, :], t[16 * (2 * G + h):16 * (2 * G + h) + 16, :])
-                for G in range(4) for h in range(2)], [], [k])
-    dma("y", [(T.RAW[:], T.opts[:])], [], ["RAW"])
+    dma([("ys"[u], T.O32[64 * hl:64 * hl + 64, 160 * u:160 * u + 160], T.opts[64 * u:64 * u + 64, :])
+         for hl in range(2) for u in range(2)], [], ["O32"])
+    dma([("ys"[sd], T.X32[64 * u + 32 * sd:64 * u + 32 * sd + 32, 160 * j:160 * j + 160],
+          (T.rw, T.lw)[sd][64 * u + 32 * j:64 * u + 32 * j + 32, :]) for u in range(2) for j in range(2) for sd in range(2)], [], ["X32"])
 
-    def iota(name, pat, base=0, ch=0):
-        if name in ("CI", "mI", "slT"):
-            out = T.CI[:, 0:1] if name == "CI" else T[name][:]
-            op("g", lambda e: e.iota(out, pat, base, ch), [], [name])
-        else:
-            op("g", lambda e: e.iota(T[name][:], pat, base, ch, allow_small_or_imprecise_dtypes=True), [], [name])
-    iota("CI", [[0, 1]], 0, 1)
-    iota("ci", [[1, 143]])
-    iota("kr", [[16, 2], [0, 4], [1, 16]])
-    names = ["p", "i", "i8", "pg", "sd", "Gp", "xi", "xG", "rs", "g1", "gG", "b0", "b1", "b2", "xh", "Gh"]
-    spec = [None, (0, 15), (0, 7), (4, 7), (6, 1), (4, 3), (1, 15), (0, 1), (3, 1), (4, 1), (5, 3), (0, 1), (1, 1), (2, 1),
-            (5, 1), (5, 1)]
-    for k, s in enumerate(spec):
-        if s:
-            ts(T.CI[:, k:k + 1], T.CI[:, 0:1], s[0], A.logical_shift_right, s[1], A.bitwise_and, ["CI"], ["CI%d" % k])
-    cp(T.CF[:], T.CI[:], ["CI"] + ["CI%d" % k for k in range(1, 16)], ["CF"])
-    col = {n: T.CF[:, k:k + 1] for k, n in enumerate(names)}
-    ckey = {n: "CF" for n in names}
-    nc = [0]
+    iota(T.CI[:, 0:1], "CI", [[0, 1]], 0, 1, True)
+    fill(T.c64[:], 64.0, "c64")
+    col, ckey = {}, {}
+
+    def bits(lst, k0):
+        for k, (n, sh, m) in enumerate(lst):
+            ts(T.CI[:, k0 + k:k0 + k + 1], T.CI[:, 0:1], sh, A.logical_shift_right, m, A.bitwise_and, ["CI"], ["CI" + n])
+            col[n], ckey[n] = T.CF[:, k0 + k:k0 + k + 1], "CF%d" % k0
+        cp(T.CF[:, k0:k0 + len(lst)], T.CI[:, k0:k0 + len(lst)], ["CI" + n for n, _, _ in lst], ["CF%d" % k0])
 
     def mk(name, src, s1, o1, s2=None, o2=None):
-        def val(s):
-            return col[s] if isinstance(s, str) else s
-        k = nc[0]
-        nc[0] += 1
-        rk = [ckey[src]] + [ckey[s] for s in (s1, s2) if isinstance(s, str)]
-        ts(T.CC[:, k:k + 1], col[src], val(s1), o1, val(s2), o2, rk, ["CC%d" % k])
+        k = len([n for n in ckey if ckey[n][:2] == "CC"])
+        ts(T.CC[:, k:k + 1], col[src], col.get(s1, s1), o1, col.get(s2, s2), o2,
+           [ckey[s] for s in (src, s1, s2) if s in ckey], ["CC%d" % k])
         col[name], ckey[name] = T.CC[:, k:k + 1], "CC%d" % k
 
     def ma(name, src, m, a):
         mk(name, src, m, A.mult, a, A.add)
-    ma("sgn", "sd", 2.0, -1.0)
-    for b in range(2):
-        aw = T["AW%d" % b]
-        for c in range(5):
-            ts(aw[:, own + c * 32:own + c * 32 + 32], T.X[:, b, :, c::5], col["sgn"], A.mult, None, None,
-               ["XA", "XB", ckey["sgn"]], ["AW%do" % b])
-        send("w", b)
-    iota("mI", [[1, 82], [0, 16]])
-    iota("slT", [[16, 10], [0, 8]])
-    iota("RS", [[0, 10], [1, 8]])
-    iota("bI", [[1, 256]])
-    iota("KC", [[0, 10], [-16384, 8]], 141312)
-    iota("pr", [[1, 8], [0, 16]])
-    cp(T.nf[:], T.RAW[:], ["RAW"], ["nf"])
-    ts(T.tf[:], T.nf[:], 0.2, A.mult, -0.4, A.add, ["nf"], ["tf"])
-    cp(T.yi[:], T.tf[:], ["tf"], ["yi"])
-    ts(T.C[:], T.nf[:], 10240.0, A.is_ge, 5120.0, A.mult, ["nf"], ["C"])
 
-    def terms(acc, lst, n):
-        st, kacc = [], "C"
-        for j, (f, x, kx, sh) in enumerate(lst):
-            s, t, ks, kt = T["si%d" % (j % 3)][:, 0:n], T["tf%d" % (j % 3)][:, 0:n], "si%d" % (j % 3), "tf%d" % (j % 3)
-            one = [None, (ts, (t, x, float(f), A.mult, None, None, [kx], [kt])), (tt, (acc, acc, t, A.add, [kacc, kt], [kacc]))]
-            if sh:
-                one[0] = (ts, (s, x, sh, A.logical_shift_right, None, None, [kx], [ks]))
-                one[1] = (ts, (t, s, float(f), A.mult, None, None, [ks], [kt]))
-            st += [(2 * j + 3 * k, j, o) for k, o in enumerate(one) if o]
-        return [o for _, _, o in sorted(st, key=lambda z: z[:2])]
-
-    def run(steps):
-        for f, a in steps:
-            f(*a)
-    run(terms(T.C[:], [(32, T.nf[:], "nf", 0), (-159, T.yi[:], "yi", 0)] +
-              [(f, T.yi[:], "yi", sh) for sh, f in ((4, 5104), (5, -10224), (6, 608), (8, -2400), (10, 1920))], 160))
-    cp(T.ti[:], T.C[:], ["C"], ["ti"])
-    ts(T.hI[:], T.ti[:], 7, A.logical_shift_right, None, None, ["ti"], ["hI"])
-    ts(T.lI[:], T.ti[:], 127, A.bitwise_and, None, None, ["ti"], ["lI"])
-    for c in range(5):
-        cp(T.HB[:, :, c, :], T.hI[:, c::5], ["hI"], ["HB%d" % c])
-        cp(T.LB[:, :, c, :], T.lI[:, c::5], ["lI"], ["LB%d" % c])
-    ma("a4", "gG", 16.0, "i8")
-    ma("th", "rs", 64.0, "a4")
-    mk("tlo", "th", 8.0, A.add)
-    ma("m0", "g1", -1.0, 1.0)
-
-    mats = {}
-
-    def mat(name, buf, k, width, step, row, rk, t, wgt):
-        ap = T[buf][:, k * step:k * step + width]
-        rks = [rk, ckey[t]] + ([ckey[wgt]] if isinstance(wgt, str) else [])
-        ts(ap, row, col[t], A.is_equal, col[wgt] if isinstance(wgt, str) else wgt, A.mult, rks, ["M" + name])
-        mats[name] = (buf, k * step)
-
-    def lz(name, a):
-        buf, k = mats[name]
-        return T[buf][:, k + 15 - a:k + 143 - a]
-
-    def lm(name):
-        buf, k = mats[name]
-        return T[buf][:, k:k + 128]
-    c128 = T.ci[:, 0:128]
-    for k, (n, t, m) in enumerate((("TH0", "th", "m0"), ("TL0", "tlo", "m0"), ("TH1", "th", "g1"), ("TL1", "tlo", "g1"))):
-        mat(n, "M8", k, 128, 128, c128, "ci", t, m)
-    hb = ["HB%d" % c for c in range(5)] + ["LB%d" % c for c in range(5)]
-    for b in range(2):
-        for h in range(2):
-            o = (b * 2 + h) * 80
-            mm(T.P6[:, o:o + 80], [(lm("TH%d" % h), T.HB[:, b, :, :]), (lm("TL%d" % h), T.LB[:, b, :, :])],
-               ["MTH%d" % h, "MTL%d" % h] + hb, ["P6"])
-    for b in range(2):
-        for h in range(2):
-            o = (b * 2 + h) * 80
-            cp(T.T4[:, b, :, h, :], T.P6[:, o:o + 80], ["P6"], ["T4%d%d" % (b, h)])
-        cp(T["AO%d" % b][:, own:own + 160], T.T4[:, b, :, :, :], ["T4%d0" % b, "T4%d1" % b], ["AO%do" % b])
-        send("o", b)
-    ma("swr", "rs", -128.0, 64.0)
-    ma("a3", "pg", 8.0, "i8")
-    ma("qt", "rs", 64.0, "a3")
-    mk("qst", "qt", "swr", A.add)
-    ma("kc", "sd", 16.0, "i")
-    ma("xq", "xh", 2.0, "xG")
-    ma("kw", "sd", -16.0, 16.0)
-    mk("kcw", "kw", "xi", A.add)
+    def tsc(out, i, s1, o1, s2, o2, r, w, part=slice(0, 128)):
+        ts(out, i, col[s1][part] if s1 in col else s1, o1, col[s2][part] if s2 in col else s2, o2,
+           list(r) + [ckey[s] for s in (s1, s2) if s in ckey], w)
+    bits([("sd", 6, 1), ("s5", 5, 1)], 1)
+    for n, s, m, a in (("yc", "sd", 79.5, -79.5), ("ys", "sd", 1 - 1.0 / 160, 1.0 / 160), ("al", "sd", -16.0, -64.0),
+                       ("ga", "sd", 64.0, 64.0), ("be", "sd", -128.0, 129.0), ("sH", "s5", -64.0, 32.0), ("sL", "s5", -1.0 / 32, 1.0 / 64)):
+        ma(n, s, m, a)
+    for sd in range(2):
+        iota(T.kI[:, 64 * sd:64 * sd + 64], "kI%d" % sd, [[0, 4], [64, 2], [1, 8]], 8 * sd, -1)
+    for k in range(2):
+        pick(T.RW[:, k, :], "RW%d" % k, T.c64[:, 0:128], "c64", [[32, 2], [0, 4], [1, 16]], 16 * k, (16 * k + 64, 64.0))
+    iota(T.ci[:], "ci", [[1, 160]])
     for k in range(4):
-        mk("mG%d" % k, "Gp", float(k), A.is_equal)
-        mk("mX%d" % k, "xq", float(k), A.is_equal)
-    mat("QN", "M4", 0, 128, 128, c128, "ci", "qt", 1.0)
-    mat("QS", "M4", 1, 128, 128, c128, "ci", "qst", 1.0)
-    mm(T.P5[:, 0:160], [(lm("QN"), T.C[:])], ["MQN", "C"], ["P5"])
-    mm(T.P5[:, 160:320], [(lm("QS"), T.C[:])], ["MQS", "C"], ["P5"])
-    cp(T.LQn[:], T.P5[:, 0:160], ["P5"], ["LQn"])
-    cp(T.LQs[:], T.P5[:, 160:320], ["P5"], ["LQs"])
-    ts(T.eQ[:], T.P5[:, 0:160], 10240.0, A.is_ge, None, None, ["P5"], ["eQ0"])
-    lastw["eQ1"] = lastw["eQ0"]
-    for k in range(4):
-        mat("WG%d" % k, "M4", 7 + k, 128, 128, T.kr[:], "kr", "kcw", "mX%d" % k)
-        mat("RG%d" % k, "M8", 4 + k, 128, 128, T.kr[:], "kr", "kc", "mG%d" % k)
+        ts(T.RI[:, k, :], T.kI[:], -16.0 * k, A.is_equal, None, None, ["kI0", "kI1"], ["RI"])
+
+    ts(T.qi[:], T.O32[:], -39.5, A.add, 1.0 / 80, A.mult, ["O32"], ["qi"])
+    tsc(T.yi[:], T.O32[:], "yc", A.add, "ys", A.mult, ["O32"], ["yi"])
+    tsc(T.ta[:], T.qi[:], "al", A.mult, "ga", A.add, ["qi"], ["ta"])
+    tsc(T.tb[:], T.yi[:], "be", A.mult, None, None, ["yi"], ["tb"])
+    tt(T.AOi[:, rank], T.ta[:], T.tb[:], A.add, ["ta", "tb"], ["AOi%d" % rank])
+    send("AOi")
+    ts(T.hI[:], T.X32[:], 11, A.arith_shift_right, None, None, ["X32"], ["hI"])
+    ts(T.lI[:], T.X32[:], 2047, A.bitwise_and, None, None, ["X32"], ["lI"])
+    for k, (po, u, src, pi, s) in enumerate(((LO, 0, "hI", LO, "sH"), (HI, 1, "hI", HI, "sH"), (HI, 0, "lI", LO, "sL"), (LO, 1, "lI", HI, "sL"))):
+        tsc(T.AWi[po, rank, u, :], T[src][pi, :], s, A.mult, None, None, [src], ["AWi%d" % rank if k == 3 else "z%d" % k], pi)
+    send("AWi")
 
     turn = [0]
 
-    def through(e, H, out, okey, tile, tkeys, m, eng, Gs=(0, 1, 2, 3)):
-        for G in Gs:
-            for k in range(2):
-                pk = "P%d" % (turn[0] % 4)
-                o = (e % 2) * 5120 + H * 2560 + G * 640 + k * 320
-                mm(T[pk][:, 0:320], [(lm("%s%d" % (m, G)), tile[:, H * 640 + k * 320:H * 640 + k * 320 + 320])],
-                   ["M%s%d" % (m, G)] + tkeys, [pk])
-                cp(out[:, o:o + 320], T[pk][:, 0:320], [pk], ["%s%d" % (okey, o)], eng[turn[0] % 2])
-                turn[0] += 1
+    def spread(name, r, b, eng):
+        pk = "P" + "ABC"[turn[0] % 3]
+        turn[0] += 1
+        P, t = T[pk], T[name]
+        if name == "AOi":
+            lst = [(P[:, u, 80 * k:80 * k + 80], T.RI[:, k, :], t[:, r, u, 80 * b:80 * b + 80]) for u in range(2) for k in range(4)]
+            km = ["RI"]
+        elif name == "AWi":
+            lst = [(P[:, u, 80 * k:80 * k + 80], T.RW[:, k % 2, :], t[:, r, u, 160 * (k // 2) + 80 * b:160 * (k // 2) + 80 * b + 80])
+                   for u in range(2) for k in range(4)]
+            km = ["RW0", "RW1"]
+        elif name[1] == "O":
+            lst = [(P[:, k // 2, 160 * (k % 2):160 * (k % 2) + 160], T.RO[:, k, :], t[:, r, :]) for k in range(4)]
+            km = ["RO%d" % k for k in range(4)]
+        else:
+            lst = [(P[:, k // 2, 160 * (k % 2):160 * (k % 2) + 160], T.RW[:, k % 2, :], t[:, r, k // 2, :]) for k in range(4)]
+            km = ["RW0", "RW1"]
+        mms([x + (True, True) for x in lst], km + ["%s%d" % (name, r)], [pk + "0", pk + "1"])
+        im = "OT" if name[1] == "O" else "W"
+        cp(T[im][:, base(b, r):base(b, r) + 640], P[:, :, 0:320], [pk + "0", pk + "1"], ["%s%d%d" % (im, b, r)], eng)
+    kW = ["We"] + ["W%d%d" % (b, r) for b in range(2) for r in range(N)]
+    kOT = ["OTe"] + ["OT%d%d" % (b, r) for b in range(2) for r in range(N)]
 
-    def slots_in(e, eng):
-        for H in (nearH, 1 - nearH):
-            through(e, H, T.OT, "OT", T["AO%d" % e], ["AO%do" % e, "AO%dn" % e] if H == nearH else ["AO%df" % e], "RG", eng)
+    def own(im, b):
+        return T[im][:, base(b, rank):base(b, rank) + 640], "%s%d%d" % (im, b, rank)
+    for b in range(2):
+        spread("AOi", rank, b, "s")
+    for b in range(2):
+        spread("AOi", order[1], b, "s")
+    for b in range(2):
+        spread("AWi", rank, b, "s")
 
-    def walls_pe(e, eng):
-        through(e, nearH, T.W, "W", T["AW%d" % e], ["AW%do" % e, "AW%dn" % e], "WG", eng, (0, 1))
-
-    def walls_dma(e, H, halves):
-        aw = T["AW%d" % e]
-        for u in halves:
-            c0 = (e % 2) * 5120 + H * 2560 + u * 1280
-            dma("y", [(T.W[16 * q:16 * q + 16, c0:c0 + 1280],
-                       aw[(64 if q < 4 else 0) + 32 * u:(96 if q < 4 else 32) + 32 * u, H * 640:H * 640 + 640])
-                      for q in range(8)], ["AW%do" % e, "AW%dn" % e] if H == nearH else ["AW%df" % e],
-                ["W%d" % (c0 + 320 * k) for k in range(4)])
-    for e in range(2):
-        walls_dma(e, nearH, (1,))
-        walls_dma(e, 1 - nearH, (0, 1))
-    walls_pe(0, "ss")
-    walls_pe(1, "ss")
-    slots_in(0, "ss")
-    mk("lo", "i", 8.0, A.is_ge)
-    ma("w", "lo", -127.0, 128.0)
-    ma("wn", "lo", -1.0, 1.0)
-    mk("hbw", "wn", -BIG, A.mult)
-    mk("e80", "wn", 80.0, A.mult)
+    iota(T.xI[:], "xI", [[16, 10], [0, 8]], 0, 0, True)
+    bits([("s8", 0, 7), ("hl", 3, 1), ("gp", 4, 7), ("G", 4, 3), ("i", 0, 15), ("s4", 0, 3), ("b2", 2, 1), ("b1", 1, 1), ("b0", 0, 1)], 3)
+    ma("co", "G", 160.0, "i")
+    ma("w", "hl", -79.0, 80.0)
+    ma("tz", "gp", 16.0, 15.0)
     ma("sw", "sd", -128.0, 64.0)
-    ma("tz", "pg", 16.0, 15.0)
+    tsc(T.xl[:], T.xI[:], "co", A.add, None, None, ["xI"], ["xl"])
+    tsc(T.ol[:], T.xI[:, 0::8], "co", A.add, None, None, ["xI"], ["ol"])
+    mk("tq", "tz", "s8", A.subtract)
     mk("tzs", "tz", "sw", A.add)
-    ma("tl0", "pg", 16.0, "i8")
-    mk("tl1", "tl0", 8.0, A.add)
-    mk("tl0s", "tl0", "sw", A.add)
-    mk("tl1s", "tl1", "sw", A.add)
-    ma("a0", "i", 2.0, "g1")
-    ma("a1", "Gh", 32.0, "a0")
-    ma("tp", "sd", 64.0, "a1")
-    mk("tps", "tp", "sw", A.add)
-    ma("a2", "xq", 16.0, "xi")
-    ma("xst", "sd", 64.0, "a2")
-    mk("xot", "xst", "sw", A.add)
-    mk("tm", "i", 1024.0, A.mult)
-    mk("w1", "b2", "w", A.mult)
+
+    def mat(ap, key, t, wgt, width, row="ci"):
+        tsc(ap, T[row][:, 0:width], t, A.is_equal, wgt, A.mult, [row], [key])
+    mat(T.LQ[:], "LQ", "tq", "w", 136)
+    mat(T.Zs[:], "Zs", "tzs", "w", 144)
+    tsc(T.DL[:, 0:8], T.ci[:, 0:8], "s8", A.is_equal, None, None, ["ci"], ["DL"])
+
+    def own_slots(b):
+        win, k = own("OT", b)
+        cp(T["old%d" % b][:], win.indirect(T.ol[:]), [k, "ol"], ["old%d" % b], "s")
+
+    def own_walls(b):
+        win, k = own("W", b)
+        cp(T.x[:], win.indirect(T.xl[:]), [k, "xl"], ["x"], "s")
+        cp(T["XO%d" % b][:], win.indirect(T.ol[:]), [k, "ol"], ["XO%d" % b], "s", -BIG)
+
+    def lists(b, src, ks):
+        P = bank("PD1")
+        mms([(P[:, c:80:5], T.LQ[:, 8 - 8 * h:136 - 8 * h], src[:, 32 * c + 16 * h:32 * c + 16 * h + 16], h == 0, h == 1)
+             for c in range(5) for h in range(2)], ["LQ", ks], ["PD1"])
+        cp(T["LQn%d" % b][:], P[:, 0:80], ["PD1"], ["LQn%d" % b])
+        cp(T["LQs%d" % b][LO, :], P[HI, 0:80], ["PD1"], ["LQsa%d" % b])
+        cp(T["LQs%d" % b][HI, :], P[LO, 0:80], ["PD1"], ["LQsb%d" % b])
+    own_slots(0)
+    own_slots(1)
+    fill(T.W[:, 0:128], -BIG, "Wz")
+    fill(T.W[:, EC:WD], -BIG, "We")
+    lastw["We"] = lastw["We"] + lastw["Wz"]
+    fill(T.OT[:, 0:128], 128.0, "OTz")
+    fill(T.OT[:, EC:WD], 128.0, "OTe")
+    tsc(T.OT[:, EC:EC + 1], col["hl"], 8.0, A.mult, 128.0, A.add, [ckey["hl"]], ["OTe"])
+    lastw["OTe"] = lastw["OTe"] + lastw["OTz"]
+    for k in range(8):
+        ts(T.ZK[:, k, :], T.Zs[:], T.DL[:, k:k + 1], A.mult, None, None, ["Zs", "DL"], ["ZK%d" % k])
+    kZK = ["ZK%d" % k for k in range(8)]
+    lists(0, T.old0, "old0")
+    op("s", lambda e: e.activation(T.CB[:, 0:1], col["sd"], AF.Tanh, bias=-16.0, scale=32.0), [ckey["sd"]], ["CB"])
+    fill(T.c1[:], 1.0, "c1")
+    for k in range(4):
+        pick(T.RO[:, k, :], "RO%d" % k, T.c1[:, 0:128], "c1", [[64, 2], [0, 4], [1, 16]], 16 * k)
+    iota(T.bI[:], "bI", [[1, 256]])
+    iota(T.pr[:, 0:128], "pr", [[1, 8], [0, 16]])
+    ini = [(r, b) for r in order[2:] for b in range(2)]
+    for j, (r, b) in enumerate(ini[:6]):
+        spread("AOi", r, b, "s")
+    lists(1, T.old1, "old1")
+    mat(T.Z1[:], "Z1", "tz", 1.0, 144)
+    mat(T.ZV[:], "ZV", "tz", -PEN, 144)
+    mat(T.ZVs[:], "ZVs", "tzs", -PEN, 144)
+    for j, (r, b) in enumerate(ini[6:]):
+        spread("AOi", r, b, "vs"[j % 2])
+
+    def replies(t):
+        b = t % 2
+        cp(T.gO[:], T.OT[:].indirect(T["LQs%d" % b][:]), kOT + ["LQsa%d" % b, "LQsb%d" % b], ["gO"], "s")
+
+    def reply_lists(t):
+        prs = [(T.ZK[:, (a + t) % 8, 15 - a:143 - a], T.gO[:, 80 * a:80 * a + 80]) for a in range(16)]
+        P = bank("PD1")
+        mm(P[:, 0:80], prs, kZK + ["gO"], ["PD1"])
+        cp(T.L1[:], P[:, 0:80], ["PD1"], ["L1"])
+        cp(T.L2[LO, :], P[HI, 0:80], ["PD1"], ["L2a"])
+        cp(T.L2[HI, :], P[LO, 0:80], ["PD1"], ["L2b"])
+        ts(T.em[:], P[:, 0:80], EC + 4.0, A.is_gt, 100.0, A.mult, ["PD1"], ["em"])
+        mm(bank("PD0")[:, 0:80], prs, kZK + ["gO"], ["PD0"], True, False)
+    replies(0)
+    for b in range(2):
+        spread("AWi", order[1], b, "v")
+    ma("a0", "b0", -0.5, 1.0)
+    ma("a1", "b1", -0.75, 1.0)
+    ma("a2", "b2", -0.9375, 1.0)
+    mk("a3", "a0", "a1", A.mult, "a2", A.mult)
+    ma("w1", "b2", "w", 0.0)
+    ma("t4", "gp", 16.0, "s4")
+    tsc(T.fI[:], T.bI[:], "a3", A.mult, -0.5 + 2.0 ** -9, A.add, ["bI"], ["fI"])
     mk("w0", "w", "w1", A.subtract)
-    ma("t2", "b2", -4.0, "i8")
-    ma("t3", "pg", 16.0, "t2")
-    ma("a5", "sd", -0.5, 0.25)
-    mk("tb", "tm", "a5", A.add)
-    ma("a6", "b1", 3.0, 1.0)
-    ma("a7", "b2", 15.0, 1.0)
-    ma("a8", "b0", 1.0 / 128, 1.0 / 128)
-    mk("a9", "a8", "a6", A.mult)
-    mk("c1", "a9", "a7", A.mult)
-    ma("s8", "i8", -1.0, 8.0)
-    op("v", lambda e: e.memset(T.W[:, E:E + 8], -BIG), [], ["We"])
-    op("v", lambda e: e.memset(T.OT[:, E:E + 16], 0.0), [], ["OTz"])
-    cp(T.OT[:, E:E + 1], col["e80"], [ckey["e80"], "OTz"], ["OTe"])
-    ts(T.slU[:], T.slT[:], col["i"], A.add, None, None, ["slT", "CF"], ["slU"])
-    mat("XO", "M4", 2, 128, 128, c128, "ci", "xot", 1.0)
-    mat("XS", "M4", 3, 128, 128, c128, "ci", "xst", -1.0)
+    mk("tn", "t4", 12.0, A.add)
+    ts(T.fI[:], T.fI[:], 1, A.bitwise_and, None, None, ["fI"], ["fI"])
+    ma("gs", "sw", 1.0 / 16, "gp")
+    ma("tm", "i", 1024.0, 0.0)
+    cp(T.F[:], T.fI[:], ["fI"], ["F"])
+    reply_lists(0)
+    for j, (r, b) in enumerate(ini[:4]):
+        spread("AWi", r, b, "sv"[j % 2])
+    own_walls(0)
+    for j, (r, b) in enumerate(ini[4:]):
+        spread("AWi", r, b, "vs"[j % 2] if j > 1 else "v")
 
-    def own_walls(b, src, ksrc):
-        mm(T.P7[:, 0:160], [(lm("XO"), src)], ["MXO", ksrc], ["P7"])
-        mm(T.P7[:, 160:320], [(lm("XS"), src)], ["MXS", ksrc], ["P7"])
-        cp(T["XO%d" % b][:], T.P7[:, 0:160], ["P7"], ["XO%d" % b])
-        ts(T["xs%d" % b][:], T.P7[:, 160:320], col["tm"], A.add, None, None, ["P7", ckey["tm"]], ["xs%d" % b])
-        cp(T["x%d" % b][:], T["XO%d" % b][:].indirect(T.slU[:]), ["XO%d" % b, "slU"], ["x%d" % b], "s")
-    zk = (("ZKs", "tzs", "w"), ("ZK", "tz", "w"), ("Z1", "tz", 1.0), ("ZV", "tz", -262144.0), ("ZVs", "tzs", -262144.0))
-    for k, (n, t, m) in enumerate(zk):
-        mat(n, "MZ", k, 143, 144, T.ci[:], "ci", t, m)
-    ts(T.DL[:], T.ci[:, 0:16], col["i"], A.is_equal, None, None, ["ci", "CF"], ["DL"])
-    ts(T.mI[:], T.mI[:], 7, A.bitwise_and, None, None, ["mI"], ["mI"])
-    ts(T.MB[:], T.mI[:], col["i8"], A.is_equal, None, None, ["mI", "CF"], ["MB"])
-    ts(T.RS[:], T.RS[:], 0.5, A.is_gt, None, None, ["RS"], ["RS"])
-    ts(T.H2[:], T.RS[:], 2.0, A.mult, None, None, ["RS"], ["H2"])
+    def late_constants():
+        for k in range(2):
+            mat(T.LM[:, k, :], "LM%d" % k, "tn", "w%d" % k, 140)
+        mat(T.HA[:], "HA", "gs", HUGE, 128, "pr")
+        fill(T.H2[:], 2.0, "H2")
+        fill(T.RR[:], 0.0, "RR")
+        fill(T.rw4[:], 0.0, "rw4")
+        for k in range(8):
+            fill(T.CS[:, k::8], float(128 >> k), "CS%d" % k)
+        fill(T.H2[:, 0::8], 0.0, "H2")
+        fill(T.RR[:, 0::8], -1e9, "RR")
+        fill(T.rw4[:, 0::4], -HUGE, "rw4")
+        col["sg"], ckey["sg"] = T.CB[:, 0:1], "CB"
+        ma("de", "sg", 0.25, -0.25)
+        ma("a4", "G", 32.0, "s8")
+        ma("a5", "sd", 8.0, 16.0)
+        ma("wy", "hl", -159.0, 160.0)
+        ma("ci", "hl", 64.5, -64.5)
+        mk("ty", "a4", "a5", A.add)
+        mat(T.YM[:], "YM", "ty", "wy", 160)
+    kCS = ["CS%d" % k for k in range(8)]
+    fill(T.ta[:, 0:128], 1.0 / 64, "ta")
+    fill(T.tb[:, 0:128], -1.0 / 64, "tb")
+    fill(T.ta[:, 160:288], 1.0 / 128, "tc")
+    fill(T.c64[:], 0.5, "c64")
+    fill(T.r1[:], -1.0, "r1")
+    late_constants()
+    ps, po = [[32, 2], [64, 2], [1, 32]], [[32, 2], [-64, 2], [1, 32]]
+    pick(T.Ms[:], "Ms", T.ta[:, 0:128], "ta", ps, 0)
+    pick(T.Mo[:], "Mo", T.tb[:, 0:128], "tb", po, 64)
+    pick(T.Mh[:], "Mh", T.ta[:, 160:288], "tc", ps, 0)
+    op("g", lambda e: e.affine_select(T.Mh[:], T.Mh[:], po, A.not_equal, -1.0 / 128, 64, -1), ["Mh"], ["Mh"])
+    py = [[16, 5], [-1000, 2], [1, 16]]
+    pick(T.OA[:], "OA", T.c1[:], "c1", py, 1000)
+    pick(T.OB[:], "OB", T.r1[:], "r1", py, 1064)
+    pick(T.OH[:], "OH", T.c64[:], "c64", py, 1000, (1064, -0.5))
 
-    def empties(eq, keq):
-        for k in range(16):
-            op("s", lambda e: e.activation(T.EX[:, :, k], eq, AF.Identity, scale=T.DL[:, k:k + 1]), [keq, "DL"], ["EX%d" % k])
-        mm(T.P5[:, 0:80], [(lz("Z1", a), T.EX[:, 5 * a:5 * a + 5, :]) for a in range(16)],
-           ["MZ1"] + ["EX%d" % k for k in range(16)], ["P5"])
-    for dst, sc in (("f1", 1.0), ("f2", 0.5)):
-        ts(T[dst][:], T.bI[:], col["c1"], A.mult, sc, A.mult, ["bI", ckey["c1"]], [dst])
-        ts(T[dst][:], T[dst][:], -0.5 + 2.0 ** -9, A.add, None, None, [dst], [dst])
-        ts(T[dst][:], T[dst][:], MG, A.add, MG, A.subtract, [dst], [dst])
-    ts(T.f2[:], T.f2[:], -2.0, A.mult, None, None, ["f2"], ["f2"])
-    tt(T.f1[:], T.f1[:], T.f2[:], A.add, ["f1", "f2"], ["f1"])
-    ts(T.F9[:], T.ci[:, 0:9], col["s8"], A.is_equal, None, None, ["ci", ckey["s8"]], ["F9"])
-    for k in range(9):
-        ts(T.F[:, k::9], T.f1[:], T.F9[:, k:k + 1], A.max, None, None, ["f1", "F9"], ["F%d" % k])
-    kF = ["F%d" % k for k in range(9)]
-    for k, (n, t) in enumerate((("LQ0", "tl0"), ("LQ1", "tl1"), ("LQ0s", "tl0s"), ("LQ1s", "tl1s"))):
-        mat(n, "M8", 8 + k, 128, 128, c128, "ci", t, "w")
-    for h in range(2):
-        for n in range(2):
-            mk("tn%d%d" % (h, n), "t3", 8.0 * h + 4.0 * n, A.add)
-            for k in range(2):
-                mat("LN%d%d%d" % (h, n, k), "M8", 13 + 4 * h + 2 * n + k, 128, 128, c128, "ci", "tn%d%d" % (h, n), "w%d" % k)
-    mat("HA", "M8", 12, 128, 128, T.pr[:], "pr", "pg", "hbw")
-    mat("P1", "M4", 4, 128, 128, c128, "ci", "tp", 1.0)
-    mat("P2", "M4", 5, 128, 128, c128, "ci", "tp", 0.5)
-    mat("P3", "M4", 6, 128, 128, c128, "ci", "tps", -0.5)
-    tt(lm("P2"), lm("P2"), lm("P3"), A.add, ["MP2", "MP3"], ["MP2"])
-
-    kW = ["We"] + ["W%d" % (320 * k) for k in range(32)]
-    kOT = ["OTe"] + ["OT%d" % (320 * k) for k in range(32)]
-    W, OT = T.W[:, 0:E + 8], T.OT[:, 0:E + 16]
-
-    def invert(b):
-        f, i, v = T.nf[:, 0:80], T.ti[:, 0:80], T.hI[:, 0:80]
-        acc, y = T.C[:, 0:80], T.yi[:, 0:80]
-        a = [(cp, (i, T.QF[:], ["QF"], ["ti"])), (ts, (acc, T.QF[:], 10240.0, A.is_ge, 10080.0, A.mult, ["QF"], ["C"])),
-             (ts, (v, i, 5, A.logical_shift_right, None, None, ["ti"], ["hI"])),
-             (ts, (f, v, 0.2, A.mult, -0.4, A.add, ["hI"], ["nf"])), (cp, (y, f, ["nf"], ["yi"]))]
-        a += terms(acc, [(5, T.QF[:], "QF", 0), (80, i, "ti", 4), (-319, i, "ti", 5), (1275, y, "yi", 0)] +
-                   [(k, y, "yi", sh) for sh, k in ((2, -4800), (4, 3840), (5, -10160))], 80)
-        return a + [(cp, (T.YO[:, b * 80 + c:b * 80 + 80:5], T.C[:, c * 16:c * 16 + 16], ["C"], ["YO%d" % b])) for c in range(5)]
-
-    def put_slots(b):
-        dma("y", [(T.yo[16 * gg + 8 * sd:16 * gg + 8 * sd + 8, b * 80:b * 80 + 80],
-                   T.YO[64 * sd + 8 * gg:64 * sd + 8 * gg + 8, b * 80:b * 80 + 80]) for sd in range(2) for gg in range(8)],
-            ["YO%d" % b], [])
-
-    def turn_walls(b, src, ks):
-        for c in range(5):
-            ts(T.Y[:, b, :, c::5], src[:, c * 32:c * 32 + 32], col["sgn"], A.mult, None, None, [ks, ckey["sgn"]], ["Y%d" % b])
-
-    def put_walls(b, qs):
-        for sd, o in ((0, T.yl), (1, T.yr)):
-            dma(qs[sd], [(o[16 * (2 * G + h):16 * (2 * G + h) + 16, b * 80:b * 80 + 80], T.Y[wr(sd, G), b, h, :])
-                         for G in range(4) for h in range(2)], ["Y%d" % b], [])
+    def lz(name, a):
+        return T[name][:, 15 - a:143 - a]
 
     def rnd(t):
         b = t % 2
-        e = t + 2
-        lqn = (T.LQn[:, b * 80:b * 80 + 80], T.LQs[:, b * 80:b * 80 + 80]) if t < 2 else (T.LMn[:], T.LMs[:])
-        kl = ("LQn", "LQs") if t < 2 else ("LMn", "LMs")
-        x, kx = T["x%d" % b][:], "x%d" % b
-        empties(T.eQ[:, 80 * b:80 * b + 80], "eQ%d" % b)
-        op("s", lambda q: q.activation(T.u[:], W.indirect(lqn[0]), AF.Identity), kW + [kl[0]], ["u"])
-        op("v", lambda q: q.tensor_tensor(T.gO[:], OT.indirect(lqn[1]), T.MB[:, 16 * t:16 * t + 1280], A.mult), kOT + [kl[1], "MB"], ["gO"])
-        mm(T.P0[:, 0:80], [(lz("ZKs", a), T.gO[:, 80 * a:80 * a + 80]) for a in range(16)], ["MZKs", "gO"], ["P0"])
-        mm(T.P1[:, 0:80], [(lz("ZK", a), T.gO[:, 80 * a:80 * a + 80]) for a in range(16)], ["MZK", "gO"], ["P1"])
-
-        ms = [1 + (t + 3 * q) % 7 for q in range(2)]
-
-        def diffs(q):
-            m, d = ms[q], T["d%d" % q]
-            hb = m.bit_length() - 1
-            need("v", ["u"], ["d%d" % q])
-            for k in range(1 << hb):
-                out = d[:] if hb == 0 else d[:, :, :, k] if hb == 1 else d[:, :, k >> 1, k & 1]
-                tt(out, T.u[:, (k ^ m)::2 << hb], T.u[:, k::2 << hb], A.subtract, ["u"], ["d%d_%d" % (q, k)])
-            done(("qv", tot["qv"], "v"), [], ["d%d" % q])
-
-        def parts(q):
-            m, d, vv = ms[q], T["d%d" % q], T["V%d" % q]
+        W, OT = T.W[:], T.OT[:]
+        P2, P3, P4 = bank("PA0")[:, 0:80], bank("PA1")[:, 0:80], bank("PD0")[:, 0:80]
+        cp(T.u[:], W.indirect(T["LQn%d" % b][:]), kW + ["LQn%d" % b], ["u"], "s")
+        tt(T.cm1[:], W.indirect(T.L1[:]), T.x[:], A.is_gt, kW + ["L1", "x"], ["cm1"])
+        mm(P4, [(lz("ZV", a), T.cm1[:, a::16]) for a in range(16)], ["ZV", "cm1"], ["PD0"], False, False)
+        for q in range(2):
+            m, d, vv = 1 + (t + 3 * q) % 7, T["d%d" % q], T["V%d" % q]
             hb = m.bit_length() - 1
             f = m ^ (1 << hb)
-            need("s", ["d%d" % q], ["V%d" % q])
-
-            def act(o, i, s):
-                op("s", lambda qq: qq.activation(o, i, AF.Relu, scale=s), ["d%d" % q], [])
+            kd = ["d%d_%d" % (q, k) for k in range(1 << hb)]
+            for k in range(1 << hb):
+                out = d[:] if hb == 0 else d[:, :, :, k] if hb == 1 else d[:, :, k >> 1, k & 1]
+                tt(out, T.u[:, (k ^ m)::2 << hb], T.u[:, k::2 << hb], A.subtract, ["u"], [kd[k]] + (["d%d" % q] if k == 0 else []))
             if hb == 0:
-                act(vv[:, :, :, :, 0], d[:], -1.0)
-                act(vv[:, :, :, :, 1], d[:], 1.0)
+                up, dn = vv[:, :, :, :, 0], [(vv[:, :, :, :, 1], d[:])]
             elif hb == 1:
-                act(vv[:, :, :, 0, :], d[:], -1.0)
-                if f == 0:
-                    act(vv[:, :, :, 1, :], d[:], 1.0)
-                else:
-                    for k in range(2):
-                        act(vv[:, :, :, 1, 1 - k], d[:, :, :, k], 1.0)
+                up = vv[:, :, :, 0, :]
+                dn = [(vv[:, :, :, 1, :], d[:])] if f == 0 else [(vv[:, :, :, 1, 1 - k], d[:, :, :, k]) for k in range(2)]
             else:
-                act(vv[:, :, 0, :, :], d[:], -1.0)
-                if f == 0:
-                    act(vv[:, :, 1, :, :], d[:], 1.0)
-                for k in range(2 if f else 0):
-                    if f == 1:
-                        act(vv[:, :, 1, :, 1 - k], d[:, :, :, k], 1.0)
-                    else:
-                        act(vv[:, :, 1, 1 - k, :], d[:, :, k, :], 1.0)
-            done(("qs", tot["qs"], "s"), [], ["V%d" % q])
-
-        def sums(q):
-            mm(T["P%d" % (2 + q)][:, 0:80], [(lz("Z1", a), T["V%d" % q][:, 10 * a:10 * a + 10, :, :, :]) for a in range(16)],
-               ["MZ1", "V%d" % q], ["P%d" % (2 + q)])
-
-        def gone():
-            for q in range(2):
-                ts(T["g%d" % q][:], T["P%d" % (2 + q)][:, 0:80], 0.5, A.is_lt, None, None, ["P%d" % (2 + q)], ["g%d" % q])
-            for q in range(2):
-                gt, gk, m = T["g%d" % q], "g%d" % q, ms[q]
-                st = 2 << (m.bit_length() - 1)
-                need("v", [gk], [])
-                for k in range(st // 2):
-                    op("v", lambda qq: qq.tensor_tensor(gt[:, k::st], gt[:, k::st], gt[:, (k ^ m)::st], A.is_gt))
-                done(("qv", tot["qv"], "v"), [], [gk])
-        cp(T.L1[:], T.P0[:, 0:80], ["P0"], ["L1"])
-        cp(T.L2[:], T.P1[:, 0:80], ["P1"], ["L2"])
-        op("v", lambda q: q.tensor_tensor(T.cm1[:], W.indirect(T.L1[:]), x, A.is_gt), kW + ["L1", kx], ["cm1"])
-        mm(T.P4[:, 0:80], [(lz("ZV", a), T.cm1[:, a::16]) for a in range(16)], ["MZV", "cm1"], ["P4"], True, False)
-        for q in range(2):
-            diffs(q)
-            parts(q)
-            sums(q)
-        op("v", lambda q: q.tensor_tensor(T.cm2[:], W.indirect(T.L2[:]), x, A.is_lt), kW + ["L2", kx], ["cm2"])
-        mm(T.P4[:, 0:80], [(lz("ZVs", a), T.cm2[:, a::16]) for a in range(16)], ["MZVs", "cm2"], ["P4"], False, True)
-        tt(T.kb[:], T.KC[:], T.P0[:, 0:80], A.subtract, ["KC", "P0"], ["kb"])
-        gone()
-        tt(T.gs[:], T.g0[:], T.g1[:], A.max, ["g0", "g1"], ["gs"])
-        ts(T.gm[:], T.gs[:], -262144.0, A.mult, None, None, ["gs"], ["gm"])
-        tt(T.gb[:], T.P5[:, 0:80], T.gs[:], A.max, ["gs", "P5"], ["gb"])
-        tt(T.kb2[:], T.kb[:], T.gm[:], A.add, ["kb", "gm"], ["kb2"])
-        op("v", lambda q: q.tensor_tensor_scan(T.sc[:], T.H2[:], T.gb[:], 0.0, A.mult, A.add), ["H2", "gb"], ["sc"])
-        tt(T.da[:], T.P4[:, 0:80], T.kb2[:], A.add, ["P4", "kb2"], ["da"])
-        ts(T.fb[:], T.sc[:, 7::8], 9.0, A.mult, None, None, ["sc"], ["fb"])
-        op("v", lambda q: q.tensor_tensor_scan(T.RM[:], T.RS[:], T.da[:], 0.0, A.mult, A.max), ["RS", "da"], ["RM"])
-        cp(T.Mi[:], T.RM[:, 7::8], ["RM"], ["Mi"])
-        ts(T.cd[:], T.Mi[:], 14, A.logical_shift_right, None, None, ["Mi"], ["cd"])
-        ts(T.cv[:], T.Mi[:], 16383, A.bitwise_and, None, None, ["Mi"], ["cv"])
-        tt(T.cx[:], T.cd[:], T.fb[:], A.add, ["cd", "fb"], ["cx"])
-        ts(T.cu[:], T.cv[:], -1.0, A.mult, 10240.0, A.add, ["cv"], ["cu"])
+                up = vv[:, :, 0, :, :]
+                dn = [(vv[:, :, 1, :, :], d[:])] if f == 0 else \
+                    [(vv[:, :, 1, :, 1 - k], d[:, :, :, k]) if f == 1 else (vv[:, :, 1, 1 - k, :], d[:, :, k, :]) for k in range(2)]
+            kv = ["V%d_%d" % (q, k) for k in range(1 + len(dn))]
+            op("s", lambda e: e.activation(up, d[:], AF.Tanh, bias=-8.0, scale=-16.0), kd + ["d%d" % q], [kv[0], "V%d" % q])
+            for k, (o, i) in enumerate(dn):
+                op("s", lambda e: e.activation(o, i, AF.Tanh, bias=-TB, scale=16.0), kd + ["d%d" % q], [kv[1 + k]])
+            mm((P2, P3)[q], [(lz("Z1", a), vv[:, 10 * a:10 * a + 10, :, :, :]) for a in range(16)], ["Z1", "V%d" % q] + kv, ["PA%d" % q])
+        tt(T.cm2[:], W.indirect(T.L2[:]), T.x[:], A.is_lt, kW + ["L2a", "L2b", "x"], ["cm2"])
+        mm(P4, [(lz("ZVs", a), T.cm2[:, a::16]) for a in range(16)], ["ZVs", "cm2"], ["PD0"], False, True)
+        tt(T.a1[:], P2, T.em[:], A.subtract, ["PA0", "em"], ["a1"])
+        ts(T.th[:], T.a1[:], THR, A.is_lt, 100.0, A.mult, ["a1"], ["th"])
+        tt(T.y[:], P3, T.th[:], A.subtract, ["PA1", "th"], ["y"])
+        ts(T.gm[:], T.y[:], THR, A.is_lt, -PEN, A.mult, ["y"], ["gm"])
+        ts(T.gb[:], T.y[:], THR, A.is_lt, None, None, ["y"], ["gb"])
+        tt(T.gr[:], T.RR[:], T.gm[:], A.subtract, ["RR", "gm"], ["gr"])
+        tt(T.gk[:], T.gm[:], T.CS[:], A.add, ["gm"] + kCS, ["gk"])
+        tt(T.da[:], P4, T.gm[:], A.add, ["PD0", "gm"], ["da"])
+        tt(T.e0[:], P4, T.gr[:], A.is_lt, ["PD0", "gr"], ["e0"])
+        tt(T.e1[:], P4, T.gk[:], A.min, ["PD0", "gk"], ["e1"])
+        scan(T.sc[:], T.H2[:], T.gb[:], A.mult, A.add, ["H2", "gb"], ["sc"])
+        scan(T.S1[:], T.e0[:], T.da[:], A.mult, A.max, ["e0", "da"], ["S1"])
+        scan(T.S2[:], T.e0[:], T.e1[:], A.mult, A.max, ["e0", "e1"], ["S2"])
+        cp(T.cu[:], T.S1[:, 7::8], ["S1"], ["cu"])
+        tt(T.cx[:], T.S2[:, 7::8], T.sc[:, 7::8], A.add, ["S2", "sc"], ["cx"])
+        old, ko = (T["old%d" % t][:], "old%d" % t) if t < 2 else (T.AO0[:, rank], "AO0%d" % rank)
+        tt(T.dT[:], OT.indirect(T.cu[:]), old, A.subtract, kOT + ["cu", ko], ["dT"])
         cp(T.iu[:], T.cx[:], ["cx"], ["iu"])
-        op("s", lambda q: q.activation(T.FT[:], T.F[:].indirect(T.iu[:]), AF.Identity), kF + ["iu"], ["FT"])
-        old, ko = T["AO%d" % t][:, own:own + 160], "AO%do" % t
-        op("v", lambda q: q.tensor_tensor(T.dT[:], OT.indirect(T.cu[:]), old, A.subtract), kOT + ["cu", ko], ["dT"])
-        tt(T.mT[:], T.dT[:], T.FT[:], A.mult, ["dT", "FT"], ["mT"])
-        tt(T.TN[:], T.mT[:], old, A.add, ["mT", ko], ["TN"])
-        for k in range(2):
-            mm(T.P5[:, 40 * k:40 * k + 40], [(lm("LN%d%d%d" % (h, n, k)), T.TN[:, :, h, n::2]) for h in range(2) for n in range(2)],
-               ["MLN%d%d%d" % (h, n, k) for h in range(2) for n in range(2)] + ["TN"], ["P5"])
-        cp(T.LN[:], T.P5[:, 0:80], ["P5"], ["LN"])
+        tt(T.mT[:], T.F[:].indirect(T.iu[:]), T.dT[:], A.mult, ["F", "iu", "dT"], ["mT"])
+        tn, kt = (T["AO%d" % t][:, rank], "AO%d%d" % (t, rank)) if t < 2 else (T.TN[:], "TN")
+        tt(tn, T.mT[:], old, A.add, ["mT", ko], [kt])
+        PL, PH = bank("PB0"), bank("PB1")[:, 0:160]
+        mms([(PL[:, 40 * k:40 * k + 40], T.LM[:, k, 12 - 4 * j:140 - 4 * j], tn[:, j::4], j == 0, j == 3) for k in range(2) for j in range(4)],
+            ["LM0", "LM1", kt], ["PB0"])
         if t < 2:
-            cp(T["AO%d" % e][:, own:own + 160], T.TN[:], ["TN"], ["AO%do" % e], "s")
-            send("o", e)
-        mm(T.P4[:, 160:240], [(lm("LQ0"), T.TN[:, :, 0, :]), (lm("LQ1"), T.TN[:, :, 1, :])], ["MLQ0", "MLQ1", "TN"], ["P4"])
+            send("AO%d" % t)
+        ts(T.nd[:], tn, 127.5, A.is_lt, None, None, [kt], ["nd"])
+        cp(T.LN[:], PL[:, 0:80], ["PB0"], ["LN"])
+        mm(PH, [(T.HA[:], T.nd[:])], ["HA", "nd"], ["PB1"])
         for k in range(2):
             cp(T.w[:, 320 * k:320 * k + 320], W.indirect(T.LN[:, 20 * k:20 * k + 20]), kW + ["LN"], ["w%d" % k], "s")
-        inv = []
-        if t > 0:
-            cp(T.QF[:], T.P4[:, 160:240], ["P4"], ["QF"])
-            inv = invert(b) if t == 2 else []
-        ts(T.nd[:], T.TN[:], 79.5, A.is_lt, None, None, ["TN"], ["nd"])
-        run(inv[0:5])
-        mm(T.P6[:, 0:160], [(lm("HA"), T.nd[:])], ["MHA", "nd"], ["P6"])
+        tt(T.y1[:], PH, T["XO%d" % b][:], A.add, ["PB1", "XO%d" % b], ["y1"])
+        tsc(T.q2[:], T.y1[:], "tm", A.min, "de", A.add, ["y1"], ["q2"])
         for k in range(2):
             o = 320 * k
-            op("v", lambda q: q.tensor_tensor(T.t1[:, o:o + 320], W.indirect(T.LN[:, 40 + 20 * k:60 + 20 * k]), T.w[:, o:o + 320], A.max),
-               kW + ["LN", "w%d" % k], ["t1%d" % k])
-        tt(T.xx[:], T.P6[:, 0:160], T["xs%d" % b][:], A.add, ["P6", "xs%d" % b], ["xx"])
-        tt(T.t2[:], T.t1[:, 0::2], T.t1[:, 1::2], A.max, ["t10", "t11"], ["t2"])
-        for h in range(2):
-            for n in range(2):
-                tt(T.m4[:, :, h, n::2], T.t2[:, :, :, h, n, 0], T.t2[:, :, :, h, n, 1], A.max, ["t2"], ["m4%d%d" % (h, n)])
-        tt(T.mm[:], T.m4[:], T.xx[:], A.max, ["m400", "m401", "m410", "m411", "xx"], ["mm"])
-        ts(T.nn[:], T.mm[:], -1.0, A.mult, col["tb"], A.add, ["mm", ckey["tb"]], ["nn"])
-        mm(T.P6[:, 0:160], [(lm("P1"), T.nn[:])], ["MP1", "nn"], ["P6"])
-        mm(T.P7[:, 0:160], [(lm("P2"), T.nn[:])], ["MP2", "nn"], ["P7"])
-        run(inv[5:13])
-        cp(T.pp[:], T.P6[:, 0:160], ["P6"], ["pp"], "s")
-        tt(T.qq[:], T.P7[:, 0:160], T.pp[:], A.min, ["P7", "pp"], ["qq"])
-        dst, kd = (T["AW%d" % e][:, own:own + 160], "AW%do" % e) if t < 2 else (T.RF[:], "RF")
-        ts(dst, T.qq[:], MG, A.add, MG, A.subtract, ["qq"], [kd])
-        if t < 2:
-            send("w", e)
-        return dst, kd, inv[13:]
+            tt(T.t1[:, o:o + 320], W.indirect(T.LN[:, 40 + 20 * k:60 + 20 * k]), T.w[:, o:o + 320], A.max, kW + ["LN", "w%d" % k], ["t1%d" % k])
+            if k == 0:
+                tsc(T.q1[:], T.y1[:], "tm", A.min, None, None, ["y1"], ["q1"])
+        scan(T.sw[:], T.rw4[:], T.t1[:], A.add, A.max, ["rw4", "t10", "t11"], ["sw"])
+        return tn, kt
 
-    own_walls(0, T.AW0[:, own:own + 160], "AW0o")
-    slots_in(1, "sv")
-    dst, kd, inv = rnd(0)
-    own_walls(1, T.AW1[:, own:own + 160], "AW1o")
-    mm(T.P4[:, 240:320], [(lm("LQ0s"), T.TN[:, :, 0, :]), (lm("LQ1s"), T.TN[:, :, 1, :])], ["MLQ0s", "MLQ1s", "TN"], ["P4"])
-    for c in range(5):
-        cp(T.LMn[:, c::5], T.P4[:, 160 + c * 16:176 + c * 16], ["P4"], ["LMn"])
-        cp(T.LMs[:, c::5], T.P4[:, 240 + c * 16:256 + c * 16], ["P4"], ["LMs"])
-    ts(T.eQ[:, 0:80], T.LMn[:], 10240.0, A.is_ge, None, None, ["LMn"], ["eQ0"])
-    own_walls(0, dst, kd)
-    for H in (nearH, 1 - nearH):
-        walls_dma(2, H, (0, 1))
-    slots_in(2, "sv")
-    dst, kd, inv = rnd(1)
-    turn_walls(1, dst, kd)
-    run(invert(1))
-    for H in (nearH, 1 - nearH):
-        walls_dma(3, H, (0, 1))
-    slots_in(3, "sv")
-    put_walls(1, "yy")
-    put_slots(1)
-    dst, kd, inv = rnd(2)
-    turn_walls(0, dst, kd)
-    put_walls(0, "ys")
-    run(inv)
-    put_slots(0)
+    def tile(t):
+        P1, P2 = bank("PC0")[:, 0:160], bank("PC1")[:, 0:160]
+        mm(P2, [(T.Mh[:], T.q2[:])], ["Mh", "q2"], ["PC1"], True, False)
+        mm(P1, [(T.Ms[:], T.q1[:])], ["Ms", "q1"], ["PC0"], True, False)
+        mm(P2, [(T.Mh[:], T.sw[:, 3::4])], ["Mh", "sw"], ["PC1"], False, True)
+        mm(P1, [(T.Mo[:], T.sw[:, 3::4])], ["Mo", "sw"], ["PC0"], False, True)
+        ts(T.r1[:], P2, MG / 64, A.add, MG / 64, A.subtract, ["PC1"], ["r1"])
+        tt(T.FF[:], P1, T.r1[:], A.min, ["PC0", "r1"], ["FF"])
+        Z, kz = T["AW%d" % t], "AW%d%d" % (t, rank)
+        cp(Z[LO, rank, 0, :], T.FF[LO, :], ["FF"], ["z0"])
+        cp(Z[HI, rank, 1, :], T.FF[HI, :], ["FF"], ["z1"])
+        tt(Z[HI, rank, 0, :], T.FF[LO, :], Z[LO, rank, 0, :], A.subtract, ["FF", "z0"], ["z2"])
+        tt(Z[LO, rank, 1, :], T.FF[HI, :], Z[HI, rank, 1, :], A.subtract, ["FF", "z1"], [kz])
+        send("AW%d" % t)
+
+    def put_slots(b, tn, kt):
+        P = bank("PD0")[:, 0:80]
+        tsc(T.ind[:], tn, 63.5, A.is_gt, "ci", A.mult, [kt], ["ind"])
+        mm(P, [(T.YM[:, 16 - 16 * k:144 - 16 * k], s[:, 80 * k:80 * k + 80]) for k in range(2) for s in (tn, T.ind)], ["YM", kt, "ind"], ["PD0"])
+        cp(T.Yo[:, 80 * b:80 * b + 80], P, ["PD0"], ["Yo%d" % b], "s", -48.0)
+        dma([("y", T.yo[:, 80 * b:80 * b + 80], T.Yo[:, 80 * b:80 * b + 80])], ["Yo%d" % b], [])
+
+    def put_walls(b):
+        jobs = (("PA0", "OH", "q2", "OH"), ("PA1", "OA", "q1", "OB"), ("PD1", "OB", "q1", "OA"))
+        for z in range(2):
+            for pk, mq, q, ms in jobs:
+                mm(bank(pk)[:, 0:80], [(T[(mq, ms)[z]][:, 16 - 16 * k:144 - 16 * k],
+                                        T.sw[:, 3 + 320 * k:320 * k + 320:4] if z else T[q][:, 80 * k:80 * k + 80]) for k in range(2)],
+                   [mq, ms, "sw" if z else q], [pk], z == 0, z == 1)
+        ts(T.mid[:], bank("PA0")[:, 0:80], MG, A.add, MG, A.subtract, ["PA0"], ["mid"])
+        for q, pk, y, o, f in (("y", "PA1", "Yr", T.yr, A.min), ("s", "PD1", "Yl", T.yl, A.max)):
+            tt(T[y][:, 80 * b:80 * b + 80], bank(pk)[:, 0:80], T.mid[:], f, [pk, "mid"], [y + str(b)])
+            dma([(q if b == 0 else "y", o[:, 80 * b:80 * b + 80], T[y][:, 80 * b:80 * b + 80])], [y + str(b)], [])
+
+    for t in range(2):
+        tn, kt = rnd(t)
+        own_walls(1 - t)
+        tile(t)
+        if t == 0:
+            lists(0, tn, kt)
+        else:
+            put_slots(1, tn, kt)
+            put_walls(1)
+        for j, r in enumerate(order):
+            spread("AO%d" % t, r, t, "ssvsvsvv"[j])
+        replies(t + 1)
+        for j, r in enumerate(order[:2]):
+            spread("AW%d" % t, r, t, "v")
+        reply_lists(t + 1)
+        for j, r in enumerate(order[2:]):
+            spread("AW%d" % t, r, t, "svsvsv"[j])
+    tn, kt = rnd(2)
+    put_slots(0, tn, kt)
+    put_walls(0)
     for s in tot:
         if waited["g"].get(s, 0) < tot[s]:
             g.wait_ge(T.sem[s], tot[s])

@@ -18,9 +18,9 @@ SCRATCH = {
     "ZK": ("sbuf", [128, 8, 144], FB), "RW": ("sbuf", [128, 2, 128], FB), "RI": ("sbuf", [128, 4, 128], FB),
     "RO": ("sbuf", [128, 4, 128], FB), "LM": ("sbuf", [128, 2, 140], FB),
 }
-for _n, _w, _t in (("u x", 1280, FI), ("gO cm1 cm2", 1280, FB), ("w t1 sw", 640, FI), ("rw4", 640, FB),
+for _n, _w, _t in (("u x", 1280, FI), ("gO cm1 cm2", 1280, FB), ("w t1 sw", 640, FI), ("rw4 zz", 640, FB),
                    ("O32 X32 qi yi hI lI", 320, II), ("ta tb", 320, FI), ("bI", 256, FI), ("fI", 256, II), ("F", 256, FB),
-                   ("ci pr OA OB OH c64 c1 XO0 XO1 y1 q1 q2 r1 FF Yl Yr Yo", 160, FI), ("old0 old1 dT mT nd ind YM", 160, FB),
+                   ("ci OA OB OH XO0 XO1 y1 q1 q2 r1 Yl Yr Yo", 160, FI), ("old0 old1 dT mT nd ind YM", 160, FB),
                    ("Zs Z1 ZV ZVs", 144, FB), ("LQ", 136, FB), ("kI HA", 128, FB), ("Ms Mo Mh", 128, FI),
                    ("LQn0 LQn1 LQs0 LQs1 L1 L2 LN xl", 80, UU), ("xI", 80, II),
                    ("em a1 th y gm gb gk gr sc da e0 e1 S1 S2 H2 CS RR mid", 80, FI), ("cx DL", 10, FI), ("cu iu ol", 10, UU)):
@@ -29,6 +29,7 @@ for _n, _w, _t in (("u x", 1280, FI), ("gO cm1 cm2", 1280, FB), ("w t1 sw", 640,
 for _k in "ABCD":
     SCRATCH["P" + _k] = ("psum", [128, 2, 512], FI)
 TILES = ("AOi", "AWi", "AO0", "AW0", "AO1", "AW1")
+HANDED = ()
 SEMAPHORES = ["qv", "qt", "qs", "qg", "ls"] + ["%s%d" % (a, r) for a in TILES for r in range(N)] + ["dm%d" % k for k in range(12)]
 
 
@@ -121,46 +122,58 @@ def rank_program(g, core, T, topo):
         else:
             op("g", lambda e: e.iota(ap, pat, base, ch, allow_small_or_imprecise_dtypes=True), [], [key])
 
-    def pick(ap, key, src, ksrc, pat, base, more=None):
-        op("g", lambda e: e.affine_select(ap, src, pat, A.is_equal, 0.0, base, -1), [ksrc], [key])
-        if more:
-            op("g", lambda e: e.affine_select(ap, ap, pat, A.not_equal, more[1], more[0], -1), [key], [key])
+    def pick(ap, key, *terms):
+        src, ks = T.zz[:, 0:ap.shape[1]], "zz"
+        for pat, b0, val in terms:
+            op("g", lambda e: e.affine_select(ap, src, pat, A.not_equal, val, b0, -1), [ks], [key])
+            src, ks = ap, key
 
     def bank(k):
         return T["P" + k[1]][:, int(k[2]), :]
     LO, HI = slice(0, 64), slice(64, 128)
 
-    def kind(c):
-        same = topo.die(c) == topo.die(core)
-        if c in topo.cores_of(core):
-            return 0
-        if topo.mates(core, c):
-            return 1 if same else 3
-        if topo.same_plane(core, c):
-            return 2 if same else 4
-        return 5 if same else 6
-    others = sorted([c for c in T.cores if c != core], key=kind)
-    order = [rank] + [T.rank_of(c) for c in others]
-    offe = topo.engines(core, others[-1])
-    one = [e for e in topo.engines(core, others[0]) if e not in offe]
+    def way(c):
+        return 0 if c in topo.cores_of(core) else 1 if topo.mates(core, c) else 2 if topo.same_plane(core, c) else 3
+    others = sorted([c for c in T.cores if c != core], key=way)
+    partner = others[0]
+    same = [c for c in others[1:] if topo.die(c) == topo.die(core)]
+    cross = [c for c in others[1:] if c not in same]
+    offe = topo.engines(core, same[0])
+    one = [e for e in topo.engines(core, partner) if e not in offe]
+    hand = (((0, one[:len(one) // 2]), (1, one[len(one) // 2:])), ((2, one),))
 
-    def send(name):
-        src = T[name][:, rank]
-        need("g", ["%s%d" % (name, rank)], [])
+    def order(name):
+        far = same + cross if name in HANDED else [same[0], same[1], cross[0], cross[1], same[2], cross[2]]
+        return [T.rank_of(c) for c in [core, partner] + far]
+
+    def write(parts):
         trs = []
-        for dst, es in ((others[:1], one), (others[1:], offe)):
+        for name, r, dst, es in parts:
+            need("g", ["%s%d" % (name, r)], [])
             ids = []
             for c in dst:
                 rid, pid = topo.addr(c, core)
                 ids.append(DstId(rid=rid, pnc=pid))
-            trs.append(RemoteDMATransfer(dst_ids=ids, dma_engine_mask=sum(1 << e for e in es), remote_sem=T.sem["%s%d" % (name, rank)],
-                                         srcs=[src], dsts=[src for _ in dst], alu_op=0))
+            trs.append(RemoteDMATransfer(dst_ids=ids, dma_engine_mask=sum(1 << e for e in es), remote_sem=T.sem["%s%d" % (name, r)],
+                                         srcs=[T[name][:, r]], dsts=[T[name][:, r] for _ in dst], alu_op=0))
+            tot["ls"] = tot.get("ls", 0) + len(es)
         g.remote_dma_fused(trs, local_sem=T.sem.ls)
-        tot["ls"] = tot.get("ls", 0) + len(one) + len(offe)
-        for j, r in enumerate(order[1:]):
-            k = "%s%d" % (name, r)
-            tot[k] = len(offe) if j else len(one)
-            lastw[k] = [(k, tot[k], "x")]
+
+    def send(name):
+        far = same if name in HANDED else [T.cores[r] for r in order(name)[2:]]
+        write([(name, rank, [partner], one), (name, rank, far, offe)])
+        cnt = [(partner, len(one))] + [(c, len(offe)) for c in far]
+        if name in HANDED:
+            cnt += [(cross[k], len(es)) for call in hand for k, es in call]
+        for c, n in cnt:
+            k = "%s%d" % (name, T.rank_of(c))
+            tot[k] = n
+            lastw[k] = [(k, n, "x")]
+
+    def hand_on(name):
+        if name in HANDED:
+            for call in hand:
+                write([(name, T.rank_of(same[k]), [partner], es) for k, es in call])
 
     def base(b, r):
         return 128 + 5120 * (1 - b) + 640 * r
@@ -171,7 +184,7 @@ def rank_program(g, core, T, topo):
           (T.rw, T.lw)[sd][64 * u + 32 * j:64 * u + 32 * j + 32, :]) for u in range(2) for j in range(2) for sd in range(2)], [], ["X32"])
 
     iota(T.CI[:, 0:1], "CI", [[0, 1]], 0, 1, True)
-    fill(T.c64[:], 64.0, "c64")
+    fill(T.zz[:], 0.0, "zz")
     col, ckey = {}, {}
 
     def bits(lst, k0):
@@ -192,17 +205,29 @@ def rank_program(g, core, T, topo):
     def tsc(out, i, s1, o1, s2, o2, r, w, part=slice(0, 128)):
         ts(out, i, col[s1][part] if s1 in col else s1, o1, col[s2][part] if s2 in col else s2, o2,
            list(r) + [ckey[s] for s in (s1, s2) if s in ckey], w)
+
+    def mat(ap, key, t, wgt, width, row="ci"):
+        tsc(ap, T[row][:, 0:width], t, A.is_equal, wgt, A.mult, [row], [key])
     bits([("sd", 6, 1), ("s5", 5, 1)], 1)
     for n, s, m, a in (("yc", "sd", 79.5, -79.5), ("ys", "sd", 1 - 1.0 / 160, 1.0 / 160), ("al", "sd", -16.0, -64.0),
                        ("ga", "sd", 64.0, 64.0), ("be", "sd", -128.0, 129.0), ("sH", "s5", -64.0, 32.0), ("sL", "s5", -1.0 / 32, 1.0 / 64)):
         ma(n, s, m, a)
+    op("s", lambda e: e.activation(T.CB[:, 0:1], col["sd"], AF.Tanh, bias=-16.0, scale=32.0), [ckey["sd"]], ["CB"])
+    col["sg"], ckey["sg"] = T.CB[:, 0:1], "CB"
     for sd in range(2):
         iota(T.kI[:, 64 * sd:64 * sd + 64], "kI%d" % sd, [[0, 4], [64, 2], [1, 8]], 8 * sd, -1)
-    for k in range(2):
-        pick(T.RW[:, k, :], "RW%d" % k, T.c64[:, 0:128], "c64", [[32, 2], [0, 4], [1, 16]], 16 * k, (16 * k + 64, 64.0))
     iota(T.ci[:], "ci", [[1, 160]])
+    iota(T.xI[:], "xI", [[16, 10], [0, 8]], 0, 0, True)
+    iota(T.bI[:], "bI", [[1, 256]])
+    pw = [[32, 2], [0, 4], [1, 16]]
+    for k in range(2):
+        pick(T.RW[:, k, :], "RW%d" % k, (pw, 16 * k, 64.0), (pw, 16 * k + 64, 64.0))
+    fill(T.W[:, 0:128], -BIG, "Wz")
+    fill(T.W[:, EC:WD], -BIG, "We")
+    fill(T.OT[:, 0:128], 128.0, "OTz")
+    fill(T.OT[:, EC:WD], 128.0, "OTe")
     for k in range(4):
-        ts(T.RI[:, k, :], T.kI[:], -16.0 * k, A.is_equal, None, None, ["kI0", "kI1"], ["RI"])
+        ts(T.RI[:, k, :], T.kI[:], -16.0 * k, A.is_equal, None, None, ["kI0", "kI1"], ["RI%d" % k])
 
     ts(T.qi[:], T.O32[:], -39.5, A.add, 1.0 / 80, A.mult, ["O32"], ["qi"])
     tsc(T.yi[:], T.O32[:], "yc", A.add, "ys", A.mult, ["O32"], ["yi"])
@@ -215,16 +240,19 @@ def rank_program(g, core, T, topo):
     for k, (po, u, src, pi, s) in enumerate(((LO, 0, "hI", LO, "sH"), (HI, 1, "hI", HI, "sH"), (HI, 0, "lI", LO, "sL"), (LO, 1, "lI", HI, "sL"))):
         tsc(T.AWi[po, rank, u, :], T[src][pi, :], s, A.mult, None, None, [src], ["AWi%d" % rank if k == 3 else "z%d" % k], pi)
     send("AWi")
+    hand_on("AOi")
+    hand_on("AWi")
 
     turn = [0]
 
-    def spread(name, r, b, eng):
-        pk = "P" + "ABC"[turn[0] % 3]
-        turn[0] += 1
+    def spread(name, r, b, eng, pk=None):
+        if pk is None:
+            pk = "P" + "ACB"[turn[0] % 3]
+            turn[0] += 1
         P, t = T[pk], T[name]
         if name == "AOi":
             lst = [(P[:, u, 80 * k:80 * k + 80], T.RI[:, k, :], t[:, r, u, 80 * b:80 * b + 80]) for u in range(2) for k in range(4)]
-            km = ["RI"]
+            km = ["RI%d" % k for k in range(4)]
         elif name == "AWi":
             lst = [(P[:, u, 80 * k:80 * k + 80], T.RW[:, k % 2, :], t[:, r, u, 160 * (k // 2) + 80 * b:160 * (k // 2) + 80 * b + 80])
                    for u in range(2) for k in range(4)]
@@ -238,34 +266,11 @@ def rank_program(g, core, T, topo):
         mms([x + (True, True) for x in lst], km + ["%s%d" % (name, r)], [pk + "0", pk + "1"])
         im = "OT" if name[1] == "O" else "W"
         cp(T[im][:, base(b, r):base(b, r) + 640], P[:, :, 0:320], [pk + "0", pk + "1"], ["%s%d%d" % (im, b, r)], eng)
-    kW = ["We"] + ["W%d%d" % (b, r) for b in range(2) for r in range(N)]
-    kOT = ["OTe"] + ["OT%d%d" % (b, r) for b in range(2) for r in range(N)]
+    kW = ["We", "Wz"] + ["W%d%d" % (b, r) for b in range(2) for r in range(N)]
+    kOT = ["OTe", "OTz"] + ["OT%d%d" % (b, r) for b in range(2) for r in range(N)]
 
     def own(im, b):
         return T[im][:, base(b, rank):base(b, rank) + 640], "%s%d%d" % (im, b, rank)
-    for b in range(2):
-        spread("AOi", rank, b, "s")
-    for b in range(2):
-        spread("AOi", order[1], b, "s")
-    for b in range(2):
-        spread("AWi", rank, b, "s")
-
-    iota(T.xI[:], "xI", [[16, 10], [0, 8]], 0, 0, True)
-    bits([("s8", 0, 7), ("hl", 3, 1), ("gp", 4, 7), ("G", 4, 3), ("i", 0, 15), ("s4", 0, 3), ("b2", 2, 1), ("b1", 1, 1), ("b0", 0, 1)], 3)
-    ma("co", "G", 160.0, "i")
-    ma("w", "hl", -79.0, 80.0)
-    ma("tz", "gp", 16.0, 15.0)
-    ma("sw", "sd", -128.0, 64.0)
-    tsc(T.xl[:], T.xI[:], "co", A.add, None, None, ["xI"], ["xl"])
-    tsc(T.ol[:], T.xI[:, 0::8], "co", A.add, None, None, ["xI"], ["ol"])
-    mk("tq", "tz", "s8", A.subtract)
-    mk("tzs", "tz", "sw", A.add)
-
-    def mat(ap, key, t, wgt, width, row="ci"):
-        tsc(ap, T[row][:, 0:width], t, A.is_equal, wgt, A.mult, [row], [key])
-    mat(T.LQ[:], "LQ", "tq", "w", 136)
-    mat(T.Zs[:], "Zs", "tzs", "w", 144)
-    tsc(T.DL[:, 0:8], T.ci[:, 0:8], "s8", A.is_equal, None, None, ["ci"], ["DL"])
 
     def own_slots(b):
         win, k = own("OT", b)
@@ -283,107 +288,113 @@ def rank_program(g, core, T, topo):
         cp(T["LQn%d" % b][:], P[:, 0:80], ["PD1"], ["LQn%d" % b])
         cp(T["LQs%d" % b][LO, :], P[HI, 0:80], ["PD1"], ["LQsa%d" % b])
         cp(T["LQs%d" % b][HI, :], P[LO, 0:80], ["PD1"], ["LQsb%d" % b])
-    own_slots(0)
-    own_slots(1)
-    fill(T.W[:, 0:128], -BIG, "Wz")
-    fill(T.W[:, EC:WD], -BIG, "We")
-    lastw["We"] = lastw["We"] + lastw["Wz"]
-    fill(T.OT[:, 0:128], 128.0, "OTz")
-    fill(T.OT[:, EC:WD], 128.0, "OTe")
-    tsc(T.OT[:, EC:EC + 1], col["hl"], 8.0, A.mult, 128.0, A.add, [ckey["hl"]], ["OTe"])
-    lastw["OTe"] = lastw["OTe"] + lastw["OTz"]
-    for k in range(8):
-        ts(T.ZK[:, k, :], T.Zs[:], T.DL[:, k:k + 1], A.mult, None, None, ["Zs", "DL"], ["ZK%d" % k])
-    kZK = ["ZK%d" % k for k in range(8)]
-    lists(0, T.old0, "old0")
-    op("s", lambda e: e.activation(T.CB[:, 0:1], col["sd"], AF.Tanh, bias=-16.0, scale=32.0), [ckey["sd"]], ["CB"])
-    fill(T.c1[:], 1.0, "c1")
-    for k in range(4):
-        pick(T.RO[:, k, :], "RO%d" % k, T.c1[:, 0:128], "c1", [[64, 2], [0, 4], [1, 16]], 16 * k)
-    iota(T.bI[:], "bI", [[1, 256]])
-    iota(T.pr[:, 0:128], "pr", [[1, 8], [0, 16]])
-    ini = [(r, b) for r in order[2:] for b in range(2)]
-    for j, (r, b) in enumerate(ini[:6]):
-        spread("AOi", r, b, "s")
-    lists(1, T.old1, "old1")
-    mat(T.Z1[:], "Z1", "tz", 1.0, 144)
-    mat(T.ZV[:], "ZV", "tz", -PEN, 144)
-    mat(T.ZVs[:], "ZVs", "tzs", -PEN, 144)
-    for j, (r, b) in enumerate(ini[6:]):
-        spread("AOi", r, b, "vs"[j % 2])
 
     def replies(t):
         b = t % 2
         cp(T.gO[:], T.OT[:].indirect(T["LQs%d" % b][:]), kOT + ["LQsa%d" % b, "LQsb%d" % b], ["gO"], "s")
+    kZK = ["ZK%d" % k for k in range(8)]
 
-    def reply_lists(t):
+    def reply_lists(t, part):
         prs = [(T.ZK[:, (a + t) % 8, 15 - a:143 - a], T.gO[:, 80 * a:80 * a + 80]) for a in range(16)]
         P = bank("PD1")
+        if part:
+            return mm(bank("PD0")[:, 0:80], prs, kZK + ["gO"], ["PD0"], True, False)
         mm(P[:, 0:80], prs, kZK + ["gO"], ["PD1"])
         cp(T.L1[:], P[:, 0:80], ["PD1"], ["L1"])
         cp(T.L2[LO, :], P[HI, 0:80], ["PD1"], ["L2a"])
         cp(T.L2[HI, :], P[LO, 0:80], ["PD1"], ["L2b"])
         ts(T.em[:], P[:, 0:80], EC + 4.0, A.is_gt, 100.0, A.mult, ["PD1"], ["em"])
-        mm(bank("PD0")[:, 0:80], prs, kZK + ["gO"], ["PD0"], True, False)
-    replies(0)
-    for b in range(2):
-        spread("AWi", order[1], b, "v")
+    for name in ("AOi", "AWi"):
+        for b in range(2):
+            spread(name, rank, b, "s")
+
+    bits([("s8", 0, 7), ("hl", 3, 1), ("gp", 4, 7), ("G", 4, 3), ("i", 0, 15), ("s4", 0, 3), ("b2", 2, 1), ("b1", 1, 1), ("b0", 0, 1)], 3)
+    ma("co", "G", 160.0, "i")
+    ma("w", "hl", -79.0, 80.0)
+    ma("tz", "gp", 16.0, 15.0)
+    ma("sw", "sd", -128.0, 64.0)
+    tsc(T.xl[:], T.xI[:], "co", A.add, None, None, ["xI"], ["xl"])
+    tsc(T.ol[:], T.xI[:, 0::8], "co", A.add, None, None, ["xI"], ["ol"])
+    mk("tq", "tz", "s8", A.subtract)
+    mk("tzs", "tz", "sw", A.add)
+    tsc(T.DL[:, 0:8], T.ci[:, 0:8], "s8", A.is_equal, None, None, ["ci"], ["DL"])
+    mat(T.LQ[:], "LQ", "tq", "w", 136)
+    mat(T.Zs[:], "Zs", "tzs", "w", 144)
+    own_slots(0)
+    own_slots(1)
+    own_walls(0)
+    tsc(T.OT[:, EC:EC + 1], col["hl"], 8.0, A.mult, 128.0, A.add, [ckey["hl"]], ["OTe"])
     ma("a0", "b0", -0.5, 1.0)
     ma("a1", "b1", -0.75, 1.0)
     ma("a2", "b2", -0.9375, 1.0)
-    mk("a3", "a0", "a1", A.mult, "a2", A.mult)
     ma("w1", "b2", "w", 0.0)
     ma("t4", "gp", 16.0, "s4")
+    mk("a3", "a0", "a1", A.mult, "a2", A.mult)
+    for k in range(8):
+        ts(T.ZK[:, k, :], T.Zs[:], T.DL[:, k:k + 1], A.mult, None, None, ["Zs", "DL"], ["ZK%d" % k])
+    lists(0, T.old0, "old0")
     tsc(T.fI[:], T.bI[:], "a3", A.mult, -0.5 + 2.0 ** -9, A.add, ["bI"], ["fI"])
     mk("w0", "w", "w1", A.subtract)
     mk("tn", "t4", 12.0, A.add)
     ts(T.fI[:], T.fI[:], 1, A.bitwise_and, None, None, ["fI"], ["fI"])
-    ma("gs", "sw", 1.0 / 16, "gp")
     ma("tm", "i", 1024.0, 0.0)
     cp(T.F[:], T.fI[:], ["fI"], ["F"])
-    reply_lists(0)
-    for j, (r, b) in enumerate(ini[:4]):
-        spread("AWi", r, b, "sv"[j % 2])
-    own_walls(0)
-    for j, (r, b) in enumerate(ini[4:]):
-        spread("AWi", r, b, "vs"[j % 2] if j > 1 else "v")
+    lists(1, T.old1, "old1")
+    for k in range(2):
+        mat(T.LM[:, k, :], "LM%d" % k, "tn", "w%d" % k, 140)
+    ma("de", "sg", 0.25, -0.25)
 
-    def late_constants():
-        for k in range(2):
-            mat(T.LM[:, k, :], "LM%d" % k, "tn", "w%d" % k, 140)
-        mat(T.HA[:], "HA", "gs", HUGE, 128, "pr")
-        fill(T.H2[:], 2.0, "H2")
-        fill(T.RR[:], 0.0, "RR")
-        fill(T.rw4[:], 0.0, "rw4")
-        for k in range(8):
-            fill(T.CS[:, k::8], float(128 >> k), "CS%d" % k)
-        fill(T.H2[:, 0::8], 0.0, "H2")
-        fill(T.RR[:, 0::8], -1e9, "RR")
-        fill(T.rw4[:, 0::4], -HUGE, "rw4")
-        col["sg"], ckey["sg"] = T.CB[:, 0:1], "CB"
-        ma("de", "sg", 0.25, -0.25)
+    def sel(out, src, pat, cmp, val, b0, ch, r, w):
+        op("g", lambda e: e.affine_select(out, src, pat, cmp, val, b0, ch), r, w)
+
+    def block(name, cols, pat, b0, val):
+        ap = T[name][:, cols]
+        if cols.step:
+            sel(T[name][:], T.zz[:, 0:144], [[0, 144]], A.is_equal, 0.0, 0, 0, ["zz"], [name])
+        sel(ap, T.zz[:, 0:ap.shape[1]], pat, A.is_gt, val, b0, -1, ["zz"], [name])
+        sel(ap, ap, pat, A.is_ge, 0.0, b0 + 15, -1, [name], [name])
+    block("Z1", slice(15, 143, 16), [[16, 8]], 0, 1.0)
+    block("ZV", slice(15, 143, 16), [[16, 8]], 0, -PEN)
+    block("ZVs", slice(15, 143, 16), [[-64, 2], [16, 4]], 64, -PEN)
+    p8 = [[0, 10], [1, 8]]
+    sel(T.H2[:], T.zz[:, 0:80], p8, A.is_equal, 2.0, 0, 0, ["zz"], ["H2"])
+    sel(T.RR[:], T.zz[:, 0:80], p8, A.not_equal, -1e9, 0, 0, ["zz"], ["RR"])
+    for k in range(8):
+        sel(T.CS[:, k::8], T.zz[:, 0:10], [[0, 10]], A.not_equal, float(128 >> k), 0, 0, ["zz"], ["CS%d" % k])
+    kCS = ["CS%d" % k for k in range(8)]
+    block("HA", slice(0, 128), [[-64, 2], [16, 4], [0, 16]], 64, HUGE)
+    sel(T.rw4[:], T.zz[:], [[0, 160], [1, 4]], A.not_equal, -HUGE, 0, 0, ["zz"], ["rw4"])
+
+    def output_constants():
         ma("a4", "G", 32.0, "s8")
         ma("a5", "sd", 8.0, 16.0)
         ma("wy", "hl", -159.0, 160.0)
         ma("ci", "hl", 64.5, -64.5)
         mk("ty", "a4", "a5", A.add)
         mat(T.YM[:], "YM", "ty", "wy", 160)
-    kCS = ["CS%d" % k for k in range(8)]
-    fill(T.ta[:, 0:128], 1.0 / 64, "ta")
-    fill(T.tb[:, 0:128], -1.0 / 64, "tb")
-    fill(T.ta[:, 160:288], 1.0 / 128, "tc")
-    fill(T.c64[:], 0.5, "c64")
-    fill(T.r1[:], -1.0, "r1")
-    late_constants()
-    ps, po = [[32, 2], [64, 2], [1, 32]], [[32, 2], [-64, 2], [1, 32]]
-    pick(T.Ms[:], "Ms", T.ta[:, 0:128], "ta", ps, 0)
-    pick(T.Mo[:], "Mo", T.tb[:, 0:128], "tb", po, 64)
-    pick(T.Mh[:], "Mh", T.ta[:, 160:288], "tc", ps, 0)
-    op("g", lambda e: e.affine_select(T.Mh[:], T.Mh[:], po, A.not_equal, -1.0 / 128, 64, -1), ["Mh"], ["Mh"])
-    py = [[16, 5], [-1000, 2], [1, 16]]
-    pick(T.OA[:], "OA", T.c1[:], "c1", py, 1000)
-    pick(T.OB[:], "OB", T.r1[:], "r1", py, 1064)
-    pick(T.OH[:], "OH", T.c64[:], "c64", py, 1000, (1064, -0.5))
+    for k in range(4):
+        pick(T.RO[:, k, :], "RO%d" % k, ([[64, 2], [0, 4], [1, 16]], 16 * k, 1.0))
+    ps, po, py = [[32, 2], [64, 2], [1, 32]], [[32, 2], [-64, 2], [1, 32]], [[16, 5], [-1000, 2], [1, 16]]
+    pick(T.Mh[:], "Mh", (ps, 0, 1.0 / 128), (po, 64, -1.0 / 128))
+    pick(T.Ms[:], "Ms", (ps, 0, 1.0 / 64))
+    pick(T.Mo[:], "Mo", (po, 64, -1.0 / 64))
+    pick(T.OA[:], "OA", (py, 1000, 1.0))
+    pick(T.OB[:], "OB", (py, 1064, -1.0))
+    pick(T.OH[:], "OH", (py, 1000, 0.5), (py, 1064, -0.5))
+
+    for j, r in enumerate(order("AOi")[1:]):
+        for b in range(2):
+            spread("AOi", r, b, "sv"[b] if j > 1 else "s")
+    replies(0)
+    ow = order("AWi")
+    for b in range(2):
+        spread("AWi", ow[1], b, "v")
+    reply_lists(0, 0)
+    for j, r in enumerate(ow[2:]):
+        for b in range(2):
+            spread("AWi", r, b, "sv"[b])
+        if j == 0:
+            reply_lists(0, 1)
 
     def lz(name, a):
         return T[name][:, 15 - a:143 - a]
@@ -419,6 +430,8 @@ def rank_program(g, core, T, topo):
             mm((P2, P3)[q], [(lz("Z1", a), vv[:, 10 * a:10 * a + 10, :, :, :]) for a in range(16)], ["Z1", "V%d" % q] + kv, ["PA%d" % q])
         tt(T.cm2[:], W.indirect(T.L2[:]), T.x[:], A.is_lt, kW + ["L2a", "L2b", "x"], ["cm2"])
         mm(P4, [(lz("ZVs", a), T.cm2[:, a::16]) for a in range(16)], ["ZVs", "cm2"], ["PD0"], False, True)
+        if t < 2:
+            own_walls(1 - t)
         tt(T.a1[:], P2, T.em[:], A.subtract, ["PA0", "em"], ["a1"])
         ts(T.th[:], T.a1[:], THR, A.is_lt, 100.0, A.mult, ["a1"], ["th"])
         tt(T.y[:], P3, T.th[:], A.subtract, ["PA1", "th"], ["y"])
@@ -450,6 +463,8 @@ def rank_program(g, core, T, topo):
         mm(PH, [(T.HA[:], T.nd[:])], ["HA", "nd"], ["PB1"])
         for k in range(2):
             cp(T.w[:, 320 * k:320 * k + 320], W.indirect(T.LN[:, 20 * k:20 * k + 20]), kW + ["LN"], ["w%d" % k], "s")
+        if t < 2:
+            spread("AO%d" % t, rank, t, "s", "PA")
         tt(T.y1[:], PH, T["XO%d" % b][:], A.add, ["PB1", "XO%d" % b], ["y1"])
         tsc(T.q2[:], T.y1[:], "tm", A.min, "de", A.add, ["y1"], ["q2"])
         for k in range(2):
@@ -461,19 +476,18 @@ def rank_program(g, core, T, topo):
         return tn, kt
 
     def tile(t):
-        P1, P2 = bank("PC0")[:, 0:160], bank("PC1")[:, 0:160]
-        mm(P2, [(T.Mh[:], T.q2[:])], ["Mh", "q2"], ["PC1"], True, False)
-        mm(P1, [(T.Ms[:], T.q1[:])], ["Ms", "q1"], ["PC0"], True, False)
-        mm(P2, [(T.Mh[:], T.sw[:, 3::4])], ["Mh", "sw"], ["PC1"], False, True)
-        mm(P1, [(T.Mo[:], T.sw[:, 3::4])], ["Mo", "sw"], ["PC0"], False, True)
-        ts(T.r1[:], P2, MG / 64, A.add, MG / 64, A.subtract, ["PC1"], ["r1"])
-        tt(T.FF[:], P1, T.r1[:], A.min, ["PC0", "r1"], ["FF"])
+        P1, P2, FF = bank("PD0")[:, 0:160], bank("PD1")[:, 0:160], bank("PD1")[:, 160:320]
+        mm(P2, [(T.Mh[:], T.q2[:])], ["Mh", "q2"], ["PD1"], True, False)
+        mm(P1, [(T.Ms[:], T.q1[:])], ["Ms", "q1"], ["PD0"], True, False)
+        mm(P2, [(T.Mh[:], T.sw[:, 3::4])], ["Mh", "sw"], ["PD1"], False, True)
+        mm(P1, [(T.Mo[:], T.sw[:, 3::4])], ["Mo", "sw"], ["PD0"], False, True)
+        ts(T.r1[:], P2, MG / 64, A.add, MG / 64, A.subtract, ["PD1"], ["r1"])
+        tt(FF, P1, T.r1[:], A.min, ["PD0", "r1"], ["PD1"])
         Z, kz = T["AW%d" % t], "AW%d%d" % (t, rank)
-        cp(Z[LO, rank, 0, :], T.FF[LO, :], ["FF"], ["z0"])
-        cp(Z[HI, rank, 1, :], T.FF[HI, :], ["FF"], ["z1"])
-        tt(Z[HI, rank, 0, :], T.FF[LO, :], Z[LO, rank, 0, :], A.subtract, ["FF", "z0"], ["z2"])
-        tt(Z[LO, rank, 1, :], T.FF[HI, :], Z[HI, rank, 1, :], A.subtract, ["FF", "z1"], [kz])
-        send("AW%d" % t)
+        cp(Z[LO, rank, 0, :], FF[LO, :], ["PD1"], ["z0"])
+        cp(Z[HI, rank, 1, :], FF[HI, :], ["PD1"], ["z1"])
+        tt(Z[HI, rank, 0, :], FF[LO, :], Z[LO, rank, 0, :], A.subtract, ["PD1", "z0"], ["z2"])
+        tt(Z[LO, rank, 1, :], FF[HI, :], Z[HI, rank, 1, :], A.subtract, ["PD1", "z1"], [kz])
 
     def put_slots(b, tn, kt):
         P = bank("PD0")[:, 0:80]
@@ -496,21 +510,27 @@ def rank_program(g, core, T, topo):
 
     for t in range(2):
         tn, kt = rnd(t)
-        own_walls(1 - t)
+        hand_on("AO%d" % t)
         tile(t)
+        send("AW%d" % t)
+        hand_on("AW%d" % t)
+        for j, r in enumerate(order("AO%d" % t)[1:]):
+            spread("AO%d" % t, r, t, "sssvsvv"[j])
+        replies(t + 1)
+        ow = order("AW%d" % t)
+        spread("AW%d" % t, rank, t, "v")
         if t == 0:
             lists(0, tn, kt)
+            output_constants()
         else:
             put_slots(1, tn, kt)
             put_walls(1)
-        for j, r in enumerate(order):
-            spread("AO%d" % t, r, t, "ssvsvsvv"[j])
-        replies(t + 1)
-        for j, r in enumerate(order[:2]):
-            spread("AW%d" % t, r, t, "v")
-        reply_lists(t + 1)
-        for j, r in enumerate(order[2:]):
+        spread("AW%d" % t, ow[1], t, "v")
+        reply_lists(t + 1, 0)
+        for j, r in enumerate(ow[2:]):
             spread("AW%d" % t, r, t, "svsvsv"[j])
+            if j == 1:
+                reply_lists(t + 1, 1)
     tn, kt = rnd(2)
     put_slots(0, tn, kt)
     put_walls(0)

@@ -17,20 +17,30 @@ SCRATCH = {
     "CI": ("sbuf", [128, 12], II), "CF": ("sbuf", [128, 12], FI), "CC": ("sbuf", [128, 48], FI), "CB": ("sbuf", [128, 2], FB),
     "ZK": ("sbuf", [128, 8, 144], FB), "RW": ("sbuf", [128, 2, 128], FB), "RI": ("sbuf", [128, 4, 128], FB),
     "RO": ("sbuf", [128, 4, 128], FB), "LM": ("sbuf", [128, 2, 140], FB),
+    "PC": ("psum", [128, 2, 128, 2, 2], FI),
 }
-for _n, _w, _t in (("u x", 1280, FI), ("gO cm1 cm2", 1280, FB), ("w t1 sw", 640, FI), ("rw4 zz", 640, FB),
+for _n, _w, _t in (("u x0 x1", 1280, FI), ("gO cm1 cm2", 1280, FB), ("w t1 sw", 640, FI), ("rw4 zz", 640, FB),
                    ("O32 X32 qi yi hI lI", 320, II), ("ta tb", 320, FI), ("bI", 256, FI), ("fI", 256, II), ("F", 256, FB),
-                   ("ci OA OB OH XO0 XO1 y1 q1 q2 r1 Yl Yr Yo", 160, FI), ("old0 old1 dT mT nd ind YM", 160, FB),
-                   ("Zs Z1 ZV ZVs", 144, FB), ("LQ", 136, FB), ("kI HA", 128, FB), ("Ms Mo Mh", 128, FI),
-                   ("LQn0 LQn1 LQs0 LQs1 L1 L2 LN xl", 80, UU), ("xI", 80, II),
-                   ("em a1 th y gm gb gk gr sc da e0 e1 S1 S2 H2 CS RR mid", 80, FI), ("cx DL", 10, FI), ("cu iu ol", 10, UU)):
+                   ("ci OA OB OH NA NB NH XO0 XO1 XY y1 q1 q2 r1 Yl Yr Yo", 160, FI), ("old0 old1 dT mT nd ind YM", 160, FB),
+                   ("Zs Z1 ZV ZVs", 144, FB), ("LQ", 136, FB), ("kI HA IP", 128, FB), ("Ms Mo Mh Mn Ip In", 128, FI),
+                   ("LQn0 LQn1 LQs0 LQs1 L1 L2 LN xl", 80, UU), ("xI", 80, II), ("sE s0 s1 m3", 80, FB),
+                   ("kk gb sc e0 e1 S1 S2 H2 CS RR mid", 80, FI), ("cx DL", 10, FI), ("cu iu ol", 10, UU)):
     for _k in _n.split():
         SCRATCH[_k] = ("sbuf", [128, _w], _t)
-for _k in "ABCD":
+for _k in "ABD":
     SCRATCH["P" + _k] = ("psum", [128, 2, 512], FI)
 TILES = ("AOi", "AWi", "AO0", "AW0", "AO1", "AW1")
+SEMAPHORES = ["qv", "qt", "qs", "qg", "ls"] + ["%s%d" % (a, r) for a in TILES for r in range(N)] + ["dm%d" % k for k in range(12)] \
+    + ["l%s%d" % (a, k) for a in ("OT", "W") for k in range(4)]
+CY, GA, PE, FX, WAKE, DMA, BYTE = 0.00083, 0.00125, 0.0006, 0.06, 0.06, 2.0, 1.0 / 200000
+CALL, H0, H1, H2 = 0.5, 3.0, 2.0, 2.0
+HOP = {"Oi": H0, "Wi": H0, "O0": H1, "O1": H1, "W0": H2, "W1": H2}
 HANDED = ()
-SEMAPHORES = ["qv", "qt", "qs", "qg", "ls"] + ["%s%d" % (a, r) for a in TILES for r in range(N)] + ["dm%d" % k for k in range(12)]
+SHARED = {"AOi": 4, "AWi": 1}
+M3 = 3.0
+GATE = 1
+ONPE = 1
+M1, M2 = 1.5, 0.5
 
 
 def rank_program(g, core, T, topo):
@@ -38,150 +48,209 @@ def rank_program(g, core, T, topo):
     if rank is None:
         return
     QU = {"v": g.vector, "t": g.tensor, "s": g.scalar, "g": g, "y": g.sync}
-    tot = {}
-    waited = {q: {} for q in QU}
-    lastw, lastr = {}, {}
-    ndma = [0]
+    nodes, lastw, lastr = [], {}, {}
+    gate = {}
 
-    def wait(q, tok):
-        sem, val, tq = tok
-        if waited[q].get(sem, 0) < val:
-            QU[q].wait_ge(T.sem[sem], val)
-            waited[q][sem] = val
+    def node(qs, fn, cost, r=(), w=(), lag=0.0, sem=None):
+        k = len(nodes)
+        hard = {j for x in r for j in lastw.get(x, [])} | {j for x in w for j in lastw.get(x, []) + lastr.get(x, [])}
+        soft = {j for x in r if x[0] == "P" for j in lastr.get(x, [])} - hard
+        nodes.append({"qs": qs, "fn": fn, "cost": cost, "hard": hard, "soft": soft, "lag": lag, "sem": sem, "after": dict(gate)})
+        for x in r:
+            lastr.setdefault(x, []).append(k)
+        for x in w:
+            lastw[x], lastr[x] = [k], []
 
-    def need(q, r, w):
-        for k in r:
-            for t in lastw.get(k, []):
-                wait(q, t)
-            if k[0] == "P":
-                for t in lastr.get(k, []):
-                    if t[2] != q:
-                        wait(q, t)
-        for k in w:
-            for t in lastw.get(k, []) + lastr.get(k, []):
-                if not (q == "t" and t[2] == "t"):
-                    wait(q, t)
+    def size(ap):
+        n = 1
+        for s in ap.shape[1:]:
+            n *= s
+        return n
 
-    def done(tok, r, w):
-        for k in r:
-            lastr.setdefault(k, []).append(tok)
-        for k in w:
-            lastw[k], lastr[k] = [tok], []
+    def op(qs, fn, out, c, r, w):
+        node(qs, fn, FX + max(64 * CY, size(out) * c), r, w)
 
-    def op(q, fn, r=(), w=()):
-        need(q, r, w)
-        s = "q" + q
-        tot[s] = tot.get(s, 0) + 1
-        fn(QU[q]).then_inc(T.sem[s], 1)
-        done((s, tot[s], q), r, w)
+    def dma(q, parts, r=(), w=()):
+        s = "dm%d" % len([x for x in nodes if x["sem"] and x["sem"][0][:2] == "dm"])
 
-    def dma(parts, r=(), w=()):
-        s = "dm%d" % ndma[0]
-        ndma[0] += 1
-        for q, o, i in parts:
-            need(q, r, w)
-            QU[q].dma_start(o, i).then_inc(T.sem[s], 16)
-        tot[s] = 16 * len(parts)
-        done((s, tot[s], "d" + s), r, w)
+        def fn(e, _):
+            for o, i in parts:
+                e.dma_start(o, i).then_inc(T.sem[s], 16)
+        node(q, fn, 0.05 * len(parts), r, w, DMA, (s, 16 * len(parts)))
 
-    def mms(lst, r, w):
-        need("t", r, w)
-        for o, l, x, a, z in lst:
-            ins = g.tensor.matmul(o, l, x, a, z)
-        tot["qt"] = tot.get("qt", 0) + 1
-        ins.then_inc(T.sem.qt, 1)
-        done(("qt", tot["qt"], "t"), r, w)
+    def mms(lst, r, w, c=1):
+        def fn(e, _):
+            for o, l, x, a, z in lst:
+                ins = e.matmul(o, l, x, a, z)
+            return ins
+        node("t", fn, sum(max(64, size(x[2])) for x in lst) * c * PE, r, w)
 
-    def mm(out, pairs, r, w, first=True, last=True):
-        mms([(out, l, x, first and k == 0, last and k == len(pairs) - 1) for k, (l, x) in enumerate(pairs)], r, w)
+    def mm(out, pairs, r, w, first=True, last=True, c=1):
+        mms([(out, l, x, first and k == 0, last and k == len(pairs) - 1) for k, (l, x) in enumerate(pairs)], r, w, c)
 
     def ts(out, i, s1, o1, s2=None, o2=None, r=(), w=()):
         if o2 is None:
-            op("v", lambda e: e.tensor_scalar(out, i, s1, None, o1), r, w)
+            op("v", lambda e, _: e.tensor_scalar(out, i, s1, None, o1), out, CY, r, w)
         else:
-            op("v", lambda e: e.tensor_scalar(out, i, s1, s2, o1, o2), r, w)
+            op("v", lambda e, _: e.tensor_scalar(out, i, s1, s2, o1, o2), out, CY, r, w)
 
-    def tt(out, a, b, o, r, w):
-        op("v", lambda e: e.tensor_tensor(out, a, b, o), r, w)
+    def tt(out, a, b, o, r, w, c=None):
+        op("v", lambda e, _: e.tensor_tensor(out, a, b, o), out, c or (CY if [x for x in r if x[0] == "P"] else 2 * CY), r, w)
 
-    def cp(out, i, r, w, q="v", bias=0.0):
-        if q == "v":
-            op("v", lambda e: e.tensor_copy(out, i), r, w)
-        else:
-            op("s", lambda e: e.activation(out, i, AF.Identity, bias=bias), r, w)
+    def cp(out, i, r, w, qs="v", c=CY):
+        op(qs, lambda e, q: e.tensor_copy(out, i) if q == "v" else e.activation(out, i, AF.Identity), out, c, r, w)
+
+    def act(out, i, f, bias, scale, r, w, c=CY):
+        op("s", lambda e, _: e.activation(out, i, f, bias=bias, scale=scale), out, c, r, w)
 
     def scan(out, a, b, o0, o1, r, w):
-        op("v", lambda e: e.tensor_tensor_scan(out, a, b, 0.0, o0, o1), r, w)
+        op("v", lambda e, _: e.tensor_tensor_scan(out, a, b, 0.0, o0, o1), out, CY, r, w)
 
     def fill(ap, c, key):
-        op("v", lambda e: e.memset(ap, c), [], [key])
+        op("v", lambda e, _: e.memset(ap, c), ap, CY / 2, [], [key])
 
     def iota(ap, key, pat, base=0, ch=0, whole=False):
         if whole:
-            op("g", lambda e: e.iota(ap, pat, base, ch), [], [key])
+            node("g", lambda e, _: e.iota(ap, pat, base, ch), 0.13 + 2 * CY * size(ap), [], [key])
         else:
-            op("g", lambda e: e.iota(ap, pat, base, ch, allow_small_or_imprecise_dtypes=True), [], [key])
+            node("g", lambda e, _: e.iota(ap, pat, base, ch, allow_small_or_imprecise_dtypes=True), 0.13 + 2 * CY * size(ap), [], [key])
+
+    def sel(out, src, pat, cmp, val, b0, ch, r, w):
+        node("g", lambda e, _: e.affine_select(out, src, pat, cmp, val, b0, ch), 0.17 + 2 * CY * size(out), r, w)
 
     def pick(ap, key, *terms):
         src, ks = T.zz[:, 0:ap.shape[1]], "zz"
         for pat, b0, val in terms:
-            op("g", lambda e: e.affine_select(ap, src, pat, A.not_equal, val, b0, -1), [ks], [key])
+            sel(ap, src, pat, A.not_equal, val, b0, -1, [ks], [key])
             src, ks = ap, key
 
-    def bank(k):
-        return T["P" + k[1]][:, int(k[2]), :]
+    def block(name, cols, pat, b0, val):
+        ap = T[name][:, cols]
+        if cols.step:
+            sel(T[name][:], T.zz[:, 0:144], [[0, 144]], A.is_equal, 0.0, 0, 0, ["zz"], [name])
+        sel(ap, T.zz[:, 0:ap.shape[1]], pat, A.is_gt, val, b0, -1, ["zz"], [name])
+        sel(ap, ap, pat, A.is_ge, 0.0, b0 + 15, -1, [name], [name])
+
+    def issue():
+        rk = [0.0] * len(nodes)
+        for k in range(len(nodes) - 1, -1, -1):
+            x = nodes[k]
+            rk[k] += x["cost"] + x["lag"] + x.get("more", 0.0)
+            for j in x["hard"] | x["soft"] | set(x["after"].values()):
+                rk[j] = max(rk[j], rk[k] + WAKE)
+        busy = {q: [] for q in "vtsgyxz"}
+        for k in sorted(range(len(nodes)), key=lambda k: -rk[k]):
+            x, best = nodes[k], None
+            for q in x["qs"]:
+                t = max([0.0] + [nodes[j]["end"] + (0.0 if nodes[j]["q"] == q == "t" else WAKE) for j in x["hard"]]
+                        + [nodes[j]["end"] + (0.0 if nodes[j]["q"] == q else WAKE) for j in x["soft"]])
+                if q in x["after"]:
+                    t = max(t, nodes[x["after"][q]]["end"])
+                for a, z in busy[q]:
+                    if t + x["cost"] <= a:
+                        break
+                    t = max(t, z)
+                if best is None or t < best[0]:
+                    best = (t, q)
+            x["at"], x["q"] = best
+            x["end"] = x["at"] + x["cost"] + x["lag"]
+            busy[x["q"]] = sorted(busy[x["q"]] + [(x["at"], x["at"] + x["cost"])])
+        line = sorted(nodes, key=lambda x: x["at"])
+        tot, waited = {}, {q: {} for q in QU}
+        for x in line:
+            s, n = x["sem"] or ("q" + x["q"], 1)
+            tot[s] = tot.get(s, 0) + n
+            x["tok"] = (s, tot[s])
+        for x in line:
+            q = x["q"]
+            if q not in QU:
+                continue
+            need = {}
+            for j in x["hard"] | x["soft"]:
+                y = nodes[j]
+                if not (y["q"] == q and (q == "t" or j in x["soft"])):
+                    need[y["tok"][0]] = max(need.get(y["tok"][0], 0), y["tok"][1])
+            for s, n in need.items():
+                if waited[q].get(s, 0) < n:
+                    QU[q].wait_ge(T.sem[s], n)
+                    waited[q][s] = n
+            ins = x["fn"](QU[q], q)
+            if not x["sem"]:
+                ins.then_inc(T.sem["q" + q], 1)
+        for s in tot:
+            g.wait_ge(T.sem[s], tot[s])
+
+    def pv(k, a, n):
+        h = int(k[2])
+        return T.PC[:, h, a // 4:(a + n) // 4, :, :] if k[1] == "C" else T[k[:2]][:, h, a:a + n]
     LO, HI = slice(0, 64), slice(64, 128)
 
     def way(c):
         return 0 if c in topo.cores_of(core) else 1 if topo.mates(core, c) else 2 if topo.same_plane(core, c) else 3
-    others = sorted([c for c in T.cores if c != core], key=way)
-    partner = others[0]
+    others = sorted([c for c in T.cores if c != core], key=lambda c: (way(c) == 3, way(c) > 0, topo.die(c) != topo.die(core), way(c)))
+    order = [T.rank_of(c) for c in [core] + others]
+    offe = topo.engines(core, others[-1])
+    one = [e for e in topo.engines(core, others[0]) if e not in offe]
+
     same = [c for c in others[1:] if topo.die(c) == topo.die(core)]
     cross = [c for c in others[1:] if c not in same]
-    offe = topo.engines(core, same[0])
-    one = [e for e in topo.engines(core, partner) if e not in offe]
     hand = (((0, one[:len(one) // 2]), (1, one[len(one) // 2:])), ((2, one),))
 
-    def order(name):
-        far = same + cross if name in HANDED else [same[0], same[1], cross[0], cross[1], same[2], cross[2]]
-        return [T.rank_of(c) for c in [core, partner] + far]
-
-    def write(parts):
+    def write(name, parts, cost, come):
         trs = []
-        for name, r, dst, es in parts:
-            need("g", ["%s%d" % (name, r)], [])
+        for r, dst, es in parts:
             ids = []
             for c in dst:
                 rid, pid = topo.addr(c, core)
                 ids.append(DstId(rid=rid, pnc=pid))
             trs.append(RemoteDMATransfer(dst_ids=ids, dma_engine_mask=sum(1 << e for e in es), remote_sem=T.sem["%s%d" % (name, r)],
                                          srcs=[T[name][:, r]], dsts=[T[name][:, r] for _ in dst], alu_op=0))
-            tot["ls"] = tot.get("ls", 0) + len(es)
-        g.remote_dma_fused(trs, local_sem=T.sem.ls)
+        sent = "sent%d" % len(nodes)
+        node("g", lambda e, _: e.remote_dma_fused(trs, local_sem=T.sem.ls), cost, ["%s%d" % (name, r) for r, _, _ in parts], [sent],
+             0.0, ("ls", sum(len(es) for _, _, es in parts)))
+        for c, es in come:
+            k = "%s%d" % (name, T.rank_of(c))
+            node("x" if es is offe else "z", None, 256 * size(T[name][:, 0]) * BYTE, [sent], [k], HOP[name[1:]], (k, len(es)))
+
+    def theirs(name):
+        return ([others[0]] + cross)[:SHARED.get(name, 0)]
 
     def send(name):
-        far = same if name in HANDED else [T.cores[r] for r in order(name)[2:]]
-        write([(name, rank, [partner], one), (name, rank, far, offe)])
-        cnt = [(partner, len(one))] + [(c, len(offe)) for c in far]
-        if name in HANDED:
-            cnt += [(cross[k], len(es)) for call in hand for k, es in call]
-        for c, n in cnt:
-            k = "%s%d" % (name, T.rank_of(c))
-            tot[k] = n
-            lastw[k] = [(k, n, "x")]
+        far = same if name in HANDED else [c for c in others[1:] if c not in theirs(name)]
+        near = [] if theirs(name) else others[:1]
+        write(name, [(rank, near, one)] * len(near) + [(rank, far, offe)], 2.5 if name == TILES[0] else CALL,
+              [(c, one) for c in near] + [(c, offe) for c in far])
+        for call in hand if name in HANDED else ():
+            write(name, [(T.rank_of(same[k]), others[:1], es) for k, es in call], CALL, [(cross[k], es) for k, es in call])
 
-    def hand_on(name):
-        if name in HANDED:
-            for call in hand:
-                write([(name, T.rank_of(same[k]), [partner], es) for k, es in call])
+    def coming(name):
+        return [T.rank_of(c) for c in [core, others[0]] + same + cross] if name in HANDED else \
+            [r for r in order if T.cores[r] not in theirs(name)]
 
     def base(b, r):
         return 128 + 5120 * (1 - b) + 640 * r
 
-    dma([("ys"[u], T.O32[64 * hl:64 * hl + 64, 160 * u:160 * u + 160], T.opts[64 * u:64 * u + 64, :])
-         for hl in range(2) for u in range(2)], [], ["O32"])
-    dma([("ys"[sd], T.X32[64 * u + 32 * sd:64 * u + 32 * sd + 32, 160 * j:160 * j + 160],
-          (T.rw, T.lw)[sd][64 * u + 32 * j:64 * u + 32 * j + 32, :]) for u in range(2) for j in range(2) for sd in range(2)], [], ["X32"])
+    def share(name, r):
+        mine = [T.rank_of(c) for c in [core] + same][:SHARED.get(name, 0)]
+        if r in mine:
+            im, o = "OT" if name[1] == "O" else "W", T.rank_of(theirs(name)[mine.index(r)])
+            rid, pid = topo.addr(others[0], core)
+            trs = [RemoteDMATransfer(dst_ids=[DstId(rid=rid, pnc=pid)], dma_engine_mask=sum(1 << e for e in hand[0][b][1]),
+                                     remote_sem=T.sem["%s%d" % (name, r)], srcs=[T[im][:, base(b, r):base(b, r) + 640]],
+                                     dsts=[T[im][:, base(b, r):base(b, r) + 640]], alu_op=0) for b in range(2)]
+            sent = "sent%d" % len(nodes)
+            left = "l%s%d" % (im, mine.index(r))
+            node("g", lambda e, _: e.remote_dma_fused(trs, local_sem=T.sem[left]), CALL, ["%s%d%d" % (im, b, r) for b in range(2)], [sent],
+                 0.0, (left, len(one)))
+            node("z", None, 128 * 1280 * (2 if im == "OT" else 4) * BYTE, [sent], ["%s%d%d" % (im, b, o) for b in range(2)], 2.0,
+                 ("%s%d" % (name, o), len(one)))
+
+    for u in range(2):
+        dma("ys"[u], [(T.O32[64 * hl:64 * hl + 64, 160 * u:160 * u + 160], T.opts[64 * u:64 * u + 64, :]) for hl in range(2)], [], ["O32%d" % u])
+    for sd in range(2):
+        dma("ys"[sd], [(T.X32[64 * u + 32 * sd:64 * u + 32 * sd + 32, 160 * j:160 * j + 160],
+                        (T.rw, T.lw)[sd][64 * u + 32 * j:64 * u + 32 * j + 32, :]) for u in range(2) for j in range(2)], [], ["X32%d" % sd])
+    kO, kX = ["O320", "O321"], ["X320", "X321"]
 
     iota(T.CI[:, 0:1], "CI", [[0, 1]], 0, 1, True)
     fill(T.zz[:], 0.0, "zz")
@@ -193,27 +262,35 @@ def rank_program(g, core, T, topo):
             col[n], ckey[n] = T.CF[:, k0 + k:k0 + k + 1], "CF%d" % k0
         cp(T.CF[:, k0:k0 + len(lst)], T.CI[:, k0:k0 + len(lst)], ["CI" + n for n, _, _ in lst], ["CF%d" % k0])
 
-    def mk(name, src, s1, o1, s2=None, o2=None):
-        k = len([n for n in ckey if ckey[n][:2] == "CC"])
-        ts(T.CC[:, k:k + 1], col[src], col.get(s1, s1), o1, col.get(s2, s2), o2,
-           [ckey[s] for s in (src, s1, s2) if s in ckey], ["CC%d" % k])
-        col[name], ckey[name] = T.CC[:, k:k + 1], "CC%d" % k
-
     def ma(name, src, m, a):
-        mk(name, src, m, A.mult, a, A.add)
+        k = len([n for n in ckey if ckey[n][:2] == "CC"])
+        o, i, cm, ca = T.CC[:, k:k + 1], col[src], col.get(m, m), col.get(a, a)
+        op("vs", lambda e, q: e.tensor_scalar(o, i, cm, ca, A.mult, A.add) if q == "v" else e.activation(o, i, AF.Identity, bias=ca, scale=cm),
+           o, CY, [ckey[s] for s in (src, m, a) if s in ckey], ["CC%d" % k])
+        col[name], ckey[name] = o, "CC%d" % k
 
     def tsc(out, i, s1, o1, s2, o2, r, w, part=slice(0, 128)):
         ts(out, i, col[s1][part] if s1 in col else s1, o1, col[s2][part] if s2 in col else s2, o2,
            list(r) + [ckey[s] for s in (s1, s2) if s in ckey], w)
 
-    def mat(ap, key, t, wgt, width, row="ci"):
-        tsc(ap, T[row][:, 0:width], t, A.is_equal, wgt, A.mult, [row], [key])
+    def mat(ap, key, t, wgt, width):
+        tsc(ap, T.ci[:, 0:width], t, A.is_equal, wgt, A.mult, ["ci"], [key])
     bits([("sd", 6, 1), ("s5", 5, 1)], 1)
     for n, s, m, a in (("yc", "sd", 79.5, -79.5), ("ys", "sd", 1 - 1.0 / 160, 1.0 / 160), ("al", "sd", -16.0, -64.0),
                        ("ga", "sd", 64.0, 64.0), ("be", "sd", -128.0, 129.0), ("sH", "s5", -64.0, 32.0), ("sL", "s5", -1.0 / 32, 1.0 / 64)):
         ma(n, s, m, a)
-    op("s", lambda e: e.activation(T.CB[:, 0:1], col["sd"], AF.Tanh, bias=-16.0, scale=32.0), [ckey["sd"]], ["CB"])
+    act(T.CB[:, 0:1], col["sd"], AF.Tanh, -16.0, 32.0, [ckey["sd"]], ["CB"], 1.4)
     col["sg"], ckey["sg"] = T.CB[:, 0:1], "CB"
+    bits([("s8", 0, 7), ("hl", 3, 1), ("gp", 4, 7), ("G", 4, 3), ("i", 0, 15)], 3)
+    bits([("s4", 0, 3), ("b2", 2, 1), ("b1", 1, 1), ("b0", 0, 1)], 8)
+    for n, s, m, a in (("co", "G", 160.0, "i"), ("w", "hl", -79.0, 80.0), ("tz", "gp", 16.0, 15.0), ("sw", "sg", -64.0, 0.0),
+                       ("a0", "b0", -0.5, 1.0), ("a1", "b1", -0.75, 1.0), ("a2", "b2", -0.9375, 1.0), ("w1", "b2", "w", 0.0),
+                       ("t4", "gp", 16.0, "s4"), ("tm", "i", 1024.0, 0.0), ("a4", "G", 32.0, "s8"),
+                       ("a5", "sd", 8.0, 16.0), ("wy", "hl", -159.0, 160.0), ("wi", "hl", 64.5, -64.5),
+                       ("tq", "s8", -1.0, "tz"), ("tzs", "tz", 1.0, "sw"), ("a6", "a0", "a1", 0.0), ("a3", "a6", "a2", 0.0),
+                       ("w0", "w1", -1.0, "w"), ("tn", "t4", 1.0, 12.0), ("ty", "a4", 1.0, "a5")):
+        ma(n, s, m, a)
+
     for sd in range(2):
         iota(T.kI[:, 64 * sd:64 * sd + 64], "kI%d" % sd, [[0, 4], [64, 2], [1, 8]], 8 * sd, -1)
     iota(T.ci[:], "ci", [[1, 160]])
@@ -222,50 +299,93 @@ def rank_program(g, core, T, topo):
     pw = [[32, 2], [0, 4], [1, 16]]
     for k in range(2):
         pick(T.RW[:, k, :], "RW%d" % k, (pw, 16 * k, 64.0), (pw, 16 * k + 64, 64.0))
+        mat(T.LM[:, k, :], "LM%d" % k, "tn", "w%d" % k, 140)
+    for k in range(4):
+        ts(T.RI[:, k, :], T.kI[:], -16.0 * k, A.is_equal, None, None, ["kI0", "kI1"], ["RI%d" % k])
+        pick(T.RO[:, k, :], "RO%d" % k, ([[64, 2], [0, 4], [1, 16]], 16 * k, 1.0))
+    tsc(T.xl[:], T.xI[:], "co", A.add, None, None, ["xI"], ["xl"])
+    tsc(T.ol[:], T.xI[:, 0::8], "co", A.add, None, None, ["xI"], ["ol"])
+    tsc(T.DL[:, 0:8], T.ci[:, 0:8], "s8", A.is_equal, None, None, ["ci"], ["DL"])
+    mat(T.LQ[:], "LQ", "tq", "w", 136)
+    mat(T.Zs[:], "Zs", "tzs", "w", 144)
+    mat(T.YM[:], "YM", "ty", "wy", 160)
+    kZK, kCS = ["ZK%d" % k for k in range(8)], ["CS%d" % k for k in range(8)]
+    for k in range(8):
+        op("vs", lambda e, q, k=k: e.tensor_scalar(T.ZK[:, k, :], T.Zs[:], T.DL[:, k:k + 1], None, A.mult) if q == "v" else
+           e.activation(T.ZK[:, k, :], T.Zs[:], AF.Identity, scale=T.DL[:, k:k + 1]), T.Zs[:], CY / 2, ["Zs", "DL"], [kZK[k]])
+        sel(T.CS[:, k::8], T.zz[:, 0:10], [[0, 10]], A.not_equal, float(128 >> k), 0, 0, ["zz"], [kCS[k]])
+    tsc(T.fI[:], T.bI[:], "a3", A.mult, -0.5 + 2.0 ** -9, A.add, ["bI"], ["fI"])
+    ts(T.fI[:], T.fI[:], 1, A.bitwise_and, None, None, ["fI"], ["fI"])
+    cp(T.F[:], T.fI[:], ["fI"], ["F"])
+    block("Z1", slice(15, 143, 16), [[16, 8]], 0, 1.0)
+    block("ZV", slice(15, 143, 16), [[16, 8]], 0, -PEN)
+    block("ZVs", slice(15, 143, 16), [[-64, 2], [16, 4]], 64, -PEN)
+    block("HA", slice(0, 128), [[-64, 2], [16, 4], [0, 16]], 64, HUGE)
+    p8, p1 = [[0, 10], [1, 8]], [[1, 128]]
+    sel(T.H2[:], T.zz[:, 0:80], p8, A.is_equal, 2.0, 0, 0, ["zz"], ["H2"])
+    sel(T.RR[:], T.zz[:, 0:80], p8, A.not_equal, -1e9, 0, 0, ["zz"], ["RR"])
+    sel(T.m3[:], T.zz[:, 0:80], [[0, 80]], A.not_equal, -3.0, 0, 0, ["zz"], ["m3"])
+    sel(T.rw4[:], T.zz[:], [[0, 160], [1, 4]], A.not_equal, -HUGE, 0, 0, ["zz"], ["rw4"])
+    sel(T.q2[:], T.zz[:, 0:160], [[0, 160]], A.is_ge, -0.5, -64, 1, ["zz"], ["q2"])
+    pick(T.IP[:], "IP", (p1, 0, PEN / 2))
+    pick(T.Ip[:], "Ip", (p1, 0, 1.0))
+    pick(T.In[:], "In", (p1, 0, -1.0))
+    ps, po, py = [[32, 2], [64, 2], [1, 32]], [[32, 2], [-64, 2], [1, 32]], [[16, 5], [-1000, 2], [1, 16]]
+    pick(T.Mh[:], "Mh", (ps, 0, 1.0 / 128), (po, 64, -1.0 / 128))
+    pick(T.Mn[:], "Mn", (ps, 0, -1.0 / 128), (po, 64, 1.0 / 128))
+    pick(T.Ms[:], "Ms", (ps, 0, -1.0 / 64))
+    tsc(T.y1[:], T.zz[:, 0:160], "tm", A.subtract, None, None, ["zz"], ["y1"])
+    pick(T.NA[:], "NA", (py, 1000, -1.0))
+    pick(T.NB[:], "NB", (py, 1064, 1.0))
+    pick(T.NH[:], "NH", (py, 1000, -0.5), (py, 1064, 0.5))
+    pick(T.Mo[:], "Mo", (po, 64, -1.0 / 64))
+    pick(T.OA[:], "OA", (py, 1000, 1.0))
+    pick(T.OB[:], "OB", (py, 1064, -1.0))
+    pick(T.OH[:], "OH", (py, 1000, 0.5), (py, 1064, -0.5))
     fill(T.W[:, 0:128], -BIG, "Wz")
     fill(T.W[:, EC:WD], -BIG, "We")
     fill(T.OT[:, 0:128], 128.0, "OTz")
     fill(T.OT[:, EC:WD], 128.0, "OTe")
-    for k in range(4):
-        ts(T.RI[:, k, :], T.kI[:], -16.0 * k, A.is_equal, None, None, ["kI0", "kI1"], ["RI%d" % k])
+    tsc(T.OT[:, EC:EC + 1], col["hl"], 8.0, A.mult, 128.0, A.add, [ckey["hl"]], ["OTe"])
 
-    ts(T.qi[:], T.O32[:], -39.5, A.add, 1.0 / 80, A.mult, ["O32"], ["qi"])
-    tsc(T.yi[:], T.O32[:], "yc", A.add, "ys", A.mult, ["O32"], ["yi"])
+    ts(T.qi[:], T.O32[:], -39.5, A.add, 1.0 / 80, A.mult, kO, ["qi"])
+    tsc(T.yi[:], T.O32[:], "yc", A.add, "ys", A.mult, kO, ["yi"])
     tsc(T.ta[:], T.qi[:], "al", A.mult, "ga", A.add, ["qi"], ["ta"])
     tsc(T.tb[:], T.yi[:], "be", A.mult, None, None, ["yi"], ["tb"])
     tt(T.AOi[:, rank], T.ta[:], T.tb[:], A.add, ["ta", "tb"], ["AOi%d" % rank])
     send("AOi")
-    ts(T.hI[:], T.X32[:], 11, A.arith_shift_right, None, None, ["X32"], ["hI"])
-    ts(T.lI[:], T.X32[:], 2047, A.bitwise_and, None, None, ["X32"], ["lI"])
-    for k, (po, u, src, pi, s) in enumerate(((LO, 0, "hI", LO, "sH"), (HI, 1, "hI", HI, "sH"), (HI, 0, "lI", LO, "sL"), (LO, 1, "lI", HI, "sL"))):
-        tsc(T.AWi[po, rank, u, :], T[src][pi, :], s, A.mult, None, None, [src], ["AWi%d" % rank if k == 3 else "z%d" % k], pi)
+    ts(T.hI[:], T.X32[:], 11, A.arith_shift_right, None, None, kX, ["hI"])
+    ts(T.lI[:], T.X32[:], 2047, A.bitwise_and, None, None, kX, ["lI"])
+    for k, (p_o, u, src, p_i, s) in enumerate(((LO, 0, "hI", LO, "sH"), (HI, 1, "hI", HI, "sH"), (HI, 0, "lI", LO, "sL"), (LO, 1, "lI", HI, "sL"))):
+        tsc(T.AWi[p_o, rank, u, :], T[src][p_i, :], s, A.mult, None, None, [src], ["z%d" % k], p_i)
+    kz = ["z%d" % k for k in range(4)]
+    lastw["AWi%d" % rank] = [j for k in kz for j in lastw[k]]
     send("AWi")
-    hand_on("AOi")
-    hand_on("AWi")
 
     turn = [0]
 
-    def spread(name, r, b, eng, pk=None):
+    def spread(name, r, b, pk=None):
         if pk is None:
             pk = "P" + "ACB"[turn[0] % 3]
             turn[0] += 1
-        P, t = T[pk], T[name]
+        t = T[name]
         if name == "AOi":
-            lst = [(P[:, u, 80 * k:80 * k + 80], T.RI[:, k, :], t[:, r, u, 80 * b:80 * b + 80]) for u in range(2) for k in range(4)]
+            lst = [(pv(pk + str(u), 80 * k, 80), T.RI[:, k, :], t[:, r, u, 80 * b:80 * b + 80]) for u in range(2) for k in range(4)]
             km = ["RI%d" % k for k in range(4)]
         elif name == "AWi":
-            lst = [(P[:, u, 80 * k:80 * k + 80], T.RW[:, k % 2, :], t[:, r, u, 160 * (k // 2) + 80 * b:160 * (k // 2) + 80 * b + 80])
+            lst = [(pv(pk + str(u), 80 * k, 80), T.RW[:, k % 2, :], t[:, r, u, 160 * (k // 2) + 80 * b:160 * (k // 2) + 80 * b + 80])
                    for u in range(2) for k in range(4)]
             km = ["RW0", "RW1"]
         elif name[1] == "O":
-            lst = [(P[:, k // 2, 160 * (k % 2):160 * (k % 2) + 160], T.RO[:, k, :], t[:, r, :]) for k in range(4)]
+            lst = [(pv(pk + str(k // 2), 160 * (k % 2), 160), T.RO[:, k, :], t[:, r, :]) for k in range(4)]
             km = ["RO%d" % k for k in range(4)]
         else:
-            lst = [(P[:, k // 2, 160 * (k % 2):160 * (k % 2) + 160], T.RW[:, k % 2, :], t[:, r, k // 2, :]) for k in range(4)]
+            lst = [(pv(pk + str(k // 2), 160 * (k % 2), 160), T.RW[:, k % 2, :], t[:, r, k // 2, :]) for k in range(4)]
             km = ["RW0", "RW1"]
         mms([x + (True, True) for x in lst], km + ["%s%d" % (name, r)], [pk + "0", pk + "1"])
         im = "OT" if name[1] == "O" else "W"
-        cp(T[im][:, base(b, r):base(b, r) + 640], P[:, :, 0:320], [pk + "0", pk + "1"], ["%s%d%d" % (im, b, r)], eng)
+        cp(T[im][:, base(b, r):base(b, r) + 640], T.PC[:, :, 0:80, :, :] if pk == "PC" else T[pk][:, :, 0:320],
+           [pk + "0", pk + "1"], ["%s%d%d" % (im, b, r)], "sv")
     kW = ["We", "Wz"] + ["W%d%d" % (b, r) for b in range(2) for r in range(N)]
     kOT = ["OTe", "OTz"] + ["OT%d%d" % (b, r) for b in range(2) for r in range(N)]
 
@@ -274,266 +394,211 @@ def rank_program(g, core, T, topo):
 
     def own_slots(b):
         win, k = own("OT", b)
-        cp(T["old%d" % b][:], win.indirect(T.ol[:]), [k, "ol"], ["old%d" % b], "s")
+        cp(T["old%d" % b][:], win.indirect(T.ol[:]), [k, "ol"], ["old%d" % b], "sv", GA)
 
     def own_walls(b):
         win, k = own("W", b)
-        cp(T.x[:], win.indirect(T.xl[:]), [k, "xl"], ["x"], "s")
-        cp(T["XO%d" % b][:], win.indirect(T.ol[:]), [k, "ol"], ["XO%d" % b], "s", -BIG)
+        for h in range(2):
+            cp(T["x%d" % b][:, 640 * h:640 * h + 640], win.indirect(T.xl[:, 40 * h:40 * h + 40]), [k, "xl"], ["x%d%d" % (b, h)], "sv", GA)
+        act(T["XO%d" % b][:], win.indirect(T.ol[:]), AF.Identity, -BIG, 1.0, [k, "ol"], ["XO%d" % b], GA)
 
-    def lists(b, src, ks):
-        P = bank("PD1")
-        mms([(P[:, c:80:5], T.LQ[:, 8 - 8 * h:136 - 8 * h], src[:, 32 * c + 16 * h:32 * c + 16 * h + 16], h == 0, h == 1)
-             for c in range(5) for h in range(2)], ["LQ", ks], ["PD1"])
-        cp(T["LQn%d" % b][:], P[:, 0:80], ["PD1"], ["LQn%d" % b])
-        cp(T["LQs%d" % b][LO, :], P[HI, 0:80], ["PD1"], ["LQsa%d" % b])
-        cp(T["LQs%d" % b][HI, :], P[LO, 0:80], ["PD1"], ["LQsb%d" % b])
+    def lists(b, src, ks, pk):
+        P = pv(pk, 0, 80)
+        mms([(P[:, c::5], T.LQ[:, 8 - 8 * h:136 - 8 * h], src[:, 32 * c + 16 * h:32 * c + 16 * h + 16], h == 0, h == 1)
+             for c in range(5) for h in range(2)], ["LQ", ks], [pk])
+        cp(T["LQn%d" % b][:], P, [pk], ["LQn%d" % b])
+        cp(T["LQs%d" % b][LO, :], P[HI, :], [pk], ["LQsa%d" % b])
+        cp(T["LQs%d" % b][HI, :], P[LO, :], [pk], ["LQsb%d" % b])
 
     def replies(t):
         b = t % 2
-        cp(T.gO[:], T.OT[:].indirect(T["LQs%d" % b][:]), kOT + ["LQsa%d" % b, "LQsb%d" % b], ["gO"], "s")
-    kZK = ["ZK%d" % k for k in range(8)]
-
-    def reply_lists(t, part):
+        P0, P4 = pv("PD1", 0, 80), pv("PD0", 0, 80)
         prs = [(T.ZK[:, (a + t) % 8, 15 - a:143 - a], T.gO[:, 80 * a:80 * a + 80]) for a in range(16)]
-        P = bank("PD1")
-        if part:
-            return mm(bank("PD0")[:, 0:80], prs, kZK + ["gO"], ["PD0"], True, False)
-        mm(P[:, 0:80], prs, kZK + ["gO"], ["PD1"])
-        cp(T.L1[:], P[:, 0:80], ["PD1"], ["L1"])
-        cp(T.L2[LO, :], P[HI, 0:80], ["PD1"], ["L2a"])
-        cp(T.L2[HI, :], P[LO, 0:80], ["PD1"], ["L2b"])
-        ts(T.em[:], P[:, 0:80], EC + 4.0, A.is_gt, 100.0, A.mult, ["PD1"], ["em"])
-    for name in ("AOi", "AWi"):
-        for b in range(2):
-            spread(name, rank, b, "s")
-
-    bits([("s8", 0, 7), ("hl", 3, 1), ("gp", 4, 7), ("G", 4, 3), ("i", 0, 15), ("s4", 0, 3), ("b2", 2, 1), ("b1", 1, 1), ("b0", 0, 1)], 3)
-    ma("co", "G", 160.0, "i")
-    ma("w", "hl", -79.0, 80.0)
-    ma("tz", "gp", 16.0, 15.0)
-    ma("sw", "sd", -128.0, 64.0)
-    tsc(T.xl[:], T.xI[:], "co", A.add, None, None, ["xI"], ["xl"])
-    tsc(T.ol[:], T.xI[:, 0::8], "co", A.add, None, None, ["xI"], ["ol"])
-    mk("tq", "tz", "s8", A.subtract)
-    mk("tzs", "tz", "sw", A.add)
-    tsc(T.DL[:, 0:8], T.ci[:, 0:8], "s8", A.is_equal, None, None, ["ci"], ["DL"])
-    mat(T.LQ[:], "LQ", "tq", "w", 136)
-    mat(T.Zs[:], "Zs", "tzs", "w", 144)
-    own_slots(0)
-    own_slots(1)
-    own_walls(0)
-    tsc(T.OT[:, EC:EC + 1], col["hl"], 8.0, A.mult, 128.0, A.add, [ckey["hl"]], ["OTe"])
-    ma("a0", "b0", -0.5, 1.0)
-    ma("a1", "b1", -0.75, 1.0)
-    ma("a2", "b2", -0.9375, 1.0)
-    ma("w1", "b2", "w", 0.0)
-    ma("t4", "gp", 16.0, "s4")
-    mk("a3", "a0", "a1", A.mult, "a2", A.mult)
-    for k in range(8):
-        ts(T.ZK[:, k, :], T.Zs[:], T.DL[:, k:k + 1], A.mult, None, None, ["Zs", "DL"], ["ZK%d" % k])
-    lists(0, T.old0, "old0")
-    tsc(T.fI[:], T.bI[:], "a3", A.mult, -0.5 + 2.0 ** -9, A.add, ["bI"], ["fI"])
-    mk("w0", "w", "w1", A.subtract)
-    mk("tn", "t4", 12.0, A.add)
-    ts(T.fI[:], T.fI[:], 1, A.bitwise_and, None, None, ["fI"], ["fI"])
-    ma("tm", "i", 1024.0, 0.0)
-    cp(T.F[:], T.fI[:], ["fI"], ["F"])
-    lists(1, T.old1, "old1")
-    for k in range(2):
-        mat(T.LM[:, k, :], "LM%d" % k, "tn", "w%d" % k, 140)
-    ma("de", "sg", 0.25, -0.25)
-
-    def sel(out, src, pat, cmp, val, b0, ch, r, w):
-        op("g", lambda e: e.affine_select(out, src, pat, cmp, val, b0, ch), r, w)
-
-    def block(name, cols, pat, b0, val):
-        ap = T[name][:, cols]
-        if cols.step:
-            sel(T[name][:], T.zz[:, 0:144], [[0, 144]], A.is_equal, 0.0, 0, 0, ["zz"], [name])
-        sel(ap, T.zz[:, 0:ap.shape[1]], pat, A.is_gt, val, b0, -1, ["zz"], [name])
-        sel(ap, ap, pat, A.is_ge, 0.0, b0 + 15, -1, [name], [name])
-    block("Z1", slice(15, 143, 16), [[16, 8]], 0, 1.0)
-    block("ZV", slice(15, 143, 16), [[16, 8]], 0, -PEN)
-    block("ZVs", slice(15, 143, 16), [[-64, 2], [16, 4]], 64, -PEN)
-    p8 = [[0, 10], [1, 8]]
-    sel(T.H2[:], T.zz[:, 0:80], p8, A.is_equal, 2.0, 0, 0, ["zz"], ["H2"])
-    sel(T.RR[:], T.zz[:, 0:80], p8, A.not_equal, -1e9, 0, 0, ["zz"], ["RR"])
-    for k in range(8):
-        sel(T.CS[:, k::8], T.zz[:, 0:10], [[0, 10]], A.not_equal, float(128 >> k), 0, 0, ["zz"], ["CS%d" % k])
-    kCS = ["CS%d" % k for k in range(8)]
-    block("HA", slice(0, 128), [[-64, 2], [16, 4], [0, 16]], 64, HUGE)
-    sel(T.rw4[:], T.zz[:], [[0, 160], [1, 4]], A.not_equal, -HUGE, 0, 0, ["zz"], ["rw4"])
-
-    def output_constants():
-        ma("a4", "G", 32.0, "s8")
-        ma("a5", "sd", 8.0, 16.0)
-        ma("wy", "hl", -159.0, 160.0)
-        ma("ci", "hl", 64.5, -64.5)
-        mk("ty", "a4", "a5", A.add)
-        mat(T.YM[:], "YM", "ty", "wy", 160)
-    for k in range(4):
-        pick(T.RO[:, k, :], "RO%d" % k, ([[64, 2], [0, 4], [1, 16]], 16 * k, 1.0))
-    ps, po, py = [[32, 2], [64, 2], [1, 32]], [[32, 2], [-64, 2], [1, 32]], [[16, 5], [-1000, 2], [1, 16]]
-    pick(T.Mh[:], "Mh", (ps, 0, 1.0 / 128), (po, 64, -1.0 / 128))
-    pick(T.Ms[:], "Ms", (ps, 0, 1.0 / 64))
-    pick(T.Mo[:], "Mo", (po, 64, -1.0 / 64))
-    pick(T.OA[:], "OA", (py, 1000, 1.0))
-    pick(T.OB[:], "OB", (py, 1064, -1.0))
-    pick(T.OH[:], "OH", (py, 1000, 0.5), (py, 1064, -0.5))
-
-    for j, r in enumerate(order("AOi")[1:]):
-        for b in range(2):
-            spread("AOi", r, b, "sv"[b] if j > 1 else "s")
-    replies(0)
-    ow = order("AWi")
-    for b in range(2):
-        spread("AWi", ow[1], b, "v")
-    reply_lists(0, 0)
-    for j, r in enumerate(ow[2:]):
-        for b in range(2):
-            spread("AWi", r, b, "sv"[b])
-        if j == 0:
-            reply_lists(0, 1)
+        for h in range(2):
+            cp(T.gO[:, 640 * h:640 * h + 640], T.OT[:].indirect(T["LQs%d" % b][:, 40 * h:40 * h + 40]), kOT + ["LQsa%d" % b, "LQsb%d" % b],
+               ["gO%d" % h], "sv", GA)
+        for h in range(2):
+            mm(P0, prs[8 * h:8 * h + 8], kZK + ["gO%d" % h], ["PD1"], h == 0, h == 1)
+        cp(T.L1[:], P0, ["PD1"], ["L1"])
+        nodes[-1]["more"] = M3
+        cp(T.L2[LO, :], P0[HI, :], ["PD1"], ["L2a"])
+        cp(T.L2[HI, :], P0[LO, :], ["PD1"], ["L2b"])
+        nodes[-1]["more"] = M3
+        cp(T.kk[:], P0, ["PD1"], ["kk"], "sv")
+        act(T.sE[:], T.kk[:], AF.Sign, EC + 4.0, -1.0, ["kk"], ["sE"])
+        mm(P4, [(T.Ip[:], T.kk[:])], ["Ip", "kk"], ["PD0"], True, False, 4)
+        mm(P4, [(T.IP[:], T.m3[:]), (T.IP[:], T.sE[:])], ["IP", "m3", "sE"], ["PD0"], False, False)
 
     def lz(name, a):
         return T[name][:, 15 - a:143 - a]
 
     def rnd(t):
         b = t % 2
-        W, OT = T.W[:], T.OT[:]
-        P2, P3, P4 = bank("PA0")[:, 0:80], bank("PA1")[:, 0:80], bank("PD0")[:, 0:80]
-        cp(T.u[:], W.indirect(T["LQn%d" % b][:]), kW + ["LQn%d" % b], ["u"], "s")
-        tt(T.cm1[:], W.indirect(T.L1[:]), T.x[:], A.is_gt, kW + ["L1", "x"], ["cm1"])
+        W, OT, x, kx = T.W[:], T.OT[:], T["x%d" % b][:], ["x%d0" % b, "x%d1" % b]
+        P4, PG = pv("PD0", 0, 80), pv("PB0", 0, 80)
+        for h in range(2):
+            cp(T.u[:, 640 * h:640 * h + 640], W.indirect(T["LQn%d" % b][:, 40 * h:40 * h + 40]), kW + ["LQn%d" % b], ["u%d" % h], "s", GA)
+        tt(T.cm1[:], W.indirect(T.L1[:]), x, A.is_gt, kW + ["L1"] + kx, ["cm1"], GA)
+        tt(T.cm2[:], W.indirect(T.L2[:]), x, A.is_lt, kW + ["L2a", "L2b"] + kx, ["cm2"], GA)
+        def signs(parts, kd, key):
+            for k, (o, i, lower) in enumerate(parts):
+                act(o, i, AF.Tanh, (-8.0, -TB)[lower], (-16.0, 16.0)[lower], kd, [key + str(k)])
+            return [key + str(k) for k in range(len(parts))]
         mm(P4, [(lz("ZV", a), T.cm1[:, a::16]) for a in range(16)], ["ZV", "cm1"], ["PD0"], False, False)
-        for q in range(2):
-            m, d, vv = 1 + (t + 3 * q) % 7, T["d%d" % q], T["V%d" % q]
-            hb = m.bit_length() - 1
-            f = m ^ (1 << hb)
-            kd = ["d%d_%d" % (q, k) for k in range(1 << hb)]
-            for k in range(1 << hb):
-                out = d[:] if hb == 0 else d[:, :, :, k] if hb == 1 else d[:, :, k >> 1, k & 1]
-                tt(out, T.u[:, (k ^ m)::2 << hb], T.u[:, k::2 << hb], A.subtract, ["u"], [kd[k]] + (["d%d" % q] if k == 0 else []))
-            if hb == 0:
-                up, dn = vv[:, :, :, :, 0], [(vv[:, :, :, :, 1], d[:])]
-            elif hb == 1:
-                up = vv[:, :, :, 0, :]
-                dn = [(vv[:, :, :, 1, :], d[:])] if f == 0 else [(vv[:, :, :, 1, 1 - k], d[:, :, :, k]) for k in range(2)]
+        m = 1 + t
+        for h in range(2):
+            d, vv, o = T.d0[:, 80 * h:80 * h + 80], T.V0[:, 80 * h:80 * h + 80], 640 * h
+            kd = ["d0%d%d" % (h, k) for k in range(2 if m > 1 else 1)]
+            for k in range(len(kd)):
+                tt(d[:, :, :, k] if m > 1 else d, T.u[:, o + (k ^ m):o + 640:2 * len(kd)], T.u[:, o + k:o + 640:2 * len(kd)], A.subtract,
+                   ["u%d" % h], [kd[k]])
+            parts = [(vv[:, :, :, 0, :] if m > 1 else vv[:, :, :, :, 0], d, 0)]
+            parts += [(vv[:, :, :, :, 1], d, 1)] if m == 1 else [(vv[:, :, :, 1, :], d, 1)] if m == 2 else \
+                [(vv[:, :, :, 1, 1 - k], d[:, :, :, k], 1) for k in range(2)]
+            kv = [signs(parts, kd, "V0%d" % h)]
+            nodes[-1]["more"] = M1
+            d, vv, pk = T.PC[:, h, 0:80], T.V1[:, 80 * h:80 * h + 80], "PC%d" % h
+            if h < ONPE:
+                mms([(d[:, :, k >> 1, k & 1], (T.Ip, T.In)[z][:], T.u[:, o + (k, k ^ (4 + t))[1 - z]:o + 640:8], z == 0, z == 1)
+                     for k in range(4) for z in range(2)], ["Ip", "In", "u%d" % h], [pk], 4)
             else:
-                up = vv[:, :, 0, :, :]
-                dn = [(vv[:, :, 1, :, :], d[:])] if f == 0 else \
-                    [(vv[:, :, 1, :, 1 - k], d[:, :, :, k]) if f == 1 else (vv[:, :, 1, 1 - k, :], d[:, :, k, :]) for k in range(2)]
-            kv = ["V%d_%d" % (q, k) for k in range(1 + len(dn))]
-            op("s", lambda e: e.activation(up, d[:], AF.Tanh, bias=-8.0, scale=-16.0), kd + ["d%d" % q], [kv[0], "V%d" % q])
-            for k, (o, i) in enumerate(dn):
-                op("s", lambda e: e.activation(o, i, AF.Tanh, bias=-TB, scale=16.0), kd + ["d%d" % q], [kv[1 + k]])
-            mm((P2, P3)[q], [(lz("Z1", a), vv[:, 10 * a:10 * a + 10, :, :, :]) for a in range(16)], ["Z1", "V%d" % q] + kv, ["PA%d" % q])
-        tt(T.cm2[:], W.indirect(T.L2[:]), T.x[:], A.is_lt, kW + ["L2a", "L2b", "x"], ["cm2"])
-        mm(P4, [(lz("ZVs", a), T.cm2[:, a::16]) for a in range(16)], ["ZVs", "cm2"], ["PD0"], False, True)
-        if t < 2:
-            own_walls(1 - t)
-        tt(T.a1[:], P2, T.em[:], A.subtract, ["PA0", "em"], ["a1"])
-        ts(T.th[:], T.a1[:], THR, A.is_lt, 100.0, A.mult, ["a1"], ["th"])
-        tt(T.y[:], P3, T.th[:], A.subtract, ["PA1", "th"], ["y"])
-        ts(T.gm[:], T.y[:], THR, A.is_lt, -PEN, A.mult, ["y"], ["gm"])
-        ts(T.gb[:], T.y[:], THR, A.is_lt, None, None, ["y"], ["gb"])
-        tt(T.gr[:], T.RR[:], T.gm[:], A.subtract, ["RR", "gm"], ["gr"])
-        tt(T.gk[:], T.gm[:], T.CS[:], A.add, ["gm"] + kCS, ["gk"])
-        tt(T.da[:], P4, T.gm[:], A.add, ["PD0", "gm"], ["da"])
-        tt(T.e0[:], P4, T.gr[:], A.is_lt, ["PD0", "gr"], ["e0"])
-        tt(T.e1[:], P4, T.gk[:], A.min, ["PD0", "gk"], ["e1"])
+                d, pk = T.d1[:, 80 * h:80 * h + 80], "d1%d" % h
+                for k in range(4):
+                    tt(d[:, :, k >> 1, k & 1], T.u[:, o + (k ^ (4 + t)):o + 640:8], T.u[:, o + k:o + 640:8], A.subtract, ["u%d" % h], [pk + str(k)])
+                lastw[pk], lastr[pk] = [lastw[pk + str(k)][0] for k in range(4)], []
+                for k in range(4):
+                    lastr[pk + str(k)] = lastr[pk]
+            parts = [(vv[:, :, 0, :, :], d, 0)]
+            parts += [(vv[:, :, 1, :, :], d, 1)] if t == 0 else [(vv[:, :, 1, :, 1 - k], d[:, :, :, k], 1) if t == 1 else
+                                                                  (vv[:, :, 1, 1 - k, :], d[:, :, k, :], 1) for k in range(2)]
+            kv.append(signs(parts, [pk], "V1%d" % h))
+            for q in range(2):
+                mm(pv("PA%d" % q, 0, 80), [(lz("Z1", a), T["V%d" % q][:, 10 * a:10 * a + 10, :, :, :]) for a in range(8 * h, 8 * h + 8)],
+                   ["Z1"] + kv[q], ["PA%d" % q], h == 0, h == 1)
+        for q in range(2):
+            act(T["s%d" % q][:], pv("PA%d" % q, 0, 80), AF.Sign, -THR, 1.0, ["PA%d" % q], ["s%d" % q])
+        mm(P4, [(lz("ZVs", a), T.cm2[:, a::16]) for a in range(16)], ["ZVs", "cm2"], ["PD0"], False, False)
+        ks = ["sE", "s0", "s1"]
+        mm(P4, [(T.IP[:], T[s][:]) for s in ks[1:]], ["IP"] + ks[1:], ["PD0"], False, True)
+        mm(PG, [(T.IP[:], T[s][:]) for s in ["m3"] + ks], ["IP", "m3"] + ks, ["PB0"])
+        act(T.gb[:], PG, AF.Sign, 0.0, -1.0, ["PB0"], ["gb"])
         scan(T.sc[:], T.H2[:], T.gb[:], A.mult, A.add, ["H2", "gb"], ["sc"])
-        scan(T.S1[:], T.e0[:], T.da[:], A.mult, A.max, ["e0", "da"], ["S1"])
+        tt(T.e0[:], P4, T.RR[:], A.is_lt, ["PD0", "RR"], ["e0"])
+        tt(T.e1[:], P4, T.CS[:], A.min, ["PD0"] + kCS, ["e1"])
+        scan(T.S1[:], T.e0[:], P4, A.mult, A.max, ["e0", "PD0"], ["S1"])
         scan(T.S2[:], T.e0[:], T.e1[:], A.mult, A.max, ["e0", "e1"], ["S2"])
         cp(T.cu[:], T.S1[:, 7::8], ["S1"], ["cu"])
         tt(T.cx[:], T.S2[:, 7::8], T.sc[:, 7::8], A.add, ["S2", "sc"], ["cx"])
         old, ko = (T["old%d" % t][:], "old%d" % t) if t < 2 else (T.AO0[:, rank], "AO0%d" % rank)
-        tt(T.dT[:], OT.indirect(T.cu[:]), old, A.subtract, kOT + ["cu", ko], ["dT"])
+        tt(T.dT[:], OT.indirect(T.cu[:]), old, A.subtract, kOT + ["cu", ko], ["dT"], GA)
         cp(T.iu[:], T.cx[:], ["cx"], ["iu"])
-        tt(T.mT[:], T.F[:].indirect(T.iu[:]), T.dT[:], A.mult, ["F", "iu", "dT"], ["mT"])
+        tt(T.mT[:], T.F[:].indirect(T.iu[:]), T.dT[:], A.mult, ["F", "iu", "dT"], ["mT"], GA)
         tn, kt = (T["AO%d" % t][:, rank], "AO%d%d" % (t, rank)) if t < 2 else (T.TN[:], "TN")
         tt(tn, T.mT[:], old, A.add, ["mT", ko], [kt])
-        PL, PH = bank("PB0"), bank("PB1")[:, 0:160]
-        mms([(PL[:, 40 * k:40 * k + 40], T.LM[:, k, 12 - 4 * j:140 - 4 * j], tn[:, j::4], j == 0, j == 3) for k in range(2) for j in range(4)],
-            ["LM0", "LM1", kt], ["PB0"])
         if t < 2:
             send("AO%d" % t)
+        PH = pv("PB1", 0, 160)
+        for z, (s, ks) in enumerate(((old, ko), (T.mT[:], "mT"))):
+            for k in range(2):
+                mm(pv("PA%d" % k, 0, 40), [(T.LM[:, k, 12 - 4 * j:140 - 4 * j], s[:, j::4]) for j in range(4)], ["LM%d" % k, ks], ["PA%d" % k],
+                   z == 0, z == 1)
+        cp(T.LN[:], T.PA[:, :, 0:40], ["PA0", "PA1"], ["LN"])
         ts(T.nd[:], tn, 127.5, A.is_lt, None, None, [kt], ["nd"])
-        cp(T.LN[:], PL[:, 0:80], ["PB0"], ["LN"])
-        mm(PH, [(T.HA[:], T.nd[:])], ["HA", "nd"], ["PB1"])
-        for k in range(2):
-            cp(T.w[:, 320 * k:320 * k + 320], W.indirect(T.LN[:, 20 * k:20 * k + 20]), kW + ["LN"], ["w%d" % k], "s")
-        if t < 2:
-            spread("AO%d" % t, rank, t, "s", "PA")
-        tt(T.y1[:], PH, T["XO%d" % b][:], A.add, ["PB1", "XO%d" % b], ["y1"])
-        tsc(T.q2[:], T.y1[:], "tm", A.min, "de", A.add, ["y1"], ["q2"])
+        mm(PH, [(T.Ip[:], T["XO%d" % b][:])], ["Ip", "XO%d" % b], ["PB1"], True, False, 4)
+        mm(PH, [(T.HA[:], T.nd[:])], ["HA", "nd"], ["PB1"], False, True)
+        act(T.q1[:], PH, AF.Relu, col["tm"], -1.0, ["PB1", ckey["tm"]], ["q1"])
+        nodes[-1]["more"] = M2
         for k in range(2):
             o = 320 * k
-            tt(T.t1[:, o:o + 320], W.indirect(T.LN[:, 40 + 20 * k:60 + 20 * k]), T.w[:, o:o + 320], A.max, kW + ["LN", "w%d" % k], ["t1%d" % k])
-            if k == 0:
-                tsc(T.q1[:], T.y1[:], "tm", A.min, None, None, ["y1"], ["q1"])
+            cp(T.w[:, o:o + 320], W.indirect(T.LN[:, 20 * k:20 * k + 20]), kW + ["LN"], ["w%d" % k], "s", GA)
+            tt(T.t1[:, o:o + 320], W.indirect(T.LN[:, 40 + 20 * k:60 + 20 * k]), T.w[:, o:o + 320], A.max, kW + ["LN", "w%d" % k], ["t1%d" % k], GA)
         scan(T.sw[:], T.rw4[:], T.t1[:], A.add, A.max, ["rw4", "t10", "t11"], ["sw"])
         return tn, kt
 
     def tile(t):
-        P1, P2, FF = bank("PD0")[:, 0:160], bank("PD1")[:, 0:160], bank("PD1")[:, 160:320]
-        mm(P2, [(T.Mh[:], T.q2[:])], ["Mh", "q2"], ["PD1"], True, False)
-        mm(P1, [(T.Ms[:], T.q1[:])], ["Ms", "q1"], ["PD0"], True, False)
-        mm(P2, [(T.Mh[:], T.sw[:, 3::4])], ["Mh", "sw"], ["PD1"], False, True)
-        mm(P1, [(T.Mo[:], T.sw[:, 3::4])], ["Mo", "sw"], ["PD0"], False, True)
+        P1, P2, FF = pv("PD0", 0, 160), pv("PD1", 0, 160), pv("PD1", 160, 160)
+        mm(P2, [(T.Mh[:], T.q2[:])], ["Mh", "q2"], ["PD1"], True, False, 4)
+        mm(P1, [(T.Ms[:], T.y1[:])], ["Ms", "y1"], ["PD0"], True, False, 4)
+        mm(P2, [(T.Mn[:], T.q1[:])], ["Mn", "q1"], ["PD1"], False, False, 4)
+        mm(P1, [(T.Ms[:], T.q1[:])], ["Ms", "q1"], ["PD0"], False, False, 4)
+        mm(P2, [(T.Mh[:], T.sw[:, 3::4])], ["Mh", "sw"], ["PD1"], False, True, 4)
+        mm(P1, [(T.Mo[:], T.sw[:, 3::4])], ["Mo", "sw"], ["PD0", "tile"], False, True, 4)
         ts(T.r1[:], P2, MG / 64, A.add, MG / 64, A.subtract, ["PD1"], ["r1"])
         tt(FF, P1, T.r1[:], A.min, ["PD0", "r1"], ["PD1"])
-        Z, kz = T["AW%d" % t], "AW%d%d" % (t, rank)
-        cp(Z[LO, rank, 0, :], FF[LO, :], ["PD1"], ["z0"])
-        cp(Z[HI, rank, 1, :], FF[HI, :], ["PD1"], ["z1"])
+        Z = T["AW%d" % t]
+        tt(Z[LO, rank, 0, :], P1[LO, :], T.r1[LO, :], A.min, ["PD0", "r1"], ["z0"])
+        tt(Z[HI, rank, 1, :], P1[HI, :], T.r1[HI, :], A.min, ["PD0", "r1"], ["z1"])
         tt(Z[HI, rank, 0, :], FF[LO, :], Z[LO, rank, 0, :], A.subtract, ["PD1", "z0"], ["z2"])
-        tt(Z[LO, rank, 1, :], FF[HI, :], Z[HI, rank, 1, :], A.subtract, ["PD1", "z1"], [kz])
+        tt(Z[LO, rank, 1, :], FF[HI, :], Z[HI, rank, 1, :], A.subtract, ["PD1", "z1"], ["z3"])
+        lastw["AW%d%d" % (t, rank)] = [j for k in kz for j in lastw[k]]
+        send("AW%d" % t)
 
-    def put_slots(b, tn, kt):
-        P = bank("PD0")[:, 0:80]
-        tsc(T.ind[:], tn, 63.5, A.is_gt, "ci", A.mult, [kt], ["ind"])
-        mm(P, [(T.YM[:, 16 - 16 * k:144 - 16 * k], s[:, 80 * k:80 * k + 80]) for k in range(2) for s in (tn, T.ind)], ["YM", kt, "ind"], ["PD0"])
-        cp(T.Yo[:, 80 * b:80 * b + 80], P, ["PD0"], ["Yo%d" % b], "s", -48.0)
-        dma([("y", T.yo[:, 80 * b:80 * b + 80], T.Yo[:, 80 * b:80 * b + 80])], ["Yo%d" % b], [])
+    def put(y, o, b, q="y"):
+        dma(q, [(o[:, 80 * b:80 * b + 80], T[y][:, 80 * b:80 * b + 80])], [y + str(b)], [])
+
+    def put_slots(b, tn, kt, pk):
+        tsc(T.ind[:], tn, 63.5, A.is_gt, "wi", A.mult, [kt], ["ind"])
+        mm(pv(pk, 0, 80), [(T.YM[:, 16 - 16 * k:144 - 16 * k], s[:, 80 * k:80 * k + 80]) for k in range(2) for s in (tn, T.ind)],
+           ["YM", kt, "ind"], [pk])
+        act(T.Yo[:, 80 * b:80 * b + 80], pv(pk, 0, 80), AF.Identity, -48.0, 1.0, [pk], ["Yo%d" % b])
+        put("Yo", T.yo, b)
+
+    def put_old_walls(b):
+        win, k = own("W", b)
+        cp(T.XY[:], win.indirect(T.ol[:]), [k, "ol"], ["XY"], "sv", GA)
+        for pk, m, y, o in (("PB0", "OA", "Yr", T.yr), ("PB1", "OB", "Yl", T.yl)):
+            mm(pv(pk, 0, 80), [(T[m][:, 16 - 16 * k:144 - 16 * k], T.XY[:, 80 * k:80 * k + 80]) for k in range(2)], [m, "XY"], [pk], True, True, 4)
+            cp(T[y][:, 80 * b:80 * b + 80], pv(pk, 0, 80), [pk], [y + str(b)], "sv")
+            put(y, o, b)
 
     def put_walls(b):
-        jobs = (("PA0", "OH", "q2", "OH"), ("PA1", "OA", "q1", "OB"), ("PD1", "OB", "q1", "OA"))
-        for z in range(2):
-            for pk, mq, q, ms in jobs:
-                mm(bank(pk)[:, 0:80], [(T[(mq, ms)[z]][:, 16 - 16 * k:144 - 16 * k],
-                                        T.sw[:, 3 + 320 * k:320 * k + 320:4] if z else T[q][:, 80 * k:80 * k + 80]) for k in range(2)],
-                   [mq, ms, "sw" if z else q], [pk], z == 0, z == 1)
-        ts(T.mid[:], bank("PA0")[:, 0:80], MG, A.add, MG, A.subtract, ["PA0"], ["mid"])
-        for q, pk, y, o, f in (("y", "PA1", "Yr", T.yr, A.min), ("s", "PD1", "Yl", T.yl, A.max)):
-            tt(T[y][:, 80 * b:80 * b + 80], bank(pk)[:, 0:80], T.mid[:], f, [pk, "mid"], [y + str(b)])
-            dma([(q if b == 0 else "y", o[:, 80 * b:80 * b + 80], T[y][:, 80 * b:80 * b + 80])], [y + str(b)], [])
+        jobs = (("PC0", ("OH", "NH", "OH"), "q2"), ("PC1", ("NA", "NA", "OB"), "y1"), ("PD1", ("NB", "NB", "OA"), "y1"))
+        for z in range(3):
+            for pk, ms, c in jobs:
+                s = (c, "q1", "sw")[z]
+                mm(pv(pk, 0, 80), [(T[ms[z]][:, 16 - 16 * k:144 - 16 * k],
+                                    T.sw[:, 3 + 320 * k:320 * k + 320:4] if z == 2 else T[s][:, 80 * k:80 * k + 80]) for k in range(2)],
+                   [ms[z], s], [pk], z == 0, z == 2, 4)
+        ts(T.mid[:], pv("PC0", 0, 80), MG, A.add, MG, A.subtract, ["PC0"], ["mid"])
+        for q, pk, y, o, f in (("y", "PC1", "Yr", T.yr, A.min), ("s", "PD1", "Yl", T.yl, A.max)):
+            tt(T[y][:, 80 * b:80 * b + 80], pv(pk, 0, 80), T.mid[:], f, [pk, "mid"], [y + str(b)])
+            put(y, o, b, q)
 
-    for t in range(2):
+    for name in ("AOi", "AWi"):
+        for b in range(2):
+            spread(name, rank, b)
+        share(name, rank)
+    for b in range(2):
+        own_slots(b)
+        own_walls(b)
+        lists(b, T["old%d" % b], "old%d" % b, "PD%d" % b)
+    for name in ("AOi", "AWi"):
+        for r in coming(name)[1:]:
+            for b in range(2):
+                spread(name, r, b)
+            share(name, r)
+    for t in range(3):
+        replies(t)
+        if t == 2:
+            put_old_walls(1)
         tn, kt = rnd(t)
-        hand_on("AO%d" % t)
+        if t == 2:
+            put_slots(0, tn, kt, "PD0")
+            put_walls(0)
+            break
+        turn[0] = 0
         tile(t)
-        send("AW%d" % t)
-        hand_on("AW%d" % t)
-        for j, r in enumerate(order("AO%d" % t)[1:]):
-            spread("AO%d" % t, r, t, "sssvsvv"[j])
-        replies(t + 1)
-        ow = order("AW%d" % t)
-        spread("AW%d" % t, rank, t, "v")
+        for j, r in enumerate(coming("AO%d" % t)):
+            if j == GATE:
+                gate.update({"t": lastw["tile"][0], "v": lastw["z3"][0]})
+            spread("AO%d" % t, r, t)
+        gate.clear()
         if t == 0:
-            lists(0, tn, kt)
-            output_constants()
+            lists(0, tn, kt, "PD1")
         else:
-            put_slots(1, tn, kt)
-            put_walls(1)
-        spread("AW%d" % t, ow[1], t, "v")
-        reply_lists(t + 1, 0)
-        for j, r in enumerate(ow[2:]):
-            spread("AW%d" % t, r, t, "svsvsv"[j])
-            if j == 1:
-                reply_lists(t + 1, 1)
-    tn, kt = rnd(2)
-    put_slots(0, tn, kt)
-    put_walls(0)
-    for s in tot:
-        if waited["g"].get(s, 0) < tot[s]:
-            g.wait_ge(T.sem[s], tot[s])
+            put_slots(1, tn, kt, "PD0")
+        for r in coming("AW%d" % t):
+            spread("AW%d" % t, r, t)
+        if t == 0:
+            own_walls(0)
+    issue()

@@ -20,7 +20,7 @@ SCRATCH = {
     "PC": ("psum", [128, 2, 128, 2, 2], FI),
 }
 for _n, _w, _t in (("u x0 x1", 1280, FI), ("gO cm1 cm2", 1280, FB), ("w t1 sw", 640, FI), ("rw4 zz", 640, FB),
-                   ("O32 X32 qi yi hI lI", 320, II), ("ta tb", 320, FI), ("bI", 256, FI), ("fI", 256, II), ("F", 256, FB),
+                   ("O32 X32 qi yi", 320, II), ("tb", 320, FI), ("bI", 256, FI), ("fI", 256, II), ("F", 256, FB),
                    ("ci OA OB OH NA NB NH XO0 XO1 XY y1 q1 q2 r1 Yl Yr Yo", 160, FI), ("old0 old1 dT mT nd ind YM", 160, FB),
                    ("Zs Z1 ZV ZVs", 144, FB), ("LQ", 136, FB), ("kI HA IP", 128, FB), ("Ms Mo Mh Mn Ip In", 128, FI),
                    ("LQn0 LQn1 LQs0 LQs1 L1 L2 LN xl", 80, UU), ("xI", 80, II), ("sE s0 s1 m3", 80, FB),
@@ -36,11 +36,16 @@ CY, GA, PE, FX, WAKE, DMA, BYTE = 0.00083, 0.00125, 0.0006, 0.06, 0.06, 2.0, 1.0
 CALL, H0, H1, H2 = 0.5, 3.0, 2.0, 2.0
 HOP = {"Oi": H0, "Wi": H0, "O0": H1, "O1": H1, "W0": H2, "W1": H2}
 HANDED = ()
-SHARED = {"AOi": 4, "AWi": 1}
+SHARED = {"AOi": (0, 1, 2, 3), "AWi": (0,), "AO0": (1, 2), "AO1": (1, 2)}
+HS = 2.5
+M4, M5 = 3.0, 0.5
+SPLIT = 1
+M6 = 4.0
 M3 = 3.0
 GATE = 1
+PASSES = 4
 ONPE = 1
-M1, M2 = 1.5, 0.5
+M1, M2 = 1.0, 0.5
 
 
 def rank_program(g, core, T, topo):
@@ -138,23 +143,48 @@ def rank_program(g, core, T, topo):
             rk[k] += x["cost"] + x["lag"] + x.get("more", 0.0)
             for j in x["hard"] | x["soft"] | set(x["after"].values()):
                 rk[j] = max(rk[j], rk[k] + WAKE)
-        busy = {q: [] for q in "vtsgyxz"}
-        for k in sorted(range(len(nodes)), key=lambda k: -rk[k]):
-            x, best = nodes[k], None
-            for q in x["qs"]:
-                t = max([0.0] + [nodes[j]["end"] + (0.0 if nodes[j]["q"] == q == "t" else WAKE) for j in x["hard"]]
-                        + [nodes[j]["end"] + (0.0 if nodes[j]["q"] == q else WAKE) for j in x["soft"]])
-                if q in x["after"]:
-                    t = max(t, nodes[x["after"][q]]["end"])
-                for a, z in busy[q]:
-                    if t + x["cost"] <= a:
-                        break
-                    t = max(t, z)
-                if best is None or t < best[0]:
-                    best = (t, q)
-            x["at"], x["q"] = best
-            x["end"] = x["at"] + x["cost"] + x["lag"]
-            busy[x["q"]] = sorted(busy[x["q"]] + [(x["at"], x["at"] + x["cost"])])
+
+        def gap(busy, t, c):
+            for a, z in busy:
+                if t + c <= a:
+                    break
+                t = max(t, z)
+            return t
+
+        def wake(j, k, q):
+            return 0.0 if nodes[j]["q"] == q and (q == "t" or j not in nodes[k]["hard"]) else WAKE
+
+        def forward():
+            busy = {q: [] for q in "vtsgyxz"}
+            for k in sorted(range(len(nodes)), key=lambda k: -rk[k]):
+                x, best = nodes[k], None
+                for q in x["qs"]:
+                    t = max([0.0] + [nodes[j]["end"] + wake(j, k, q) for j in x["hard"] | x["soft"]])
+                    if q in x["after"]:
+                        t = max(t, nodes[x["after"][q]]["end"])
+                    t = gap(busy[q], t, x["cost"])
+                    if best is None or t < best[0]:
+                        best = (t, q)
+                x["at"], x["q"] = best
+                x["end"] = x["at"] + x["cost"] + x["lag"]
+                busy[x["q"]] = sorted(busy[x["q"]] + [(x["at"], x["at"] + x["cost"])])
+            return max(x["end"] for x in nodes)
+
+        def backward():
+            busy, t = {q: [] for q in "vtsgyxz"}, [0.0] * len(nodes)
+            for k in sorted(range(len(nodes)), key=lambda k: (-nodes[k]["end"], -k)):
+                x = nodes[k]
+                a = gap(busy[x["q"]], t[k] + x["lag"] + x.get("more", 0.0), x["cost"])
+                rk[k] = a + x["cost"]
+                busy[x["q"]] = sorted(busy[x["q"]] + [(a, rk[k])])
+                for j in x["hard"] | x["soft"] | {x["after"][q] for q in x["after"] if q in x["qs"]}:
+                    t[j] = max(t[j], rk[k] + wake(j, k, x["q"]) + 1e-6)
+        tried = []
+        for _ in range(PASSES):
+            tried.append((forward(), list(rk)))
+            backward()
+        rk[:] = min(tried)[1]
+        forward()
         line = sorted(nodes, key=lambda x: x["at"])
         tot, waited = {}, {q: {} for q in QU}
         for x in line:
@@ -208,41 +238,48 @@ def rank_program(g, core, T, topo):
         sent = "sent%d" % len(nodes)
         node("g", lambda e, _: e.remote_dma_fused(trs, local_sem=T.sem.ls), cost, ["%s%d" % (name, r) for r, _, _ in parts], [sent],
              0.0, ("ls", sum(len(es) for _, _, es in parts)))
+        nodes[-1]["more"] = M4
         for c, es in come:
             k = "%s%d" % (name, T.rank_of(c))
-            node("x" if es is offe else "z", None, 256 * size(T[name][:, 0]) * BYTE, [sent], [k], HOP[name[1:]], (k, len(es)))
+            node("x" if es[0] in offe else "z", None, 256 * size(T[name][:, 0]) * BYTE, [sent], [k], HOP[name[1:]], (k, len(es)))
 
     def theirs(name):
-        return ([others[0]] + cross)[:SHARED.get(name, 0)]
+        return [([others[0]] + cross)[k] for k in SHARED.get(name, ())]
 
     def send(name):
         far = same if name in HANDED else [c for c in others[1:] if c not in theirs(name)]
-        near = [] if theirs(name) else others[:1]
-        write(name, [(rank, near, one)] * len(near) + [(rank, far, offe)], 2.5 if name == TILES[0] else CALL,
-              [(c, one) for c in near] + [(c, offe) for c in far])
+        near = [c for c in others[:1] if c not in theirs(name)]
+        if len(far) == 6 and SPLIT:
+            ways = [(far[0::2], offe[:len(offe) // 2]), (far[1::2], offe[len(offe) // 2:])]
+        else:
+            ways = [(far, offe)]
+        write(name, [(rank, near, one)] * len(near) + [(rank, cs, es) for cs, es in ways], 2.5 if name == TILES[0] else CALL,
+              [(c, one) for c in near] + [(c, es) for c in far for cs, es in ways if c in cs])
         for call in hand if name in HANDED else ():
             write(name, [(T.rank_of(same[k]), others[:1], es) for k, es in call], CALL, [(cross[k], es) for k, es in call])
 
     def coming(name):
-        return [T.rank_of(c) for c in [core, others[0]] + same + cross] if name in HANDED else \
-            [r for r in order if T.cores[r] not in theirs(name)]
+        return [r for r in ([T.rank_of(c) for c in [core, others[0]] + same + cross] if name in HANDED else order)
+                if T.cores[r] not in theirs(name)]
 
     def base(b, r):
         return 128 + 5120 * (1 - b) + 640 * r
 
     def share(name, r):
-        mine = [T.rank_of(c) for c in [core] + same][:SHARED.get(name, 0)]
+        mine = [T.rank_of(([core] + same)[k]) for k in SHARED.get(name, ())]
         if r in mine:
             im, o = "OT" if name[1] == "O" else "W", T.rank_of(theirs(name)[mine.index(r)])
             rid, pid = topo.addr(others[0], core)
-            trs = [RemoteDMATransfer(dst_ids=[DstId(rid=rid, pnc=pid)], dma_engine_mask=sum(1 << e for e in hand[0][b][1]),
+            first = name in TILES[:2]
+            bs = ((0, hand[0][0][1]), (1, hand[0][1][1])) if first else ((int(name[2]), one),)
+            trs = [RemoteDMATransfer(dst_ids=[DstId(rid=rid, pnc=pid)], dma_engine_mask=sum(1 << e for e in es),
                                      remote_sem=T.sem["%s%d" % (name, r)], srcs=[T[im][:, base(b, r):base(b, r) + 640]],
-                                     dsts=[T[im][:, base(b, r):base(b, r) + 640]], alu_op=0) for b in range(2)]
+                                     dsts=[T[im][:, base(b, r):base(b, r) + 640]], alu_op=0) for b, es in bs]
             sent = "sent%d" % len(nodes)
-            left = "l%s%d" % (im, mine.index(r))
-            node("g", lambda e, _: e.remote_dma_fused(trs, local_sem=T.sem[left]), CALL, ["%s%d%d" % (im, b, r) for b in range(2)], [sent],
-                 0.0, (left, len(one)))
-            node("z", None, 128 * 1280 * (2 if im == "OT" else 4) * BYTE, [sent], ["%s%d%d" % (im, b, o) for b in range(2)], 2.0,
+            left = "l%s%d" % (im, mine.index(r)) if first else "ls"
+            node("g", lambda e, _: e.remote_dma_fused(trs, local_sem=T.sem[left]), CALL,
+                 ["%s%d%d" % (im, b, r) for b, _ in bs] + ([] if first else ["%s%d" % (name, order[1])]), [sent], 0.0, (left, len(one)))
+            node("z", None, 128 * 640 * len(bs) * (2 if im == "OT" else 4) * BYTE / 2, [sent], ["%s%d%d" % (im, b, o) for b, _ in bs], HS,
                  ("%s%d" % (name, o), len(one)))
 
     for u in range(2):
@@ -277,7 +314,7 @@ def rank_program(g, core, T, topo):
         tsc(ap, T.ci[:, 0:width], t, A.is_equal, wgt, A.mult, ["ci"], [key])
     bits([("sd", 6, 1), ("s5", 5, 1)], 1)
     for n, s, m, a in (("yc", "sd", 79.5, -79.5), ("ys", "sd", 1 - 1.0 / 160, 1.0 / 160), ("al", "sd", -16.0, -64.0),
-                       ("ga", "sd", 64.0, 64.0), ("be", "sd", -128.0, 129.0), ("sH", "s5", -64.0, 32.0), ("sL", "s5", -1.0 / 32, 1.0 / 64)):
+                       ("ga", "sd", 64.0, 64.0), ("be", "sd", -128.0, 129.0), ("sL", "s5", -1.0 / 32, 1.0 / 64)):
         ma(n, s, m, a)
     act(T.CB[:, 0:1], col["sd"], AF.Tanh, -16.0, 32.0, [ckey["sd"]], ["CB"], 1.4)
     col["sg"], ckey["sg"] = T.CB[:, 0:1], "CB"
@@ -350,14 +387,15 @@ def rank_program(g, core, T, topo):
 
     ts(T.qi[:], T.O32[:], -39.5, A.add, 1.0 / 80, A.mult, kO, ["qi"])
     tsc(T.yi[:], T.O32[:], "yc", A.add, "ys", A.mult, kO, ["yi"])
-    tsc(T.ta[:], T.qi[:], "al", A.mult, "ga", A.add, ["qi"], ["ta"])
+    tsc(pv("PD0", 0, 320), T.qi[:], "al", A.mult, "ga", A.add, ["qi"], ["PD0"])
     tsc(T.tb[:], T.yi[:], "be", A.mult, None, None, ["yi"], ["tb"])
-    tt(T.AOi[:, rank], T.ta[:], T.tb[:], A.add, ["ta", "tb"], ["AOi%d" % rank])
+    tt(T.AOi[:, rank], pv("PD0", 0, 320), T.tb[:], A.add, ["PD0", "tb"], ["AOi%d" % rank])
     send("AOi")
-    ts(T.hI[:], T.X32[:], 11, A.arith_shift_right, None, None, kX, ["hI"])
-    ts(T.lI[:], T.X32[:], 2047, A.bitwise_and, None, None, kX, ["lI"])
-    for k, (p_o, u, src, p_i, s) in enumerate(((LO, 0, "hI", LO, "sH"), (HI, 1, "hI", HI, "sH"), (HI, 0, "lI", LO, "sL"), (LO, 1, "lI", HI, "sL"))):
-        tsc(T.AWi[p_o, rank, u, :], T[src][p_i, :], s, A.mult, None, None, [src], ["z%d" % k], p_i)
+    FF = pv("PD1", 0, 320)
+    tsc(FF, T.X32[:], "sL", A.mult, None, None, kX, ["PD1"])
+    for u, (p, o) in enumerate(((LO, HI), (HI, LO))):
+        tsc(T.AWi[p, rank, u, :], T.X32[p, :], "sL", A.mult, None, None, kX, ["z%d" % u], p)
+        tt(T.AWi[o, rank, u, :], FF[p, :], T.AWi[p, rank, u, :], A.subtract, ["PD1", "z%d" % u], ["z%d" % (2 + u)])
     kz = ["z%d" % k for k in range(4)]
     lastw["AWi%d" % rank] = [j for k in kz for j in lastw[k]]
     send("AWi")
@@ -396,10 +434,11 @@ def rank_program(g, core, T, topo):
         win, k = own("OT", b)
         cp(T["old%d" % b][:], win.indirect(T.ol[:]), [k, "ol"], ["old%d" % b], "sv", GA)
 
-    def own_walls(b):
+    def own_walls(b, more=0.0):
         win, k = own("W", b)
         for h in range(2):
             cp(T["x%d" % b][:, 640 * h:640 * h + 640], win.indirect(T.xl[:, 40 * h:40 * h + 40]), [k, "xl"], ["x%d%d" % (b, h)], "sv", GA)
+            nodes[-1]["more"] = more
         act(T["XO%d" % b][:], win.indirect(T.ol[:]), AF.Identity, -BIG, 1.0, [k, "ol"], ["XO%d" % b], GA)
 
     def lists(b, src, ks, pk):
@@ -472,11 +511,13 @@ def rank_program(g, core, T, topo):
             parts += [(vv[:, :, 1, :, :], d, 1)] if t == 0 else [(vv[:, :, 1, :, 1 - k], d[:, :, :, k], 1) if t == 1 else
                                                                   (vv[:, :, 1, 1 - k, :], d[:, :, k, :], 1) for k in range(2)]
             kv.append(signs(parts, [pk], "V1%d" % h))
+            nodes[-1]["more"] = M1
             for q in range(2):
                 mm(pv("PA%d" % q, 0, 80), [(lz("Z1", a), T["V%d" % q][:, 10 * a:10 * a + 10, :, :, :]) for a in range(8 * h, 8 * h + 8)],
                    ["Z1"] + kv[q], ["PA%d" % q], h == 0, h == 1)
         for q in range(2):
             act(T["s%d" % q][:], pv("PA%d" % q, 0, 80), AF.Sign, -THR, 1.0, ["PA%d" % q], ["s%d" % q])
+            nodes[-1]["more"] = M5
         mm(P4, [(lz("ZVs", a), T.cm2[:, a::16]) for a in range(16)], ["ZVs", "cm2"], ["PD0"], False, False)
         ks = ["sE", "s0", "s1"]
         mm(P4, [(T.IP[:], T[s][:]) for s in ks[1:]], ["IP"] + ks[1:], ["PD0"], False, True)
@@ -570,7 +611,7 @@ def rank_program(g, core, T, topo):
         share(name, rank)
     for b in range(2):
         own_slots(b)
-        own_walls(b)
+        own_walls(b, (M6, 0.0)[b])
         lists(b, T["old%d" % b], "old%d" % b, "PD%d" % b)
     for name in ("AOi", "AWi"):
         for r in coming(name)[1:]:
@@ -592,6 +633,7 @@ def rank_program(g, core, T, topo):
             if j == GATE:
                 gate.update({"t": lastw["tile"][0], "v": lastw["z3"][0]})
             spread("AO%d" % t, r, t)
+            share("AO%d" % t, r)
         gate.clear()
         if t == 0:
             lists(0, tn, kt, "PD1")
@@ -599,6 +641,7 @@ def rank_program(g, core, T, topo):
             put_slots(1, tn, kt, "PD0")
         for r in coming("AW%d" % t):
             spread("AW%d" % t, r, t)
+            share("AW%d" % t, r)
         if t == 0:
             own_walls(0)
     issue()

from concourse.bass import DstId, RemoteDMATransfer
from concourse.mybir import AluOpType as A, ActivationFunctionType as AF

N = 8
EC, WD = 10368, 10384
BIG, HUGE, PEN = 2097152.0, 8388608.0, 262144.0
MG = 12582912.0
THR, TB = -15.03, 1.71699
FI, FB, FH, II, UU = "float32", "bfloat16", "float16", "int32", "uint16"
SCRATCH = {
    "W": ("sbuf", [128, WD], FI), "OT": ("sbuf", [128, WD], FB),
    "AOi": ("sbuf", [128, N, 2, 160], FB), "AWi": ("sbuf", [128, N, 2, 320], FH),
    "AO0": ("sbuf", [128, N, 160], FB), "AO1": ("sbuf", [128, N, 160], FB), "TN": ("sbuf", [128, 160], FB),
    "AW0": ("sbuf", [128, N, 2, 160], FH), "AW1": ("sbuf", [128, N, 2, 160], FH),
    "d0": ("sbuf", [128, 160, 2, 2], FB), "d1": ("sbuf", [128, 160, 2, 2], FB),
    "V0": ("sbuf", [128, 160, 2, 2, 2], FB), "V1": ("sbuf", [128, 160, 2, 2, 2], FB),
    "CI": ("sbuf", [128, 12], II), "CF": ("sbuf", [128, 12], FI), "CC": ("sbuf", [128, 48], FI), "CB": ("sbuf", [128, 2], FB),
    "ZK": ("sbuf", [128, 8, 144], FB), "RW": ("sbuf", [128, 2, 128], FB), "RI": ("sbuf", [128, 4, 128], FB),
    "RO": ("sbuf", [128, 4, 128], FB), "LM": ("sbuf", [128, 2, 140], FB),
    "PC": ("psum", [128, 2, 128, 2, 2], FI),
}
for _n, _w, _t in (("u x0 x1", 1280, FI), ("gO cm1 cm2", 1280, FB), ("w t1 sw", 640, FI), ("rw4 zz", 640, FB),
                   ("O32 X32 qi yi", 320, II), ("tb", 320, FI), ("bI", 256, FI), ("fI", 256, II), ("F", 256, FB),
                   ("ci OA OB OH NA NB NH XO0 XO1 XY y1 q1 q2 r1 Yl Yr Yo", 160, FI), ("old0 old1 dT mT nd ind YM", 160, FB),
                   ("Zs Z1 ZV ZVs", 144, FB), ("LQ", 136, FB), ("kI HA IP", 128, FB), ("Ms Mo Mh Mn Ip In", 128, FI),
                   ("LQn0 LQn1 LQs0 LQs1 L1 L2 LN xl", 80, UU), ("xI", 80, II), ("sE s0 s1 m3", 80, FB),
                   ("kk gb sc e0 e1 S1 S2 H2 CS RR mid", 80, FI), ("cx DL", 10, FI), ("cu iu ol", 10, UU)):
    for _k in _n.split():
        SCRATCH[_k] = ("sbuf", [128, _w], _t)
for _k in "ABD":
    SCRATCH["P" + _k] = ("psum", [128, 2, 512], FI)
TILES = ("AOi", "AWi", "AO0", "AW0", "AO1", "AW1")
SEMAPHORES = ["qv", "qt", "qs", "qg", "ls"] + ["%s%d" % (a, r) for a in TILES for r in range(N)] + ["dm%d" % k for k in range(12)] \
    + ["l%s%d" % (a, k) for a in ("OT", "W") for k in range(4)]
CY, GA, PE, FX, WAKE, DMA, BYTE = 0.00083, 0.00125, 0.0006, 0.06, 0.06, 2.0, 1.0 / 200000
CALL, H0, H1, H2 = 0.5, 3.0, 2.0, 2.0
HOP = {"Oi": H0, "Wi": H0, "O0": H1, "O1": H1, "W0": H2, "W1": H2}
HANDED = ()
SHARED = {"AOi": (0, 1, 2, 3), "AWi": (0,), "AO0": (1, 2), "AO1": (1, 2)}
HS = 2.5
M4, M5 = 3.0, 0.5
SPLIT = 1
M6 = 4.0
M3 = 3.0
GATE = 1
PASSES = 4
ONPE = 1
M1, M2 = 1.0, 0.5


def rank_program(g, core, T, topo):
    rank = T.rank_of(core)
    if rank is None:
        return
    QU = {"v": g.vector, "t": g.tensor, "s": g.scalar, "g": g, "y": g.sync}
    nodes, lastw, lastr = [], {}, {}
    gate = {}

    def node(qs, fn, cost, r=(), w=(), lag=0.0, sem=None):
        k = len(nodes)
        hard = {j for x in r for j in lastw.get(x, [])} | {j for x in w for j in lastw.get(x, []) + lastr.get(x, [])}
        soft = {j for x in r if x[0] == "P" for j in lastr.get(x, [])} - hard
        nodes.append({"qs": qs, "fn": fn, "cost": cost, "hard": hard, "soft": soft, "lag": lag, "sem": sem, "after": dict(gate)})
        for x in r:
            lastr.setdefault(x, []).append(k)
        for x in w:
            lastw[x], lastr[x] = [k], []

    def size(ap):
        n = 1
        for s in ap.shape[1:]:
            n *= s
        return n

    def op(qs, fn, out, c, r, w):
        node(qs, fn, FX + max(64 * CY, size(out) * c), r, w)

    def dma(q, parts, r=(), w=()):
        s = "dm%d" % len([x for x in nodes if x["sem"] and x["sem"][0][:2] == "dm"])

        def fn(e, _):
            for o, i in parts:
                e.dma_start(o, i).then_inc(T.sem[s], 16)
        node(q, fn, 0.05 * len(parts), r, w, DMA, (s, 16 * len(parts)))

    def mms(lst, r, w, c=1):
        def fn(e, _):
            for o, l, x, a, z in lst:
                ins = e.matmul(o, l, x, a, z)
            return ins
        node("t", fn, sum(max(64, size(x[2])) for x in lst) * c * PE, r, w)

    def mm(out, pairs, r, w, first=True, last=True, c=1):
        mms([(out, l, x, first and k == 0, last and k == len(pairs) - 1) for k, (l, x) in enumerate(pairs)], r, w, c)

    def ts(out, i, s1, o1, s2=None, o2=None, r=(), w=()):
        if o2 is None:
            op("v", lambda e, _: e.tensor_scalar(out, i, s1, None, o1), out, CY, r, w)
        else:
            op("v", lambda e, _: e.tensor_scalar(out, i, s1, s2, o1, o2), out, CY, r, w)

    def tt(out, a, b, o, r, w, c=None):
        op("v", lambda e, _: e.tensor_tensor(out, a, b, o), out, c or (CY if [x for x in r if x[0] == "P"] else 2 * CY), r, w)

    def cp(out, i, r, w, qs="v", c=CY):
        op(qs, lambda e, q: e.tensor_copy(out, i) if q == "v" else e.activation(out, i, AF.Identity), out, c, r, w)

    def act(out, i, f, bias, scale, r, w, c=CY):
        op("s", lambda e, _: e.activation(out, i, f, bias=bias, scale=scale), out, c, r, w)

    def scan(out, a, b, o0, o1, r, w):
        op("v", lambda e, _: e.tensor_tensor_scan(out, a, b, 0.0, o0, o1), out, CY, r, w)

    def fill(ap, c, key):
        op("v", lambda e, _: e.memset(ap, c), ap, CY / 2, [], [key])

    def iota(ap, key, pat, base=0, ch=0, whole=False):
        if whole:
            node("g", lambda e, _: e.iota(ap, pat, base, ch), 0.13 + 2 * CY * size(ap), [], [key])
        else:
            node("g", lambda e, _: e.iota(ap, pat, base, ch, allow_small_or_imprecise_dtypes=True), 0.13 + 2 * CY * size(ap), [], [key])

    def sel(out, src, pat, cmp, val, b0, ch, r, w):
        node("g", lambda e, _: e.affine_select(out, src, pat, cmp, val, b0, ch), 0.17 + 2 * CY * size(out), r, w)

    def pick(ap, key, *terms):
        src, ks = T.zz[:, 0:ap.shape[1]], "zz"
        for pat, b0, val in terms:
            sel(ap, src, pat, A.not_equal, val, b0, -1, [ks], [key])
            src, ks = ap, key

    def block(name, cols, pat, b0, val):
        ap = T[name][:, cols]
        if cols.step:
            sel(T[name][:], T.zz[:, 0:144], [[0, 144]], A.is_equal, 0.0, 0, 0, ["zz"], [name])
        sel(ap, T.zz[:, 0:ap.shape[1]], pat, A.is_gt, val, b0, -1, ["zz"], [name])
        sel(ap, ap, pat, A.is_ge, 0.0, b0 + 15, -1, [name], [name])

    def issue():
        rk = [0.0] * len(nodes)
        for k in range(len(nodes) - 1, -1, -1):
            x = nodes[k]
            rk[k] += x["cost"] + x["lag"] + x.get("more", 0.0)
            for j in x["hard"] | x["soft"] | set(x["after"].values()):
                rk[j] = max(rk[j], rk[k] + WAKE)

        def gap(busy, t, c):
            for a, z in busy:
                if t + c <= a:
                    break
                t = max(t, z)
            return t

        def wake(j, k, q):
            return 0.0 if nodes[j]["q"] == q and (q == "t" or j not in nodes[k]["hard"]) else WAKE

        def forward():
            busy = {q: [] for q in "vtsgyxz"}
            for k in sorted(range(len(nodes)), key=lambda k: -rk[k]):
                x, best = nodes[k], None
                for q in x["qs"]:
                    t = max([0.0] + [nodes[j]["end"] + wake(j, k, q) for j in x["hard"] | x["soft"]])
                    if q in x["after"]:
                        t = max(t, nodes[x["after"][q]]["end"])
                    t = gap(busy[q], t, x["cost"])
                    if best is None or t < best[0]:
                        best = (t, q)
                x["at"], x["q"] = best
                x["end"] = x["at"] + x["cost"] + x["lag"]
                busy[x["q"]] = sorted(busy[x["q"]] + [(x["at"], x["at"] + x["cost"])])
            return max(x["end"] for x in nodes)

        def backward():
            busy, t = {q: [] for q in "vtsgyxz"}, [0.0] * len(nodes)
            for k in sorted(range(len(nodes)), key=lambda k: (-nodes[k]["end"], -k)):
                x = nodes[k]
                a = gap(busy[x["q"]], t[k] + x["lag"] + x.get("more", 0.0), x["cost"])
                rk[k] = a + x["cost"]
                busy[x["q"]] = sorted(busy[x["q"]] + [(a, rk[k])])
                for j in x["hard"] | x["soft"] | {x["after"][q] for q in x["after"] if q in x["qs"]}:
                    t[j] = max(t[j], rk[k] + wake(j, k, x["q"]) + 1e-6)
        tried = []
        for _ in range(PASSES):
            tried.append((forward(), list(rk)))
            backward()
        rk[:] = min(tried)[1]
        forward()
        line = sorted(nodes, key=lambda x: x["at"])
        tot, waited = {}, {q: {} for q in QU}
        for x in line:
            s, n = x["sem"] or ("q" + x["q"], 1)
            tot[s] = tot.get(s, 0) + n
            x["tok"] = (s, tot[s])
        for x in line:
            q = x["q"]
            if q not in QU:
                continue
            need = {}
            for j in x["hard"] | x["soft"]:
                y = nodes[j]
                if not (y["q"] == q and (q == "t" or j in x["soft"])):
                    need[y["tok"][0]] = max(need.get(y["tok"][0], 0), y["tok"][1])
            for s, n in need.items():
                if waited[q].get(s, 0) < n:
                    QU[q].wait_ge(T.sem[s], n)
                    waited[q][s] = n
            ins = x["fn"](QU[q], q)
            if not x["sem"]:
                ins.then_inc(T.sem["q" + q], 1)
        for s in tot:
            g.wait_ge(T.sem[s], tot[s])

    def pv(k, a, n):
        h = int(k[2])
        return T.PC[:, h, a // 4:(a + n) // 4, :, :] if k[1] == "C" else T[k[:2]][:, h, a:a + n]
    LO, HI = slice(0, 64), slice(64, 128)

    def way(c):
        return 0 if c in topo.cores_of(core) else 1 if topo.mates(core, c) else 2 if topo.same_plane(core, c) else 3
    others = sorted([c for c in T.cores if c != core], key=lambda c: (way(c) == 3, way(c) > 0, topo.die(c) != topo.die(core), way(c)))
    order = [T.rank_of(c) for c in [core] + others]
    offe = topo.engines(core, others[-1])
    one = [e for e in topo.engines(core, others[0]) if e not in offe]

    same = [c for c in others[1:] if topo.die(c) == topo.die(core)]
    cross = [c for c in others[1:] if c not in same]
    hand = (((0, one[:len(one) // 2]), (1, one[len(one) // 2:])), ((2, one),))

    def write(name, parts, cost, come):
        trs = []
        for r, dst, es in parts:
            ids = []
            for c in dst:
                rid, pid = topo.addr(c, core)
                ids.append(DstId(rid=rid, pnc=pid))
            trs.append(RemoteDMATransfer(dst_ids=ids, dma_engine_mask=sum(1 << e for e in es), remote_sem=T.sem["%s%d" % (name, r)],
                                         srcs=[T[name][:, r]], dsts=[T[name][:, r] for _ in dst], alu_op=0))
        sent = "sent%d" % len(nodes)
        node("g", lambda e, _: e.remote_dma_fused(trs, local_sem=T.sem.ls), cost, ["%s%d" % (name, r) for r, _, _ in parts], [sent],
             0.0, ("ls", sum(len(es) for _, _, es in parts)))
        nodes[-1]["more"] = M4
        for c, es in come:
            k = "%s%d" % (name, T.rank_of(c))
            node("x" if es[0] in offe else "z", None, 256 * size(T[name][:, 0]) * BYTE, [sent], [k], HOP[name[1:]], (k, len(es)))

    def theirs(name):
        return [([others[0]] + cross)[k] for k in SHARED.get(name, ())]

    def send(name):
        far = same if name in HANDED else [c for c in others[1:] if c not in theirs(name)]
        near = [c for c in others[:1] if c not in theirs(name)]
        if len(far) == 6 and SPLIT:
            ways = [(far[0::2], offe[:len(offe) // 2]), (far[1::2], offe[len(offe) // 2:])]
        else:
            ways = [(far, offe)]
        write(name, [(rank, near, one)] * len(near) + [(rank, cs, es) for cs, es in ways], 2.5 if name == TILES[0] else CALL,
              [(c, one) for c in near] + [(c, es) for c in far for cs, es in ways if c in cs])
        for call in hand if name in HANDED else ():
            write(name, [(T.rank_of(same[k]), others[:1], es) for k, es in call], CALL, [(cross[k], es) for k, es in call])

    def coming(name):
        return [r for r in ([T.rank_of(c) for c in [core, others[0]] + same + cross] if name in HANDED else order)
                if T.cores[r] not in theirs(name)]

    def base(b, r):
        return 128 + 5120 * (1 - b) + 640 * r

    def share(name, r):
        mine = [T.rank_of(([core] + same)[k]) for k in SHARED.get(name, ())]
        if r in mine:
            im, o = "OT" if name[1] == "O" else "W", T.rank_of(theirs(name)[mine.index(r)])
            rid, pid = topo.addr(others[0], core)
            first = name in TILES[:2]
            bs = ((0, hand[0][0][1]), (1, hand[0][1][1])) if first else ((int(name[2]), one),)
            trs = [RemoteDMATransfer(dst_ids=[DstId(rid=rid, pnc=pid)], dma_engine_mask=sum(1 << e for e in es),
                                     remote_sem=T.sem["%s%d" % (name, r)], srcs=[T[im][:, base(b, r):base(b, r) + 640]],
                                     dsts=[T[im][:, base(b, r):base(b, r) + 640]], alu_op=0) for b, es in bs]
            sent = "sent%d" % len(nodes)
            left = "l%s%d" % (im, mine.index(r)) if first else "ls"
            node("g", lambda e, _: e.remote_dma_fused(trs, local_sem=T.sem[left]), CALL,
                 ["%s%d%d" % (im, b, r) for b, _ in bs] + ([] if first else ["%s%d" % (name, order[1])]), [sent], 0.0, (left, len(one)))
            node("z", None, 128 * 640 * len(bs) * (2 if im == "OT" else 4) * BYTE / 2, [sent], ["%s%d%d" % (im, b, o) for b, _ in bs], HS,
                 ("%s%d" % (name, o), len(one)))

    for u in range(2):
        dma("ys"[u], [(T.O32[64 * hl:64 * hl + 64, 160 * u:160 * u + 160], T.opts[64 * u:64 * u + 64, :]) for hl in range(2)], [], ["O32%d" % u])
    for sd in range(2):
        dma("ys"[sd], [(T.X32[64 * u + 32 * sd:64 * u + 32 * sd + 32, 160 * j:160 * j + 160],
                        (T.rw, T.lw)[sd][64 * u + 32 * j:64 * u + 32 * j + 32, :]) for u in range(2) for j in range(2)], [], ["X32%d" % sd])
    kO, kX = ["O320", "O321"], ["X320", "X321"]

    iota(T.CI[:, 0:1], "CI", [[0, 1]], 0, 1, True)
    fill(T.zz[:], 0.0, "zz")
    col, ckey = {}, {}

    def bits(lst, k0):
        for k, (n, sh, m) in enumerate(lst):
            ts(T.CI[:, k0 + k:k0 + k + 1], T.CI[:, 0:1], sh, A.logical_shift_right, m, A.bitwise_and, ["CI"], ["CI" + n])
            col[n], ckey[n] = T.CF[:, k0 + k:k0 + k + 1], "CF%d" % k0
        cp(T.CF[:, k0:k0 + len(lst)], T.CI[:, k0:k0 + len(lst)], ["CI" + n for n, _, _ in lst], ["CF%d" % k0])

    def ma(name, src, m, a):
        k = len([n for n in ckey if ckey[n][:2] == "CC"])
        o, i, cm, ca = T.CC[:, k:k + 1], col[src], col.get(m, m), col.get(a, a)
        op("vs", lambda e, q: e.tensor_scalar(o, i, cm, ca, A.mult, A.add) if q == "v" else e.activation(o, i, AF.Identity, bias=ca, scale=cm),
           o, CY, [ckey[s] for s in (src, m, a) if s in ckey], ["CC%d" % k])
        col[name], ckey[name] = o, "CC%d" % k

    def tsc(out, i, s1, o1, s2, o2, r, w, part=slice(0, 128)):
        ts(out, i, col[s1][part] if s1 in col else s1, o1, col[s2][part] if s2 in col else s2, o2,
           list(r) + [ckey[s] for s in (s1, s2) if s in ckey], w)

    def mat(ap, key, t, wgt, width):
        tsc(ap, T.ci[:, 0:width], t, A.is_equal, wgt, A.mult, ["ci"], [key])
    bits([("sd", 6, 1), ("s5", 5, 1)], 1)
    for n, s, m, a in (("yc", "sd", 79.5, -79.5), ("ys", "sd", 1 - 1.0 / 160, 1.0 / 160), ("al", "sd", -16.0, -64.0),
                       ("ga", "sd", 64.0, 64.0), ("be", "sd", -128.0, 129.0), ("sL", "s5", -1.0 / 32, 1.0 / 64)):
        ma(n, s, m, a)
    act(T.CB[:, 0:1], col["sd"], AF.Tanh, -16.0, 32.0, [ckey["sd"]], ["CB"], 1.4)
    col["sg"], ckey["sg"] = T.CB[:, 0:1], "CB"
    bits([("s8", 0, 7), ("hl", 3, 1), ("gp", 4, 7), ("G", 4, 3), ("i", 0, 15)], 3)
    bits([("s4", 0, 3), ("b2", 2, 1), ("b1", 1, 1), ("b0", 0, 1)], 8)
    for n, s, m, a in (("co", "G", 160.0, "i"), ("w", "hl", -79.0, 80.0), ("tz", "gp", 16.0, 15.0), ("sw", "sg", -64.0, 0.0),
                       ("a0", "b0", -0.5, 1.0), ("a1", "b1", -0.75, 1.0), ("a2", "b2", -0.9375, 1.0), ("w1", "b2", "w", 0.0),
                       ("t4", "gp", 16.0, "s4"), ("tm", "i", 1024.0, 0.0), ("a4", "G", 32.0, "s8"),
                       ("a5", "sd", 8.0, 16.0), ("wy", "hl", -159.0, 160.0), ("wi", "hl", 64.5, -64.5),
                       ("tq", "s8", -1.0, "tz"), ("tzs", "tz", 1.0, "sw"), ("a6", "a0", "a1", 0.0), ("a3", "a6", "a2", 0.0),
                       ("w0", "w1", -1.0, "w"), ("tn", "t4", 1.0, 12.0), ("ty", "a4", 1.0, "a5")):
        ma(n, s, m, a)

    for sd in range(2):
        iota(T.kI[:, 64 * sd:64 * sd + 64], "kI%d" % sd, [[0, 4], [64, 2], [1, 8]], 8 * sd, -1)
    iota(T.ci[:], "ci", [[1, 160]])
    iota(T.xI[:], "xI", [[16, 10], [0, 8]], 0, 0, True)
    iota(T.bI[:], "bI", [[1, 256]])
    pw = [[32, 2], [0, 4], [1, 16]]
    for k in range(2):
        pick(T.RW[:, k, :], "RW%d" % k, (pw, 16 * k, 64.0), (pw, 16 * k + 64, 64.0))
        mat(T.LM[:, k, :], "LM%d" % k, "tn", "w%d" % k, 140)
    for k in range(4):
        ts(T.RI[:, k, :], T.kI[:], -16.0 * k, A.is_equal, None, None, ["kI0", "kI1"], ["RI%d" % k])
        pick(T.RO[:, k, :], "RO%d" % k, ([[64, 2], [0, 4], [1, 16]], 16 * k, 1.0))
    tsc(T.xl[:], T.xI[:], "co", A.add, None, None, ["xI"], ["xl"])
    tsc(T.ol[:], T.xI[:, 0::8], "co", A.add, None, None, ["xI"], ["ol"])
    tsc(T.DL[:, 0:8], T.ci[:, 0:8], "s8", A.is_equal, None, None, ["ci"], ["DL"])
    mat(T.LQ[:], "LQ", "tq", "w", 136)
    mat(T.Zs[:], "Zs", "tzs", "w", 144)
    mat(T.YM[:], "YM", "ty", "wy", 160)
    kZK, kCS = ["ZK%d" % k for k in range(8)], ["CS%d" % k for k in range(8)]
    for k in range(8):
        op("vs", lambda e, q, k=k: e.tensor_scalar(T.ZK[:, k, :], T.Zs[:], T.DL[:, k:k + 1], None, A.mult) if q == "v" else
           e.activation(T.ZK[:, k, :], T.Zs[:], AF.Identity, scale=T.DL[:, k:k + 1]), T.Zs[:], CY / 2, ["Zs", "DL"], [kZK[k]])
        sel(T.CS[:, k::8], T.zz[:, 0:10], [[0, 10]], A.not_equal, float(128 >> k), 0, 0, ["zz"], [kCS[k]])
    tsc(T.fI[:], T.bI[:], "a3", A.mult, -0.5 + 2.0 ** -9, A.add, ["bI"], ["fI"])
    ts(T.fI[:], T.fI[:], 1, A.bitwise_and, None, None, ["fI"], ["fI"])
    cp(T.F[:], T.fI[:], ["fI"], ["F"])
    block("Z1", slice(15, 143, 16), [[16, 8]], 0, 1.0)
    block("ZV", slice(15, 143, 16), [[16, 8]], 0, -PEN)
    block("ZVs", slice(15, 143, 16), [[-64, 2], [16, 4]], 64, -PEN)
    block("HA", slice(0, 128), [[-64, 2], [16, 4], [0, 16]], 64, HUGE)
    p8, p1 = [[0, 10], [1, 8]], [[1, 128]]
    sel(T.H2[:], T.zz[:, 0:80], p8, A.is_equal, 2.0, 0, 0, ["zz"], ["H2"])
    sel(T.RR[:], T.zz[:, 0:80], p8, A.not_equal, -1e9, 0, 0, ["zz"], ["RR"])
    sel(T.m3[:], T.zz[:, 0:80], [[0, 80]], A.not_equal, -3.0, 0, 0, ["zz"], ["m3"])
    sel(T.rw4[:], T.zz[:], [[0, 160], [1, 4]], A.not_equal, -HUGE, 0, 0, ["zz"], ["rw4"])
    sel(T.q2[:], T.zz[:, 0:160], [[0, 160]], A.is_ge, -0.5, -64, 1, ["zz"], ["q2"])
    pick(T.IP[:], "IP", (p1, 0, PEN / 2))
    pick(T.Ip[:], "Ip", (p1, 0, 1.0))
    pick(T.In[:], "In", (p1, 0, -1.0))
    ps, po, py = [[32, 2], [64, 2], [1, 32]], [[32, 2], [-64, 2], [1, 32]], [[16, 5], [-1000, 2], [1, 16]]
    pick(T.Mh[:], "Mh", (ps, 0, 1.0 / 128), (po, 64, -1.0 / 128))
    pick(T.Mn[:], "Mn", (ps, 0, -1.0 / 128), (po, 64, 1.0 / 128))
    pick(T.Ms[:], "Ms", (ps, 0, -1.0 / 64))
    tsc(T.y1[:], T.zz[:, 0:160], "tm", A.subtract, None, None, ["zz"], ["y1"])
    pick(T.NA[:], "NA", (py, 1000, -1.0))
    pick(T.NB[:], "NB", (py, 1064, 1.0))
    pick(T.NH[:], "NH", (py, 1000, -0.5), (py, 1064, 0.5))
    pick(T.Mo[:], "Mo", (po, 64, -1.0 / 64))
    pick(T.OA[:], "OA", (py, 1000, 1.0))
    pick(T.OB[:], "OB", (py, 1064, -1.0))
    pick(T.OH[:], "OH", (py, 1000, 0.5), (py, 1064, -0.5))
    fill(T.W[:, 0:128], -BIG, "Wz")
    fill(T.W[:, EC:WD], -BIG, "We")
    fill(T.OT[:, 0:128], 128.0, "OTz")
    fill(T.OT[:, EC:WD], 128.0, "OTe")
    tsc(T.OT[:, EC:EC + 1], col["hl"], 8.0, A.mult, 128.0, A.add, [ckey["hl"]], ["OTe"])

    ts(T.qi[:], T.O32[:], -39.5, A.add, 1.0 / 80, A.mult, kO, ["qi"])
    tsc(T.yi[:], T.O32[:], "yc", A.add, "ys", A.mult, kO, ["yi"])
    tsc(pv("PD0", 0, 320), T.qi[:], "al", A.mult, "ga", A.add, ["qi"], ["PD0"])
    tsc(T.tb[:], T.yi[:], "be", A.mult, None, None, ["yi"], ["tb"])
    tt(T.AOi[:, rank], pv("PD0", 0, 320), T.tb[:], A.add, ["PD0", "tb"], ["AOi%d" % rank])
    send("AOi")
    FF = pv("PD1", 0, 320)
    tsc(FF, T.X32[:], "sL", A.mult, None, None, kX, ["PD1"])
    for u, (p, o) in enumerate(((LO, HI), (HI, LO))):
        tsc(T.AWi[p, rank, u, :], T.X32[p, :], "sL", A.mult, None, None, kX, ["z%d" % u], p)
        tt(T.AWi[o, rank, u, :], FF[p, :], T.AWi[p, rank, u, :], A.subtract, ["PD1", "z%d" % u], ["z%d" % (2 + u)])
    kz = ["z%d" % k for k in range(4)]
    lastw["AWi%d" % rank] = [j for k in kz for j in lastw[k]]
    send("AWi")

    turn = [0]

    def spread(name, r, b, pk=None):
        if pk is None:
            pk = "P" + "ACB"[turn[0] % 3]
            turn[0] += 1
        t = T[name]
        if name == "AOi":
            lst = [(pv(pk + str(u), 80 * k, 80), T.RI[:, k, :], t[:, r, u, 80 * b:80 * b + 80]) for u in range(2) for k in range(4)]
            km = ["RI%d" % k for k in range(4)]
        elif name == "AWi":
            lst = [(pv(pk + str(u), 80 * k, 80), T.RW[:, k % 2, :], t[:, r, u, 160 * (k // 2) + 80 * b:160 * (k // 2) + 80 * b + 80])
                   for u in range(2) for k in range(4)]
            km = ["RW0", "RW1"]
        elif name[1] == "O":
            lst = [(pv(pk + str(k // 2), 160 * (k % 2), 160), T.RO[:, k, :], t[:, r, :]) for k in range(4)]
            km = ["RO%d" % k for k in range(4)]
        else:
            lst = [(pv(pk + str(k // 2), 160 * (k % 2), 160), T.RW[:, k % 2, :], t[:, r, k // 2, :]) for k in range(4)]
            km = ["RW0", "RW1"]
        mms([x + (True, True) for x in lst], km + ["%s%d" % (name, r)], [pk + "0", pk + "1"])
        im = "OT" if name[1] == "O" else "W"
        cp(T[im][:, base(b, r):base(b, r) + 640], T.PC[:, :, 0:80, :, :] if pk == "PC" else T[pk][:, :, 0:320],
           [pk + "0", pk + "1"], ["%s%d%d" % (im, b, r)], "sv")
    kW = ["We", "Wz"] + ["W%d%d" % (b, r) for b in range(2) for r in range(N)]
    kOT = ["OTe", "OTz"] + ["OT%d%d" % (b, r) for b in range(2) for r in range(N)]

    def own(im, b):
        return T[im][:, base(b, rank):base(b, rank) + 640], "%s%d%d" % (im, b, rank)

    def own_slots(b):
        win, k = own("OT", b)
        cp(T["old%d" % b][:], win.indirect(T.ol[:]), [k, "ol"], ["old%d" % b], "sv", GA)

    def own_walls(b, more=0.0):
        win, k = own("W", b)
        for h in range(2):
            cp(T["x%d" % b][:, 640 * h:640 * h + 640], win.indirect(T.xl[:, 40 * h:40 * h + 40]), [k, "xl"], ["x%d%d" % (b, h)], "sv", GA)
            nodes[-1]["more"] = more
        act(T["XO%d" % b][:], win.indirect(T.ol[:]), AF.Identity, -BIG, 1.0, [k, "ol"], ["XO%d" % b], GA)

    def lists(b, src, ks, pk):
        P = pv(pk, 0, 80)
        mms([(P[:, c::5], T.LQ[:, 8 - 8 * h:136 - 8 * h], src[:, 32 * c + 16 * h:32 * c + 16 * h + 16], h == 0, h == 1)
             for c in range(5) for h in range(2)], ["LQ", ks], [pk])
        cp(T["LQn%d" % b][:], P, [pk], ["LQn%d" % b])
        cp(T["LQs%d" % b][LO, :], P[HI, :], [pk], ["LQsa%d" % b])
        cp(T["LQs%d" % b][HI, :], P[LO, :], [pk], ["LQsb%d" % b])

    def replies(t):
        b = t % 2
        P0, P4 = pv("PD1", 0, 80), pv("PD0", 0, 80)
        prs = [(T.ZK[:, (a + t) % 8, 15 - a:143 - a], T.gO[:, 80 * a:80 * a + 80]) for a in range(16)]
        for h in range(2):
            cp(T.gO[:, 640 * h:640 * h + 640], T.OT[:].indirect(T["LQs%d" % b][:, 40 * h:40 * h + 40]), kOT + ["LQsa%d" % b, "LQsb%d" % b],
               ["gO%d" % h], "sv", GA)
        for h in range(2):
            mm(P0, prs[8 * h:8 * h + 8], kZK + ["gO%d" % h], ["PD1"], h == 0, h == 1)
        cp(T.L1[:], P0, ["PD1"], ["L1"])
        nodes[-1]["more"] = M3
        cp(T.L2[LO, :], P0[HI, :], ["PD1"], ["L2a"])
        cp(T.L2[HI, :], P0[LO, :], ["PD1"], ["L2b"])
        nodes[-1]["more"] = M3
        cp(T.kk[:], P0, ["PD1"], ["kk"], "sv")
        act(T.sE[:], T.kk[:], AF.Sign, EC + 4.0, -1.0, ["kk"], ["sE"])
        mm(P4, [(T.Ip[:], T.kk[:])], ["Ip", "kk"], ["PD0"], True, False, 4)
        mm(P4, [(T.IP[:], T.m3[:]), (T.IP[:], T.sE[:])], ["IP", "m3", "sE"], ["PD0"], False, False)

    def lz(name, a):
        return T[name][:, 15 - a:143 - a]

    def rnd(t):
        b = t % 2
        W, OT, x, kx = T.W[:], T.OT[:], T["x%d" % b][:], ["x%d0" % b, "x%d1" % b]
        P4, PG = pv("PD0", 0, 80), pv("PB0", 0, 80)
        for h in range(2):
            cp(T.u[:, 640 * h:640 * h + 640], W.indirect(T["LQn%d" % b][:, 40 * h:40 * h + 40]), kW + ["LQn%d" % b], ["u%d" % h], "s", GA)
        tt(T.cm1[:], W.indirect(T.L1[:]), x, A.is_gt, kW + ["L1"] + kx, ["cm1"], GA)
        tt(T.cm2[:], W.indirect(T.L2[:]), x, A.is_lt, kW + ["L2a", "L2b"] + kx, ["cm2"], GA)
        def signs(parts, kd, key):
            for k, (o, i, lower) in enumerate(parts):
                act(o, i, AF.Tanh, (-8.0, -TB)[lower], (-16.0, 16.0)[lower], kd, [key + str(k)])
            return [key + str(k) for k in range(len(parts))]
        mm(P4, [(lz("ZV", a), T.cm1[:, a::16]) for a in range(16)], ["ZV", "cm1"], ["PD0"], False, False)
        m = 1 + t
        for h in range(2):
            d, vv, o = T.d0[:, 80 * h:80 * h + 80], T.V0[:, 80 * h:80 * h + 80], 640 * h
            kd = ["d0%d%d" % (h, k) for k in range(2 if m > 1 else 1)]
            for k in range(len(kd)):
                tt(d[:, :, :, k] if m > 1 else d, T.u[:, o + (k ^ m):o + 640:2 * len(kd)], T.u[:, o + k:o + 640:2 * len(kd)], A.subtract,
                   ["u%d" % h], [kd[k]])
            parts = [(vv[:, :, :, 0, :] if m > 1 else vv[:, :, :, :, 0], d, 0)]
            parts += [(vv[:, :, :, :, 1], d, 1)] if m == 1 else [(vv[:, :, :, 1, :], d, 1)] if m == 2 else \
                [(vv[:, :, :, 1, 1 - k], d[:, :, :, k], 1) for k in range(2)]
            kv = [signs(parts, kd, "V0%d" % h)]
            nodes[-1]["more"] = M1
            d, vv, pk = T.PC[:, h, 0:80], T.V1[:, 80 * h:80 * h + 80], "PC%d" % h
            if h < ONPE:
                mms([(d[:, :, k >> 1, k & 1], (T.Ip, T.In)[z][:], T.u[:, o + (k, k ^ (4 + t))[1 - z]:o + 640:8], z == 0, z == 1)
                     for k in range(4) for z in range(2)], ["Ip", "In", "u%d" % h], [pk], 4)
            else:
                d, pk = T.d1[:, 80 * h:80 * h + 80], "d1%d" % h
                for k in range(4):
                    tt(d[:, :, k >> 1, k & 1], T.u[:, o + (k ^ (4 + t)):o + 640:8], T.u[:, o + k:o + 640:8], A.subtract, ["u%d" % h], [pk + str(k)])
                lastw[pk], lastr[pk] = [lastw[pk + str(k)][0] for k in range(4)], []
                for k in range(4):
                    lastr[pk + str(k)] = lastr[pk]
            parts = [(vv[:, :, 0, :, :], d, 0)]
            parts += [(vv[:, :, 1, :, :], d, 1)] if t == 0 else [(vv[:, :, 1, :, 1 - k], d[:, :, :, k], 1) if t == 1 else
                                                                  (vv[:, :, 1, 1 - k, :], d[:, :, k, :], 1) for k in range(2)]
            kv.append(signs(parts, [pk], "V1%d" % h))
            nodes[-1]["more"] = M1
            for q in range(2):
                mm(pv("PA%d" % q, 0, 80), [(lz("Z1", a), T["V%d" % q][:, 10 * a:10 * a + 10, :, :, :]) for a in range(8 * h, 8 * h + 8)],
                   ["Z1"] + kv[q], ["PA%d" % q], h == 0, h == 1)
        for q in range(2):
            act(T["s%d" % q][:], pv("PA%d" % q, 0, 80), AF.Sign, -THR, 1.0, ["PA%d" % q], ["s%d" % q])
            nodes[-1]["more"] = M5
        mm(P4, [(lz("ZVs", a), T.cm2[:, a::16]) for a in range(16)], ["ZVs", "cm2"], ["PD0"], False, False)
        ks = ["sE", "s0", "s1"]
        mm(P4, [(T.IP[:], T[s][:]) for s in ks[1:]], ["IP"] + ks[1:], ["PD0"], False, True)
        mm(PG, [(T.IP[:], T[s][:]) for s in ["m3"] + ks], ["IP", "m3"] + ks, ["PB0"])
        act(T.gb[:], PG, AF.Sign, 0.0, -1.0, ["PB0"], ["gb"])
        scan(T.sc[:], T.H2[:], T.gb[:], A.mult, A.add, ["H2", "gb"], ["sc"])
        tt(T.e0[:], P4, T.RR[:], A.is_lt, ["PD0", "RR"], ["e0"])
        tt(T.e1[:], P4, T.CS[:], A.min, ["PD0"] + kCS, ["e1"])
        scan(T.S1[:], T.e0[:], P4, A.mult, A.max, ["e0", "PD0"], ["S1"])
        scan(T.S2[:], T.e0[:], T.e1[:], A.mult, A.max, ["e0", "e1"], ["S2"])
        cp(T.cu[:], T.S1[:, 7::8], ["S1"], ["cu"])
        tt(T.cx[:], T.S2[:, 7::8], T.sc[:, 7::8], A.add, ["S2", "sc"], ["cx"])
        old, ko = (T["old%d" % t][:], "old%d" % t) if t < 2 else (T.AO0[:, rank], "AO0%d" % rank)
        tt(T.dT[:], OT.indirect(T.cu[:]), old, A.subtract, kOT + ["cu", ko], ["dT"], GA)
        cp(T.iu[:], T.cx[:], ["cx"], ["iu"])
        tt(T.mT[:], T.F[:].indirect(T.iu[:]), T.dT[:], A.mult, ["F", "iu", "dT"], ["mT"], GA)
        tn, kt = (T["AO%d" % t][:, rank], "AO%d%d" % (t, rank)) if t < 2 else (T.TN[:], "TN")
        tt(tn, T.mT[:], old, A.add, ["mT", ko], [kt])
        if t < 2:
            send("AO%d" % t)
        PH = pv("PB1", 0, 160)
        for z, (s, ks) in enumerate(((old, ko), (T.mT[:], "mT"))):
            for k in range(2):
                mm(pv("PA%d" % k, 0, 40), [(T.LM[:, k, 12 - 4 * j:140 - 4 * j], s[:, j::4]) for j in range(4)], ["LM%d" % k, ks], ["PA%d" % k],
                   z == 0, z == 1)
        cp(T.LN[:], T.PA[:, :, 0:40], ["PA0", "PA1"], ["LN"])
        ts(T.nd[:], tn, 127.5, A.is_lt, None, None, [kt], ["nd"])
        mm(PH, [(T.Ip[:], T["XO%d" % b][:])], ["Ip", "XO%d" % b], ["PB1"], True, False, 4)
        mm(PH, [(T.HA[:], T.nd[:])], ["HA", "nd"], ["PB1"], False, True)
        act(T.q1[:], PH, AF.Relu, col["tm"], -1.0, ["PB1", ckey["tm"]], ["q1"])
        nodes[-1]["more"] = M2
        for k in range(2):
            o = 320 * k
            cp(T.w[:, o:o + 320], W.indirect(T.LN[:, 20 * k:20 * k + 20]), kW + ["LN"], ["w%d" % k], "s", GA)
            tt(T.t1[:, o:o + 320], W.indirect(T.LN[:, 40 + 20 * k:60 + 20 * k]), T.w[:, o:o + 320], A.max, kW + ["LN", "w%d" % k], ["t1%d" % k], GA)
        scan(T.sw[:], T.rw4[:], T.t1[:], A.add, A.max, ["rw4", "t10", "t11"], ["sw"])
        return tn, kt

    def tile(t):
        P1, P2, FF = pv("PD0", 0, 160), pv("PD1", 0, 160), pv("PD1", 160, 160)
        mm(P2, [(T.Mh[:], T.q2[:])], ["Mh", "q2"], ["PD1"], True, False, 4)
        mm(P1, [(T.Ms[:], T.y1[:])], ["Ms", "y1"], ["PD0"], True, False, 4)
        mm(P2, [(T.Mn[:], T.q1[:])], ["Mn", "q1"], ["PD1"], False, False, 4)
        mm(P1, [(T.Ms[:], T.q1[:])], ["Ms", "q1"], ["PD0"], False, False, 4)
        mm(P2, [(T.Mh[:], T.sw[:, 3::4])], ["Mh", "sw"], ["PD1"], False, True, 4)
        mm(P1, [(T.Mo[:], T.sw[:, 3::4])], ["Mo", "sw"], ["PD0", "tile"], False, True, 4)
        ts(T.r1[:], P2, MG / 64, A.add, MG / 64, A.subtract, ["PD1"], ["r1"])
        tt(FF, P1, T.r1[:], A.min, ["PD0", "r1"], ["PD1"])
        Z = T["AW%d" % t]
        tt(Z[LO, rank, 0, :], P1[LO, :], T.r1[LO, :], A.min, ["PD0", "r1"], ["z0"])
        tt(Z[HI, rank, 1, :], P1[HI, :], T.r1[HI, :], A.min, ["PD0", "r1"], ["z1"])
        tt(Z[HI, rank, 0, :], FF[LO, :], Z[LO, rank, 0, :], A.subtract, ["PD1", "z0"], ["z2"])
        tt(Z[LO, rank, 1, :], FF[HI, :], Z[HI, rank, 1, :], A.subtract, ["PD1", "z1"], ["z3"])
        lastw["AW%d%d" % (t, rank)] = [j for k in kz for j in lastw[k]]
        send("AW%d" % t)

    def put(y, o, b, q="y"):
        dma(q, [(o[:, 80 * b:80 * b + 80], T[y][:, 80 * b:80 * b + 80])], [y + str(b)], [])

    def put_slots(b, tn, kt, pk):
        tsc(T.ind[:], tn, 63.5, A.is_gt, "wi", A.mult, [kt], ["ind"])
        mm(pv(pk, 0, 80), [(T.YM[:, 16 - 16 * k:144 - 16 * k], s[:, 80 * k:80 * k + 80]) for k in range(2) for s in (tn, T.ind)],
           ["YM", kt, "ind"], [pk])
        act(T.Yo[:, 80 * b:80 * b + 80], pv(pk, 0, 80), AF.Identity, -48.0, 1.0, [pk], ["Yo%d" % b])
        put("Yo", T.yo, b)

    def put_old_walls(b):
        win, k = own("W", b)
        cp(T.XY[:], win.indirect(T.ol[:]), [k, "ol"], ["XY"], "sv", GA)
        for pk, m, y, o in (("PB0", "OA", "Yr", T.yr), ("PB1", "OB", "Yl", T.yl)):
            mm(pv(pk, 0, 80), [(T[m][:, 16 - 16 * k:144 - 16 * k], T.XY[:, 80 * k:80 * k + 80]) for k in range(2)], [m, "XY"], [pk], True, True, 4)
            cp(T[y][:, 80 * b:80 * b + 80], pv(pk, 0, 80), [pk], [y + str(b)], "sv")
            put(y, o, b)

    def put_walls(b):
        jobs = (("PC0", ("OH", "NH", "OH"), "q2"), ("PC1", ("NA", "NA", "OB"), "y1"), ("PD1", ("NB", "NB", "OA"), "y1"))
        for z in range(3):
            for pk, ms, c in jobs:
                s = (c, "q1", "sw")[z]
                mm(pv(pk, 0, 80), [(T[ms[z]][:, 16 - 16 * k:144 - 16 * k],
                                    T.sw[:, 3 + 320 * k:320 * k + 320:4] if z == 2 else T[s][:, 80 * k:80 * k + 80]) for k in range(2)],
                   [ms[z], s], [pk], z == 0, z == 2, 4)
        ts(T.mid[:], pv("PC0", 0, 80), MG, A.add, MG, A.subtract, ["PC0"], ["mid"])
        for q, pk, y, o, f in (("y", "PC1", "Yr", T.yr, A.min), ("s", "PD1", "Yl", T.yl, A.max)):
            tt(T[y][:, 80 * b:80 * b + 80], pv(pk, 0, 80), T.mid[:], f, [pk, "mid"], [y + str(b)])
            put(y, o, b, q)

    for name in ("AOi", "AWi"):
        for b in range(2):
            spread(name, rank, b)
        share(name, rank)
    for b in range(2):
        own_slots(b)
        own_walls(b, (M6, 0.0)[b])
        lists(b, T["old%d" % b], "old%d" % b, "PD%d" % b)
    for name in ("AOi", "AWi"):
        for r in coming(name)[1:]:
            for b in range(2):
                spread(name, r, b)
            share(name, r)
    for t in range(3):
        replies(t)
        if t == 2:
            put_old_walls(1)
        tn, kt = rnd(t)
        if t == 2:
            put_slots(0, tn, kt, "PD0")
            put_walls(0)
            break
        turn[0] = 0
        tile(t)
        for j, r in enumerate(coming("AO%d" % t)):
            if j == GATE:
                gate.update({"t": lastw["tile"][0], "v": lastw["z3"][0]})
            spread("AO%d" % t, r, t)
            share("AO%d" % t, r)
        gate.clear()
        if t == 0:
            lists(0, tn, kt, "PD1")
        else:
            put_slots(1, tn, kt, "PD0")
        for r in coming("AW%d" % t):
            spread("AW%d" % t, r, t)
            share("AW%d" % t, r)
        if t == 0:
            own_walls(0)
    issue()
